import numpy as np
import ml_dtypes


def mxq(x, axis, fmt="e4m3"):
    dtype, down = {"e4m3": (ml_dtypes.float8_e4m3fn, 7), "e5m2": (ml_dtypes.float8_e5m2, 14)}[fmt]
    v = np.moveaxis(np.asarray(x, np.float32).astype(ml_dtypes.bfloat16).astype(np.float64), axis, -1)
    blocks = v.reshape(v.shape[:-1] + (-1, 32))
    amax = np.abs(blocks).max(-1, keepdims=True)
    byte = np.maximum(np.where(amax > 0, np.frexp(amax)[1] - 1 + 127, 0) - down, 1)
    scale = np.exp2(byte - 127.0)
    codes = (blocks / scale).astype(np.float32).astype(dtype).astype(np.float64)
    return np.moveaxis((codes * scale).reshape(v.shape), -1, axis)


WIDE = False


def mx_kscale(k):
    if not WIDE:
        return np.ones(k)
    levels = np.array([10, -10, 5, -5, 0])
    if k % 512:
        return np.exp2(np.random.permutation(np.resize(levels, k // 32))).repeat(32)
    a = np.empty((k // 512, 16))
    for p in range(k // 512):
        a[p, :8] = np.random.permutation(np.resize(levels, 8))
        for g in range(8):
            far = levels[np.abs(levels - a[p, g]) >= 10]
            a[p, g + 8] = far[np.random.randint(len(far))]
    return np.exp2(a.ravel()).repeat(32)


def f64(x):
    return np.asarray(x).astype(np.float64)


def striped(idx):
    return np.tile(idx.reshape(-1, 16).T, (8, 1)).astype(np.uint16)


def unstriped(offs):
    return offs[:16].T.reshape(-1).astype(np.int64)


E2M1 = np.array([0.0, 0.5, 1.0, 1.5, 2.0, 3.0, 4.0, 6.0, -0.0, -0.5, -1.0, -1.5, -2.0, -3.0, -4.0, -6.0])


def pack_weight(w, fmt):
    k, n = w.shape
    w = f64(np.asarray(w, np.float32).astype(ml_dtypes.bfloat16)).reshape(k // 32, 32, n)
    amax = np.abs(w).max(1)
    if fmt == "e4m3":
        byte = np.frexp(amax)[1] - 1 + 127 - 7
    else:
        mant, ex = np.frexp(amax / 6.0)
        byte = np.where(mant > 0.5, ex, ex - 1) + 127
    byte = np.clip(np.where(amax > 0, byte, 1), 1, 254)
    scaled = (w * np.exp2(127.0 - byte)[:, None, :]).reshape(k, n).astype(np.float32)
    by_word = np.ascontiguousarray(scaled.reshape(k // 512, 128, 4, n).transpose(0, 1, 3, 2))
    if fmt == "e4m3":
        words = by_word.astype(ml_dtypes.float8_e4m3fn).view(np.uint8)
    else:
        c = by_word.astype(ml_dtypes.float4_e2m1fn).view(np.uint8) & 0xF
        words = (c[..., 0::2] | (c[..., 1::2] << 4)).reshape(k // 512, 128, 2 * n)
    return np.ascontiguousarray(words), np.ascontiguousarray(byte.astype(np.uint8).reshape(k // 512, 16, n))


def unpack_weight(words, scales, fmt):
    g, _, n = scales.shape
    words = np.ascontiguousarray(words).reshape(g, 128, n, -1)
    if fmt == "e4m3":
        vals = words.view(ml_dtypes.float8_e4m3fn).astype(np.float64)
    else:
        nib = np.empty((g, 128, n, 4), np.uint8)
        nib[..., 0::2] = words & 0xF
        nib[..., 1::2] = words >> 4
        vals = E2M1[nib]
    vals = vals * np.repeat(np.exp2(scales.astype(np.float64) - 127.0), 8, axis=1)[..., None]
    return vals.transpose(0, 1, 3, 2).reshape(g * 512, n)


def gelu(v):
    return 0.5 * v * (1.0 + np.tanh(np.sqrt(2.0 / np.pi) * (v + 0.044715 * v**3)))


K, T, S, T2, P, H, N = 512, 4096, 1024, 2048, 1024, 1024, 512

def setup_inputs():
    n = np.random.standard_normal
    s = mx_kscale(K)[:, None]
    u = mx_kscale(H)[:, None]
    tab_words, tab_scales = pack_weight(n((K, T)) * s, "e4m3")
    w1_words, w1_scales = pack_weight(n((K, H)) / np.sqrt(K) / s, "e2m1")
    w2_words, w2_scales = pack_weight(n((K, H)) / np.sqrt(K) / s, "e4m3")
    return {
        "tab_words": tab_words, "tab_scales": tab_scales,
        "offs": striped(np.random.permutation(T)[:S]),
        "offs2": striped(np.random.permutation(T2)[:S]),
        "offs3": striped(np.random.permutation(T2)[:P]),
        "w1_words": w1_words, "w1_scales": w1_scales,
        "w2_words": w2_words, "w2_scales": w2_scales,
        "w3": (n((K, H)) / np.sqrt(K) / s).astype(np.float32),
        "wgs": np.exp(0.3 * n((128, S))).astype(np.float32),
        "prior": (0.7 * n((H, P))).astype(np.float32),
        "gain": (np.random.uniform(0.5, 1.5, H) * u[:, 0]).astype(np.float32),
        "w4": (1.5 * n((H, N)) / np.sqrt(H) / u).astype(np.float32),
    }

def reference(tab_words, tab_scales, offs, offs2, offs3, w1_words, w1_scales,
              w2_words, w2_scales, w3, wgs, prior, gain, w4):
    v = unpack_weight(tab_words, tab_scales, "e4m3")[:, unstriped(offs)]
    w1 = unpack_weight(w1_words, w1_scales, "e2m1")
    w2 = unpack_weight(w2_words, w2_scales, "e4m3")
    w3q = mxq(f64(w3), 0, "e4m3")
    d1 = w1.T @ v
    d2 = w2.T @ v
    d3 = w3q.T @ v
    h = d1 * d2 * d3
    page = np.zeros((H, T2))
    page[:, unstriped(offs2)] = np.tile(f64(wgs), (H // 128, 1)) * h
    x = page[:, unstriped(offs3)]
    z = np.tanh(x + f64(prior)) * f64(gain)[:, None]
    zq = mxq(z, 0, "e4m3")
    w4q = mxq(f64(w4), 0, "e4m3")
    return w4q.T @ zq

@@ -1,0 +1,314 @@
+from contextlib import ExitStack
+
+import concourse.mybir as mybir
+from concourse.masks import make_identity
+
+K, T, S, T2, PR, H, N = 512, 4096, 1024, 2048, 1024, 1024, 512
+FLOPS = 2 * (3 * K * H * S + H * N * PR)
+
+F32 = mybir.dt.float32
+BF16 = mybir.dt.bfloat16
+I32 = mybir.dt.int32
+U32 = mybir.dt.uint32
+U16 = mybir.dt.uint16
+U8 = mybir.dt.uint8
+E4M3 = mybir.dt.float8_e4m3fn_x4
+E2M1 = mybir.dt.float4_e2m1fn_x4
+MULT = mybir.AluOpType.mult
+ACT = mybir.ActivationFunctionType
+
+P = 128
+PACK = 4
+BANK = 512
+TILES = H // P
+X_LOT = (8, 4, 5, 6, 7, 8, 3)
+HEAD = 2 * P
+SIG = 6
+
+
+def tile_list_semijoin_cache_kernel(tc, tab_words, tab_scales, offs, offs2, offs3, w1_words, w1_scales,
+                                             w2_words, w2_scales, w3, wgs, prior, gain, w4, out):
+    nc = tc.nc
+    with ExitStack() as ctx:
+        keep = ctx.enter_context(tc.tile_pool(name="keep", bufs=1))
+        ring = ctx.enter_context(tc.tile_pool(name="ring", bufs=2))
+        psum = ctx.enter_context(tc.psum_pool(name="psum", bufs=1))
+
+        idx = keep.tile([P, S // 16], U16, name="idx")
+        idx2 = keep.tile([P, S // 16], U16, name="idx2")
+        idx3 = keep.tile([P, PR // 16], U16, name="idx3")
+
+        tabw = keep.tile([P, T], I32, name="tabw", align_bytes=64)
+        tabs = keep.tile([P, T], U8, name="tabs", align_bytes=64)
+        w1s = keep.tile([P, H], U8, name="w1s", align_bytes=64)
+        w2s = keep.tile([P, H], U8, name="w2s", align_bytes=64)
+        nc.vector.memset(tabs[:].bitcast(I32), 0)
+        nc.gpsimd.memset(w1s[:].bitcast(I32), 0)
+        nc.vector.memset(w2s[:].bitcast(I32), 0)
+
+        def load_scales(queue, plane, rows):
+            for q in range(4):
+                queue.dma_start(plane[32 * q:32 * q + 4, :].bitcast(I32), rows[0, 4 * q:4 * q + 4, :].bitcast(I32))
+
+        w3_rows = w3.rearrange("(p j) c -> p j c", j=PACK)
+        w1_i32 = w1_words[0].bitcast(I32)
+        w2_i32 = w2_words[0].rearrange("p c i -> p (c i)").bitcast(I32)
+
+        def load_raw(rows, width, tag, bufs, queue=nc.sync):
+            raw = ring.tile([P, PACK, width], F32, name=tag, bufs=bufs)
+            queue.dma_start(raw[:], rows)
+            return raw
+
+        def weave(raw, width, copy, grouped=None):
+            if grouped is None:
+                grouped = ring.tile([P, width, PACK], BF16, name="grouped", align_bytes=64)
+            copy(grouped[:].rearrange("p (c i) t -> p c t i", i=4), raw[:].rearrange("p t (c i) -> p c t i", i=4))
+            return grouped
+
+        def lot(n, shape, dtype, name):
+            return keep.tile(shape, dtype, name=name, tag="lot%d" % n, align_bytes=64)
+
+        def quantise(grouped, codes, scales):
+            nc.vector.quantize_mx(out=codes.bitcast(E4M3), scales=scales, in_=grouped.rearrange("p c t -> p (c t)"))
+            return codes, scales
+
+        def own(width, dtype, name):
+            return keep.tile([P, width], dtype, name=name, align_bytes=64)[:]
+
+        w3q = {}
+
+        def quantise_w3(grouped, first, count, scales):
+            for k in range(count):
+                cols = slice(k * P, (k + 1) * P)
+                w3q[first + k] = quantise(grouped[:, cols, :], lot(first + k, [P, P], U32, "w3_codes")[:], scales[:, cols])
+
+        nc.sync.dma_start(idx[:], offs)
+        raw0 = load_raw(w3_rows[:, :, 0:P], P, "raw0", 1)
+        load_scales(nc.sync, tabs, tab_scales)
+        w1a = keep.tile([P, HEAD // 2], I32, name="w1a", align_bytes=64)
+        nc.sync.dma_start(w1a[:], w1_i32[:, 0:HEAD // 2])
+        nc.sync.dma_start(tabw[:], tab_words[0].rearrange("p t i -> p (t i)").bitcast(I32))
+        load_scales(nc.gpsimd, w1s, w1_scales)
+        w2a = keep.tile([P, HEAD], I32, name="w2a", align_bytes=64)
+        nc.sync.dma_start(w2a[:], w2_i32[:, 0:HEAD])
+        load_scales(nc.sync, w2s, w2_scales)
+        wg = keep.tile([P, S], F32, name="wg")
+        nc.sync.dma_start(wg[:, 0:BANK], wgs[:, 0:BANK])
+        raw1 = load_raw(w3_rows[:, :, P:2 * P], P, "raw", 2)
+        nc.sync.dma_start(idx2[:], offs2)
+        nc.sync.dma_start(wg[:, BANK:S], wgs[:, BANK:S])
+        raw2 = load_raw(w3_rows[:, :, 2 * P:4 * P], 2 * P, "raw", 2)
+        w1b = keep.tile([P, (H - HEAD) // 2], I32, name="w1b", align_bytes=64)
+        nc.sync.dma_start(w1b[:], w1_i32[:, HEAD // 2:H // 2])
+        w2b = keep.tile([P, H - HEAD], I32, name="w2b", align_bytes=64)
+        nc.sync.dma_start(w2b[:], w2_i32[:, HEAD:H])
+        nc.sync.dma_start(idx3[:], offs3)
+        raw3 = load_raw(w3_rows[:, :, 4 * P:8 * P], 4 * P, "raw", 2)
+        g_sb = keep.tile([P, PACK], F32, name="g_sb")
+
+        quantise_w3(weave(raw0, P, nc.vector.tensor_copy), 0, 1, own(P, U8, "w3_scales0"))
+
+        vs = keep.tile([P, S], U8, name="vs", align_bytes=64)
+        nc.vector.tensor_copy(vs[:], tabs[:].indirect(idx[:]))
+        pages = []
+        for k in range(2):
+            page = keep.tile([P, T2], F32, name="page%d" % k)
+            nc.vector.memset(page[:], 0.0)
+            pages.append(page)
+
+        def page_of(i):
+            return pages[min(i, TILES - 2) % 2]
+
+        vw = []
+        for half in range(2):
+            words = keep.tile([P, BANK], U32, name="vw%d" % half, align_bytes=64)
+            nc.vector.tensor_copy(words[:], tabw[:].bitcast(U32).indirect(idx[:, 32 * half:32 * half + 32]))
+            vw.append(words)
+
+        ident = keep.tile([P, P], F32, name="ident")
+        make_identity(nc, ident[:])
+
+        def stationary(i):
+            if i * P < HEAD:
+                a, b, at = w1a, w2a, i * P
+            else:
+                a, b, at = w1b, w2b, i * P - HEAD
+            a, b = a[:, at // 2:(at + P) // 2], b[:, at:at + P]
+            codes, scales = w3q[i]
+            cols = slice(i * P, (i + 1) * P)
+            return [(a.bitcast(E2M1), w1s[:, cols]), (b.bitcast(E4M3), w2s[:, cols]),
+                    (codes.bitcast(E4M3), scales)]
+
+        def signature(i, which, half):
+            lhs, lhs_scale = stationary(i)[which]
+            bank = psum.tile([P, BANK], F32, name="sig", bufs=SIG)
+            nc.tensor.matmul_mx(out=bank[:], lhsT=lhs, lhsT_scale=lhs_scale, rhs=vw[half][:].bitcast(E4M3),
+                                rhs_scale=vs[:, half * BANK:(half + 1) * BANK], start=True, stop=True)
+            return bank
+
+        def put_vector(i):
+            src = wg
+            for k, which in enumerate((2, 0, 1)):
+                part = ring.tile([P, S], F32, name="d%d" % (k + 1), bufs=3)
+                for half in range(2):
+                    cols = slice(half * BANK, (half + 1) * BANK)
+                    nc.vector.tensor_tensor(part[:, cols], signature(i, which, half)[:], src[:, cols], MULT)
+                src = part
+            nc.vector.tensor_copy(page_of(i)[:].indirect(idx2[:]), src[:])
+
+        def put_gpsimd(i, halves):
+            page = page_of(i)
+            cols = slice(halves[0] * BANK, (halves[-1] + 1) * BANK)
+            d = [ring.tile([P, S], F32, name="d%d" % (w + 1), bufs=3) for w in range(3)]
+            for w in range(3):
+                for half in halves:
+                    nc.scalar.copy(d[w][:, half * BANK:(half + 1) * BANK], signature(i, w, half)[:])
+            h = lot((i - 1) % (TILES + 1), [P, S], F32, "h")
+            nc.gpsimd.tensor_tensor(d[0][:, cols], d[0][:, cols], d[1][:, cols], MULT)
+            nc.gpsimd.tensor_tensor(d[2][:, cols], d[2][:, cols], wg[:, cols], MULT)
+            nc.gpsimd.tensor_tensor(h[:, cols], d[0][:, cols], d[2][:, cols], MULT)
+            return lambda: nc.vector.tensor_copy(page[:].indirect(idx2[:, 32 * halves[0]:32 * halves[-1] + 32]), h[:, cols])
+
+        squashed = keep.tile([P, PR // P, PACK, P], F32, name="squashed")
+        pairs = keep.tile([P, PR // P, 2, 2 * P], BF16, name="pairs")
+        g_row = keep.tile([P, K], F32, name="g_row")
+        g_pairs = keep.tile([P, PACK, 2, 64], F32, name="g_pairs")
+        priors = {}
+
+        def load_prior(i):
+            t = ring.tile([P, PR], F32, name="prior_sb", bufs=3)
+            nc.sync.dma_start(t[:], prior[i * P:(i + 1) * P, :])
+            priors[i] = t
+
+        def turn(terms, m0, width):
+            blocks = width // P
+            bank = psum.tile([P, blocks, P], F32, name="turned")
+            for n, src in enumerate(terms):
+                for k in range(blocks):
+                    nc.tensor.matmul(bank[:, k, :], src[:, m0 + k * P:m0 + (k + 1) * P], ident[:], is_transpose=True,
+                                     start=n == 0 and k == 0, stop=n == len(terms) - 1 and k == blocks - 1)
+            return bank
+
+        def squash_pairs(i, bank, m0, width, tz, engine, whole):
+            k0, blocks = m0 // P, width // P
+            nc.scalar.activation(tz[:, :, k0:k0 + blocks, :].rearrange("m u k (p e) -> m u (k p) e", e=2),
+                                 bank[:].rearrange("m k (p u e) -> m u (k p) e", u=2, e=2), ACT.Tanh)
+            if whole:
+                k0, blocks = 0, PR // P
+            if not whole or m0 + width == PR:
+                q = i % PACK
+                engine.tensor_tensor(pairs[:, k0:k0 + blocks, :, 64 * q:64 * q + 64].rearrange("m k u c -> m u k c"),
+                                     tz[:, :, k0:k0 + blocks, :],
+                                     g_pairs[:, q, :, :].unsqueeze(2).to_broadcast([P, 2, blocks, 64]), MULT)
+
+        def fetch_whole(i):
+            x = lot(X_LOT[i], [P, PR], F32, "x")
+            nc.vector.tensor_copy(x[:], page_of(i)[:].indirect(idx3[:]))
+            if i >= PACK:
+                tz = ring.tile([P, 2, PR // P, 64], F32, name="tz")
+            for m0 in (0, BANK):
+                bank = turn((priors[i], x), m0, BANK)
+                if i < PACK:
+                    nc.scalar.activation(squashed[:, m0 // P:m0 // P + PACK, :, 32 * i:32 * i + 32],
+                                         bank[:].rearrange("m k (p t) -> m k t p", t=PACK), ACT.Tanh)
+                else:
+                    squash_pairs(i, bank, m0, BANK, tz, nc.gpsimd, True)
+
+        def weave_z0(m0, n):
+            planes = ring.tile([P, PACK, BANK], BF16, name="planes", bufs=1)
+            for t in range(PACK):
+                bank = psum.tile([P, BANK], F32, name="sig", bufs=SIG)
+                for k in range(BANK // P):
+                    nc.tensor.transpose(bank[:, k * P:(k + 1) * P], squashed[:, m0 // P + k, t, :], ident[:])
+                nc.scalar.activation(planes[:, t, :], bank[:], ACT.Copy, scale=g_sb[:, t:t + 1])
+            return weave(planes, BANK, nc.scalar.copy, lot(n, [P, BANK, PACK], BF16, "z0_woven"))
+
+        def weave_z1(m0, width):
+            blocks = width // P
+            bank = psum.tile([P, blocks, 2, P], F32, name="back")
+            for k in range(blocks):
+                for u in range(2):
+                    nc.tensor.transpose(bank[:, k, u, :], pairs[:, m0 // P + k, u, :].bitcast(F32), ident[:])
+            woven = ring.tile([P, width, PACK], BF16, name="grouped", align_bytes=64)
+            nc.scalar.copy(woven[:].rearrange("p m t -> p (m t)").bitcast(F32).rearrange("p (k m u) -> p k m u", k=blocks, u=2),
+                           bank[:].rearrange("p k u m -> p k m u"))
+            return woven
+
+        w4q = []
+        z0 = []
+
+        def estimate(m0, width, z1):
+            first_codes, first_scales = z0[m0 // BANK]
+            at = m0 % BANK
+            moving = [(first_codes[:, at:at + width], first_scales[:, at:at + width]), z1]
+            for pair in range(2):
+                bank = psum.tile([P, 2, width], F32, name="sig", bufs=SIG)
+                for b in range(2):
+                    for k in range(2):
+                        n0 = (2 * pair + k) * P
+                        codes, scales = w4q[b]
+                        nc.tensor.matmul_mx(out=bank[:, k, :], lhsT=codes[:, n0:n0 + P].bitcast(E4M3), lhsT_scale=scales[:, n0:n0 + P],
+                                            rhs=moving[b][0].bitcast(E4M3), rhs_scale=moving[b][1],
+                                            start=b == 0 and k == 0, stop=b == 1 and k == 1)
+                res = ring.tile([P, 2, width], F32, name="res", bufs=4)
+                if pair == 0 or m0 < BANK:
+                    nc.scalar.copy(res[:], bank[:])
+                else:
+                    nc.vector.tensor_copy(res[:], bank[:])
+                nc.sync.dma_start(out[2 * pair * P:2 * (pair + 1) * P, m0:m0 + width].rearrange("(k p) m -> p k m", p=P), res[:])
+
+        AHEAD = 3
+        puts = {}
+        load_prior(0)
+        quantise_w3(weave(raw1, P, nc.scalar.copy), 1, 1, own(P, U8, "w3_scales1"))
+        put_vector(0)
+        puts[1] = put_gpsimd(1, (0, 1))
+        quantise_w3(weave(raw2, 2 * P, nc.scalar.copy), 2, 2, own(2 * P, U8, "w3_scales2"))
+        puts[2] = put_gpsimd(2, (0, 1))
+        for i in range(TILES):
+            if i + 1 < TILES:
+                load_prior(i + 1)
+            if i in (1, 2):
+                raw4 = load_raw(w4[(i - 1) * K:i * K, :].rearrange("(p j) n -> p j n", j=PACK), N, "raw", 2)
+            if i == 2:
+                nc.sync.dma_start(g_sb[:], gain[0:K].rearrange("(p t) -> p t", t=PACK))
+                nc.sync.dma_start(g_row[:], gain[K:2 * K].partition_broadcast(P))
+            if i > 0:
+                puts[i]()
+            if i == 1:
+                quantise_w3(woven, 4, 4, lot(0, [P, BANK], U8, "w3_scales4")[:])
+            if i + AHEAD < TILES:
+                puts[i + AHEAD] = put_gpsimd(i + AHEAD, (0, 1))
+            if i in (2, 3):
+                w4q.append(quantise(woven[:], lot(i - 1, [P, N], U32, "w4_codes")[:], own(N, U8, "w4_scales%d" % i)))
+            if i == 0:
+                woven = weave(raw3, BANK, nc.scalar.copy)
+            if i in (1, 2):
+                woven = weave(raw4, BANK, nc.scalar.copy)
+            if i == 3:
+                nc.scalar.copy(g_pairs[:].rearrange("m q u (p e) -> m q u p e", e=2),
+                               g_row[:].rearrange("m (q p u e) -> m q u p e", q=PACK, u=2, e=2))
+            if i < 5:
+                fetch_whole(i)
+            if i == 4:
+                z0_woven = [weave_z0(0, X_LOT[5]), weave_z0(BANK, X_LOT[6])]
+            if i == 6:
+                for half in range(2):
+                    z0.append(quantise(z0_woven[half][:], lot(5 - half, [P, BANK], U32, "z0_codes")[:], own(BANK, U8, "z0_scales%d" % half)))
+                    fetch_whole(5 + half)
+
+        last = TILES - 1
+        x = lot(TILES, [P, PR], F32, "x")
+        tz = ring.tile([P, 2, PR // P, 64], F32, name="tz")
+        width = 2 * P
+        chunks = range(0, PR, width)
+        for m0 in chunks:
+            nc.vector.tensor_tensor(x[:, m0:m0 + width], page_of(last)[:].indirect(idx3[:, m0 // 16:(m0 + width) // 16]),
+                                    priors[last][:, m0:m0 + width], mybir.AluOpType.add)
+        for m0 in chunks:
+            squash_pairs(last, turn((x,), m0, width), m0, width, tz, nc.vector, False)
+        z1 = {}
+        for m0 in chunks:
+            z1[m0] = quantise(weave_z1(m0, width)[:], own(width, U32, "z1_codes%d" % m0), own(width, U8, "z1_scales%d" % m0))
+        for m0 in chunks:
+            estimate(m0, width, z1[m0])

@@ -15,15 +15,24 @@ U8 = mybir.dt.uint8
 E4M3 = mybir.dt.float8_e4m3fn_x4
 E2M1 = mybir.dt.float4_e2m1fn_x4
 MULT = mybir.AluOpType.mult
+ADD = mybir.AluOpType.add
 ACT = mybir.ActivationFunctionType
 
 P = 128
 PACK = 4
 BANK = 512
 TILES = H // P
-X_LOT = (8, 4, 5, 6, 7, 8, 3)
+X_LOT = (9, 4, 5, 6, 7, 9, 8)
 HEAD = 2 * P
 SIG = 6
+TURN = 2
+CHUNKS = (256, 256, 256, 256)
+VM = 256
+PIN = 1
+RES_LOT = (0, 4, 6, 9)
+GV = 1
+ONS = (0, 1, 2, 3, 4, 6)
+W4LOT = 7
 
 
 def tile_list_semijoin_cache_kernel(tc, tab_words, tab_scales, offs, offs2, offs3, w1_words, w1_scales,
@@ -77,13 +86,16 @@ def tile_list_semijoin_cache_kernel(tc, tab_words, tab_scales, offs, offs2, offs
 
         w3q = {}
 
-        def quantise_w3(grouped, first, count, scales):
+        def quantise_w3(grouped, first, count, codes=None):
+            codes = own(count * P, U32, "w3_codes%d" % first) if codes is None else codes
+            scales = own(count * P, U8, "w3_scales%d" % first)
+            quantise(grouped, codes, scales)
             for k in range(count):
-                cols = slice(k * P, (k + 1) * P)
-                w3q[first + k] = quantise(grouped[:, cols, :], lot(first + k, [P, P], U32, "w3_codes")[:], scales[:, cols])
+                w3q[first + k] = codes[:, k * P:(k + 1) * P], scales[:, k * P:(k + 1) * P]
 
         nc.sync.dma_start(idx[:], offs)
-        raw0 = load_raw(w3_rows[:, :, 0:P], P, "raw0", 1)
+        raw0 = keep.tile([P, PACK, P], F32, name="raw0", align_bytes=64)
+        nc.sync.dma_start(raw0[:], w3_rows[:, :, 0:P])
         load_scales(nc.sync, tabs, tab_scales)
         w1a = keep.tile([P, HEAD // 2], I32, name="w1a", align_bytes=64)
         nc.sync.dma_start(w1a[:], w1_i32[:, 0:HEAD // 2])
@@ -93,28 +105,24 @@ def tile_list_semijoin_cache_kernel(tc, tab_words, tab_scales, offs, offs2, offs
         nc.sync.dma_start(w2a[:], w2_i32[:, 0:HEAD])
         load_scales(nc.sync, w2s, w2_scales)
         wg = keep.tile([P, S], F32, name="wg")
-        nc.sync.dma_start(wg[:, 0:BANK], wgs[:, 0:BANK])
-        raw1 = load_raw(w3_rows[:, :, P:2 * P], P, "raw", 2)
+        nc.sync.dma_start(wg[:], wgs)
+        raw1 = load_raw(w3_rows[:, :, P:4 * P], 3 * P, "raw", 2)
         nc.sync.dma_start(idx2[:], offs2)
-        nc.sync.dma_start(wg[:, BANK:S], wgs[:, BANK:S])
-        raw2 = load_raw(w3_rows[:, :, 2 * P:4 * P], 2 * P, "raw", 2)
-        w1b = keep.tile([P, (H - HEAD) // 2], I32, name="w1b", align_bytes=64)
-        nc.sync.dma_start(w1b[:], w1_i32[:, HEAD // 2:H // 2])
+        w1b = keep.tile([P, HEAD // 2], I32, name="w1b", align_bytes=64)
+        nc.sync.dma_start(w1b[:], w1_i32[:, HEAD // 2:HEAD])
         w2b = keep.tile([P, H - HEAD], I32, name="w2b", align_bytes=64)
         nc.sync.dma_start(w2b[:], w2_i32[:, HEAD:H])
+        w1c = keep.tile([P, K // 2], I32, name="w1c", align_bytes=64)
+        nc.sync.dma_start(w1c[:], w1_i32[:, K // 2:K])
+        raw3 = load_raw(w3_rows[:, :, K:H], K, "raw", 2)
         nc.sync.dma_start(idx3[:], offs3)
-        raw3 = load_raw(w3_rows[:, :, 4 * P:8 * P], 4 * P, "raw", 2)
-        g_sb = keep.tile([P, PACK], F32, name="g_sb")
+        g_sb = keep.tile([P, 2, PACK], F32, name="g_sb")
 
-        quantise_w3(weave(raw0, P, nc.vector.tensor_copy), 0, 1, own(P, U8, "w3_scales0"))
+        grouped0 = keep.tile([P, P, PACK], BF16, name="grouped0", align_bytes=64)
+        quantise_w3(weave(raw0, P, nc.vector.tensor_copy, grouped0)[:], 0, 1)
 
         vs = keep.tile([P, S], U8, name="vs", align_bytes=64)
         nc.vector.tensor_copy(vs[:], tabs[:].indirect(idx[:]))
-        pages = []
-        for k in range(2):
-            page = keep.tile([P, T2], F32, name="page%d" % k)
-            nc.vector.memset(page[:], 0.0)
-            pages.append(page)
 
         def page_of(i):
             return pages[min(i, TILES - 2) % 2]
@@ -127,17 +135,32 @@ def tile_list_semijoin_cache_kernel(tc, tab_words, tab_scales, offs, offs2, offs
 
         ident = keep.tile([P, P], F32, name="ident")
         make_identity(nc, ident[:])
+        pages = []
+        for k in range(2):
+            page = keep.tile([P, T2], F32, name="page%d" % k)
+            nc.gpsimd.memset(page[:], 0.0)
+            pages.append(page)
+
+        w1_dealt = [lot(PACK + t, [P, 2 * P], U8, "w1_dealt") for t in range(PACK)]
+        w2_dealt = keep.tile([P, PACK, P], I32, name="w2_dealt", align_bytes=64)
+        s1_dealt = keep.tile([P, PACK, P], U8, name="s1_dealt", align_bytes=64)
+        s2_dealt = keep.tile([P, PACK, P], U8, name="s2_dealt", align_bytes=64)
+        nc.gpsimd.tensor_copy(s1_dealt[:], w1s[:, K:H].rearrange("k (p t) -> k t p", t=PACK))
+        nc.gpsimd.tensor_copy(s2_dealt[:], w2s[:, K:H].rearrange("k (p t) -> k t p", t=PACK))
+        nc.gpsimd.tensor_copy(w2_dealt[:], w2b[:, K - HEAD:H - HEAD].rearrange("k (p t) -> k t p", t=PACK))
+        for t in range(PACK):
+            nc.gpsimd.tensor_copy(w1_dealt[t][:].rearrange("k (p b) -> k p b", b=2),
+                                  w1c[:].bitcast(U8).rearrange("k (p t b) -> k t p b", t=PACK, b=2)[:, t, :, :])
 
         def stationary(i):
-            if i * P < HEAD:
-                a, b, at = w1a, w2a, i * P
-            else:
-                a, b, at = w1b, w2b, i * P - HEAD
-            a, b = a[:, at // 2:(at + P) // 2], b[:, at:at + P]
             codes, scales = w3q[i]
+            third = (codes.bitcast(E4M3), scales)
+            if i >= PACK:
+                t = i - PACK
+                return [(w1_dealt[t][:].bitcast(E2M1), s1_dealt[:, t, :]), (w2_dealt[:, t, :].bitcast(E4M3), s2_dealt[:, t, :]), third]
+            a, b, at = (w1a, w2a, i * P) if i * P < HEAD else (w1b, w2b, i * P - HEAD)
             cols = slice(i * P, (i + 1) * P)
-            return [(a.bitcast(E2M1), w1s[:, cols]), (b.bitcast(E4M3), w2s[:, cols]),
-                    (codes.bitcast(E4M3), scales)]
+            return [(a[:, at // 2:(at + P) // 2].bitcast(E2M1), w1s[:, cols]), (b[:, at:at + P].bitcast(E4M3), w2s[:, cols]), third]
 
         def signature(i, which, half):
             lhs, lhs_scale = stationary(i)[which]
@@ -149,70 +172,72 @@ def tile_list_semijoin_cache_kernel(tc, tab_words, tab_scales, offs, offs2, offs
         def put_vector(i):
             src = wg
             for k, which in enumerate((2, 0, 1)):
-                part = ring.tile([P, S], F32, name="d%d" % (k + 1), bufs=3)
+                part = ring.tile([P, S], F32, name="d%d" % (k + 1), bufs=3) if k < 2 else lot(8, [P, S], F32, "h")
                 for half in range(2):
                     cols = slice(half * BANK, (half + 1) * BANK)
                     nc.vector.tensor_tensor(part[:, cols], signature(i, which, half)[:], src[:, cols], MULT)
                 src = part
             nc.vector.tensor_copy(page_of(i)[:].indirect(idx2[:]), src[:])
 
-        def put_gpsimd(i, halves):
+        def put_gpsimd(i, halves, between=None):
             page = page_of(i)
             cols = slice(halves[0] * BANK, (halves[-1] + 1) * BANK)
-            d = [ring.tile([P, S], F32, name="d%d" % (w + 1), bufs=3) for w in range(3)]
-            for w in range(3):
+            d = [lot(1 + w // 2, [P, S], F32, "d_last") if i == TILES - 1 and w != 1 else
+                 ring.tile([P, S], F32, name="d%d" % (w + 1), bufs=3) for w in range(3)]
+            for w in (2, 1, 0):
                 for half in halves:
                     nc.scalar.copy(d[w][:, half * BANK:(half + 1) * BANK], signature(i, w, half)[:])
-            h = lot((i - 1) % (TILES + 1), [P, S], F32, "h")
-            nc.gpsimd.tensor_tensor(d[0][:, cols], d[0][:, cols], d[1][:, cols], MULT)
-            nc.gpsimd.tensor_tensor(d[2][:, cols], d[2][:, cols], wg[:, cols], MULT)
+            if between is not None:
+                between()
+            h = lot(i - 1, [P, S], F32, "h")
+            nc.gpsimd.tensor_tensor(d[2][:, cols], d[2][:, cols], weights[i][:, cols], MULT)
+            nc.gpsimd.tensor_tensor(d[2][:, cols], d[2][:, cols], d[1][:, cols], MULT)
             nc.gpsimd.tensor_tensor(h[:, cols], d[0][:, cols], d[2][:, cols], MULT)
             return lambda: nc.vector.tensor_copy(page[:].indirect(idx2[:, 32 * halves[0]:32 * halves[-1] + 32]), h[:, cols])
 
         squashed = keep.tile([P, PR // P, PACK, P], F32, name="squashed")
-        pairs = keep.tile([P, PR // P, 2, 2 * P], BF16, name="pairs")
-        g_row = keep.tile([P, K], F32, name="g_row")
-        g_pairs = keep.tile([P, PACK, 2, 64], F32, name="g_pairs")
+        z1_woven = keep.tile([P, PR, PACK], BF16, name="z1_woven", align_bytes=64)
         priors = {}
+        weights = {i: wg for i in range(PACK)}
 
         def load_prior(i):
-            t = ring.tile([P, PR], F32, name="prior_sb", bufs=3)
-            nc.sync.dma_start(t[:], prior[i * P:(i + 1) * P, :])
-            priors[i] = t
+            rows = prior[i * P:(i + 1) * P, :] if i < PACK else prior[K:H, :].rearrange("(p t) m -> t p m", t=PACK)[i - PACK]
+            priors[i] = ring.tile([P, PR], F32, name="prior_sb", bufs=3)
+            nc.sync.dma_start(priors[i][:], rows)
+
+        def load_weights(i):
+            weights[i] = ring.tile([P, S], F32, name="wg_dealt")
+            rows = wgs.rearrange("(p t) j -> t p j", t=PACK)[i - PACK]
+            nc.sync.dma_start(weights[i][:], rows.unsqueeze(0).to_broadcast([PACK, P // PACK, S]))
 
         def turn(terms, m0, width):
             blocks = width // P
-            bank = psum.tile([P, blocks, P], F32, name="turned")
+            bank = psum.tile([P, blocks, P], F32, name="turned", bufs=TURN)
             for n, src in enumerate(terms):
                 for k in range(blocks):
                     nc.tensor.matmul(bank[:, k, :], src[:, m0 + k * P:m0 + (k + 1) * P], ident[:], is_transpose=True,
                                      start=n == 0 and k == 0, stop=n == len(terms) - 1 and k == blocks - 1)
             return bank
 
-        def squash_pairs(i, bank, m0, width, tz, engine, whole):
-            k0, blocks = m0 // P, width // P
-            nc.scalar.activation(tz[:, :, k0:k0 + blocks, :].rearrange("m u k (p e) -> m u (k p) e", e=2),
-                                 bank[:].rearrange("m k (p u e) -> m u (k p) e", u=2, e=2), ACT.Tanh)
-            if whole:
-                k0, blocks = 0, PR // P
-            if not whole or m0 + width == PR:
-                q = i % PACK
-                engine.tensor_tensor(pairs[:, k0:k0 + blocks, :, 64 * q:64 * q + 64].rearrange("m k u c -> m u k c"),
-                                     tz[:, :, k0:k0 + blocks, :],
-                                     g_pairs[:, q, :, :].unsqueeze(2).to_broadcast([P, 2, blocks, 64]), MULT)
+        def squash_slot(t, y, tz, cols):
+            nc.scalar.activation(tz[:], y[:], ACT.Tanh)
+            if t == PACK - 1 and GV:
+                nc.vector.tensor_scalar(z1_woven[:, cols, t], tz[:], g_sb[:, 1, t:t + 1], None, MULT)
+            else:
+                nc.scalar.activation(z1_woven[:, cols, t], tz[:], ACT.Copy, scale=g_sb[:, 1, t:t + 1])
 
         def fetch_whole(i):
             x = lot(X_LOT[i], [P, PR], F32, "x")
             nc.vector.tensor_copy(x[:], page_of(i)[:].indirect(idx3[:]))
             if i >= PACK:
-                tz = ring.tile([P, 2, PR // P, 64], F32, name="tz")
+                y = lot(i - 3, [P, PR], F32, "y") if i < 6 else x
+                nc.gpsimd.tensor_tensor(y[:], x[:], priors[i][:], ADD)
+                squash_slot(i - PACK, y, ring.tile([P, PR], F32, name="planes", bufs=1), slice(0, PR))
+                return
             for m0 in (0, BANK):
                 bank = turn((priors[i], x), m0, BANK)
-                if i < PACK:
-                    nc.scalar.activation(squashed[:, m0 // P:m0 // P + PACK, :, 32 * i:32 * i + 32],
-                                         bank[:].rearrange("m k (p t) -> m k t p", t=PACK), ACT.Tanh)
-                else:
-                    squash_pairs(i, bank, m0, BANK, tz, nc.gpsimd, True)
+                nc.scalar.activation(squashed[:, m0 // P:m0 // P + PACK, :, 32 * i:32 * i + 32],
+                                     bank[:].rearrange("m k (p t) -> m k t p", t=PACK), ACT.Tanh)
 
         def weave_z0(m0, n):
             planes = ring.tile([P, PACK, BANK], BF16, name="planes", bufs=1)
@@ -220,95 +245,98 @@ def tile_list_semijoin_cache_kernel(tc, tab_words, tab_scales, offs, offs2, offs
                 bank = psum.tile([P, BANK], F32, name="sig", bufs=SIG)
                 for k in range(BANK // P):
                     nc.tensor.transpose(bank[:, k * P:(k + 1) * P], squashed[:, m0 // P + k, t, :], ident[:])
-                nc.scalar.activation(planes[:, t, :], bank[:], ACT.Copy, scale=g_sb[:, t:t + 1])
+                nc.scalar.activation(planes[:, t, :], bank[:], ACT.Copy, scale=g_sb[:, 0, t:t + 1])
             return weave(planes, BANK, nc.scalar.copy, lot(n, [P, BANK, PACK], BF16, "z0_woven"))
-
-        def weave_z1(m0, width):
-            blocks = width // P
-            bank = psum.tile([P, blocks, 2, P], F32, name="back")
-            for k in range(blocks):
-                for u in range(2):
-                    nc.tensor.transpose(bank[:, k, u, :], pairs[:, m0 // P + k, u, :].bitcast(F32), ident[:])
-            woven = ring.tile([P, width, PACK], BF16, name="grouped", align_bytes=64)
-            nc.scalar.copy(woven[:].rearrange("p m t -> p (m t)").bitcast(F32).rearrange("p (k m u) -> p k m u", k=blocks, u=2),
-                           bank[:].rearrange("p k u m -> p k m u"))
-            return woven
 
         w4q = []
         z0 = []
 
-        def estimate(m0, width, z1):
-            first_codes, first_scales = z0[m0 // BANK]
+        def estimate_pass(b, banks, z_codes, z_scales):
+            codes, scales = w4q[b]
+            for n in range(N // P):
+                cols = slice(n * P, (n + 1) * P)
+                nc.tensor.matmul_mx(out=banks[n // 2][:, n % 2, :], lhsT=codes[:, cols].bitcast(E4M3), lhsT_scale=scales[:, cols],
+                                    rhs=z_codes.bitcast(E4M3), rhs_scale=z_scales,
+                                    start=b == 0 and n % 2 == 0, stop=b == 1 and n % 2 == 1)
+
+        def estimate_open(m0, width):
+            tag, bufs = ("sig", SIG) if m0 + width < PR else ("turned", TURN)
+            banks = [psum.tile([P, 2, width], F32, name=tag, bufs=bufs) for pair in range(2)]
+            codes, scales = z0[m0 // BANK]
             at = m0 % BANK
-            moving = [(first_codes[:, at:at + width], first_scales[:, at:at + width]), z1]
+            estimate_pass(0, banks, codes[:, at:at + width], scales[:, at:at + width])
+            return banks
+
+        def estimate_close(m0, width, banks, z1, both):
+            estimate_pass(1, banks, z1[0], z1[1])
             for pair in range(2):
-                bank = psum.tile([P, 2, width], F32, name="sig", bufs=SIG)
-                for b in range(2):
-                    for k in range(2):
-                        n0 = (2 * pair + k) * P
-                        codes, scales = w4q[b]
-                        nc.tensor.matmul_mx(out=bank[:, k, :], lhsT=codes[:, n0:n0 + P].bitcast(E4M3), lhsT_scale=scales[:, n0:n0 + P],
-                                            rhs=moving[b][0].bitcast(E4M3), rhs_scale=moving[b][1],
-                                            start=b == 0 and k == 0, stop=b == 1 and k == 1)
-                res = ring.tile([P, 2, width], F32, name="res", bufs=4)
-                if pair == 0 or m0 < BANK:
-                    nc.scalar.copy(res[:], bank[:])
+                res = both[:, pair, :, :]
+                if (2 * (m0 // 256) + pair) in ONS:
+                    nc.scalar.copy(res, banks[pair][:])
                 else:
-                    nc.vector.tensor_copy(res[:], bank[:])
-                nc.sync.dma_start(out[2 * pair * P:2 * (pair + 1) * P, m0:m0 + width].rearrange("(k p) m -> p k m", p=P), res[:])
+                    nc.vector.tensor_copy(res, banks[pair][:])
+                nc.sync.dma_start(out[2 * pair * P:2 * (pair + 1) * P, m0:m0 + width].rearrange("(k p) m -> p k m", p=P), res)
 
         AHEAD = 3
         puts = {}
         load_prior(0)
-        quantise_w3(weave(raw1, P, nc.scalar.copy), 1, 1, own(P, U8, "w3_scales1"))
+        woven = weave(raw1, 3 * P, nc.scalar.copy, lot(8, [P, 3 * P, PACK], BF16, "w3_woven"))
+        quantise_w3(woven[:, 0:P, :], 1, 1)
+        quantise_w3(woven[:, P:3 * P, :], 2, 2)
         put_vector(0)
-        puts[1] = put_gpsimd(1, (0, 1))
-        quantise_w3(weave(raw2, 2 * P, nc.scalar.copy), 2, 2, own(2 * P, U8, "w3_scales2"))
+        late_codes = lot(8, [P, 2, 2 * P], U32, "w3_codes")
+        late = [(lot(n, [P, 2 * P, PACK], BF16, "w3_woven"), k) for k, n in enumerate((0, X_LOT[0]))]
+
+        def late_w3():
+            for grouped, k in late:
+                nc.scalar.copy(grouped[:].rearrange("k (t p) j -> k t p j", t=2),
+                               raw3[:].rearrange("k j (p t) -> k t p j", t=PACK)[:, 2 * k:2 * k + 2, :, :])
+                quantise_w3(grouped[:], PACK + 2 * k, 2, late_codes[:, k, :])
+
+        puts[1] = put_gpsimd(1, (0, 1), late_w3)
         puts[2] = put_gpsimd(2, (0, 1))
+        w4_woven = []
         for i in range(TILES):
             if i + 1 < TILES:
                 load_prior(i + 1)
             if i in (1, 2):
                 raw4 = load_raw(w4[(i - 1) * K:i * K, :].rearrange("(p j) n -> p j n", j=PACK), N, "raw", 2)
             if i == 2:
-                nc.sync.dma_start(g_sb[:], gain[0:K].rearrange("(p t) -> p t", t=PACK))
-                nc.sync.dma_start(g_row[:], gain[K:2 * K].partition_broadcast(P))
+                nc.sync.dma_start(g_sb[:], gain.rearrange("(b p t) -> p b t", p=P, t=PACK))
+            if PACK <= i + AHEAD < TILES:
+                load_weights(i + AHEAD)
             if i > 0:
                 puts[i]()
-            if i == 1:
-                quantise_w3(woven, 4, 4, lot(0, [P, BANK], U8, "w3_scales4")[:])
             if i + AHEAD < TILES:
                 puts[i + AHEAD] = put_gpsimd(i + AHEAD, (0, 1))
-            if i in (2, 3):
-                w4q.append(quantise(woven[:], lot(i - 1, [P, N], U32, "w4_codes")[:], own(N, U8, "w4_scales%d" % i)))
-            if i == 0:
-                woven = weave(raw3, BANK, nc.scalar.copy)
             if i in (1, 2):
-                woven = weave(raw4, BANK, nc.scalar.copy)
-            if i == 3:
-                nc.scalar.copy(g_pairs[:].rearrange("m q u (p e) -> m q u p e", e=2),
-                               g_row[:].rearrange("m (q p u e) -> m q u p e", q=PACK, u=2, e=2))
-            if i < 5:
-                fetch_whole(i)
+                w4_woven.append(weave(raw4, BANK, nc.scalar.copy))
             if i == 4:
-                z0_woven = [weave_z0(0, X_LOT[5]), weave_z0(BANK, X_LOT[6])]
+                z0_woven = [weave_z0(0, 3), weave_z0(BANK, X_LOT[6])]
+            if i < 6:
+                fetch_whole(i)
             if i == 6:
+                codes = lot(W4LOT, [P, 2, N], U32, "w4_codes")
+                for b in range(2):
+                    w4q.append(quantise(w4_woven[b][:], codes[:, b, :], own(N, U8, "w4_scales%d" % b)))
+                codes = lot(5, [P, 2, BANK], U32, "z0_codes")
                 for half in range(2):
-                    z0.append(quantise(z0_woven[half][:], lot(5 - half, [P, BANK], U32, "z0_codes")[:], own(BANK, U8, "z0_scales%d" % half)))
-                    fetch_whole(5 + half)
+                    z0.append(quantise(z0_woven[half][:], codes[:, half, :], own(BANK, U8, "z0_scales%d" % half)))
+                fetch_whole(6)
 
         last = TILES - 1
-        x = lot(TILES, [P, PR], F32, "x")
-        tz = ring.tile([P, 2, PR // P, 64], F32, name="tz")
-        width = 2 * P
-        chunks = range(0, PR, width)
-        for m0 in chunks:
-            nc.vector.tensor_tensor(x[:, m0:m0 + width], page_of(last)[:].indirect(idx3[:, m0 // 16:(m0 + width) // 16]),
-                                    priors[last][:, m0:m0 + width], mybir.AluOpType.add)
-        for m0 in chunks:
-            squash_pairs(last, turn((x,), m0, width), m0, width, tz, nc.vector, False)
-        z1 = {}
-        for m0 in chunks:
-            z1[m0] = quantise(weave_z1(m0, width)[:], own(width, U32, "z1_codes%d" % m0), own(width, U8, "z1_scales%d" % m0))
-        for m0 in chunks:
-            estimate(m0, width, z1[m0])
+        chunks = [(sum(CHUNKS[:c]), width) for c, width in enumerate(CHUNKS)]
+        opened = [estimate_open(m0, width) for m0, width in chunks]
+        z1 = []
+        for half in range(2):
+            x = ring.tile([P, BANK], F32, name="planes" if half == 1 and PIN else "x_tail%d" % half, bufs=1)
+            tz = ring.tile([P, BANK], F32, name="planes" if half == 0 else "tz_tail", bufs=1)
+            mine = [(m0, width, slice(m0 % BANK, m0 % BANK + width)) for m0, width in chunks if m0 // BANK == half]
+            for m0, width, cols in mine:
+                nc.vector.tensor_tensor(x[:, cols], page_of(last)[:].indirect(idx3[:, m0 // 16:(m0 + width) // 16]),
+                                        priors[last][:, m0:m0 + width], ADD)
+            for m0, width, cols in mine:
+                squash_slot(PACK - 1, x[:, cols], tz[:, cols], slice(m0, m0 + width))
+                z1.append(quantise(z1_woven[:, m0:m0 + width, :], own(width, U32, "z1_codes%d" % m0), own(width, U8, "z1_scales%d" % m0)))
+        for c, (m0, width) in enumerate(chunks):
+            estimate_close(m0, width, opened[c], z1[c], lot(RES_LOT[c], [P, 2, 2, width], F32, "res"))

@@ -22,321 +22,395 @@ P = 128
 PACK = 4
 BANK = 512
 TILES = H // P
-X_LOT = (9, 4, 5, 6, 7, 9, 8)
 HEAD = 2 * P
-SIG = 6
-TURN = 2
-CHUNKS = (256, 256, 256, 256)
-VM = 256
-PIN = 1
-RES_LOT = (0, 4, 6, 9)
-GV = 1
-ONS = (0, 1, 2, 3, 4, 6)
-W4LOT = 7
+SUM_BANKS = 6
+TAB_FIRST = 3 * T // 8
+CHUNKS = (128, 256, 256, 256, 128)
 
 
 def tile_list_semijoin_cache_kernel(tc, tab_words, tab_scales, offs, offs2, offs3, w1_words, w1_scales,
-                                             w2_words, w2_scales, w3, wgs, prior, gain, w4, out):
+                                                 w2_words, w2_scales, w3, wgs, prior, gain, w4, out):
     nc = tc.nc
     with ExitStack() as ctx:
         keep = ctx.enter_context(tc.tile_pool(name="keep", bufs=1))
-        ring = ctx.enter_context(tc.tile_pool(name="ring", bufs=2))
         psum = ctx.enter_context(tc.psum_pool(name="psum", bufs=1))
+
+        def slot(tag, shape, dtype):
+            return keep.tile(shape, dtype, name=tag, tag=tag, align_bytes=64)
+
+        def bank_tile(n, shape):
+            return psum.tile(shape, F32, name="bank%d" % n, tag="bank%d" % n)
+
+        def half_cols(half):
+            return slice(half * BANK, (half + 1) * BANK)
+
+        def half_list(offsets, half):
+            return offsets[:, 32 * half:32 * half + 32]
 
         idx = keep.tile([P, S // 16], U16, name="idx")
         idx2 = keep.tile([P, S // 16], U16, name="idx2")
         idx3 = keep.tile([P, PR // 16], U16, name="idx3")
 
-        tabw = keep.tile([P, T], I32, name="tabw", align_bytes=64)
-        tabs = keep.tile([P, T], U8, name="tabs", align_bytes=64)
-        w1s = keep.tile([P, H], U8, name="w1s", align_bytes=64)
-        w2s = keep.tile([P, H], U8, name="w2s", align_bytes=64)
+        tabw = slot("tab", [P, T], I32)
+        tabs = slot("tabs", [P, T], U8)
+        w1s = slot("w1s", [P, H], U8)
+        w2s = slot("w2s", [P, H], U8)
         nc.vector.memset(tabs[:].bitcast(I32), 0)
-        nc.gpsimd.memset(w1s[:].bitcast(I32), 0)
-        nc.vector.memset(w2s[:].bitcast(I32), 0)
+        nc.gpsimd.memset(w2s[:].bitcast(I32), 0)
+        nc.vector.memset(w1s[:].bitcast(I32), 0)
 
-        def load_scales(queue, plane, rows):
+        def load_scales(plane, rows):
             for q in range(4):
-                queue.dma_start(plane[32 * q:32 * q + 4, :].bitcast(I32), rows[0, 4 * q:4 * q + 4, :].bitcast(I32))
+                nc.sync.dma_start(plane[32 * q:32 * q + 4, :].bitcast(I32), rows[0, 4 * q:4 * q + 4, :].bitcast(I32))
+
+        def load(queue, tag, shape, dtype, src):
+            dst = slot(tag, shape, dtype)
+            queue.dma_start(dst[:], src)
+            return dst
 
         w3_rows = w3.rearrange("(p j) c -> p j c", j=PACK)
         w1_i32 = w1_words[0].bitcast(I32)
         w2_i32 = w2_words[0].rearrange("p c i -> p (c i)").bitcast(I32)
-
-        def load_raw(rows, width, tag, bufs, queue=nc.sync):
-            raw = ring.tile([P, PACK, width], F32, name=tag, bufs=bufs)
-            queue.dma_start(raw[:], rows)
-            return raw
-
-        def weave(raw, width, copy, grouped=None):
-            if grouped is None:
-                grouped = ring.tile([P, width, PACK], BF16, name="grouped", align_bytes=64)
-            copy(grouped[:].rearrange("p (c i) t -> p c t i", i=4), raw[:].rearrange("p t (c i) -> p c t i", i=4))
-            return grouped
-
-        def lot(n, shape, dtype, name):
-            return keep.tile(shape, dtype, name=name, tag="lot%d" % n, align_bytes=64)
-
-        def quantise(grouped, codes, scales):
-            nc.vector.quantize_mx(out=codes.bitcast(E4M3), scales=scales, in_=grouped.rearrange("p c t -> p (c t)"))
-            return codes, scales
-
-        def own(width, dtype, name):
-            return keep.tile([P, width], dtype, name=name, align_bytes=64)[:]
-
-        w3q = {}
-
-        def quantise_w3(grouped, first, count, codes=None):
-            codes = own(count * P, U32, "w3_codes%d" % first) if codes is None else codes
-            scales = own(count * P, U8, "w3_scales%d" % first)
-            quantise(grouped, codes, scales)
-            for k in range(count):
-                w3q[first + k] = codes[:, k * P:(k + 1) * P], scales[:, k * P:(k + 1) * P]
+        tab_i32 = tab_words[0].rearrange("p t i -> p (t i)").bitcast(I32)
 
         nc.sync.dma_start(idx[:], offs)
-        raw0 = keep.tile([P, PACK, P], F32, name="raw0", align_bytes=64)
-        nc.sync.dma_start(raw0[:], w3_rows[:, :, 0:P])
-        load_scales(nc.sync, tabs, tab_scales)
-        w1a = keep.tile([P, HEAD // 2], I32, name="w1a", align_bytes=64)
-        nc.sync.dma_start(w1a[:], w1_i32[:, 0:HEAD // 2])
-        nc.sync.dma_start(tabw[:], tab_words[0].rearrange("p t i -> p (t i)").bitcast(I32))
-        load_scales(nc.gpsimd, w1s, w1_scales)
-        w2a = keep.tile([P, HEAD], I32, name="w2a", align_bytes=64)
-        nc.sync.dma_start(w2a[:], w2_i32[:, 0:HEAD])
-        load_scales(nc.sync, w2s, w2_scales)
-        wg = keep.tile([P, S], F32, name="wg")
-        nc.sync.dma_start(wg[:], wgs)
-        raw1 = load_raw(w3_rows[:, :, P:4 * P], 3 * P, "raw", 2)
+        nc.sync.dma_start(tabw[:, 0:TAB_FIRST], tab_i32[:, 0:TAB_FIRST])
+        load_scales(tabs, tab_scales)
+        nc.sync.dma_start(tabw[:, TAB_FIRST:T], tab_i32[:, TAB_FIRST:T])
+        w2a = load(nc.sync, "w2a", [P, HEAD], I32, w2_i32[:, 0:HEAD])
+        load_scales(w2s, w2_scales)
+        wg = slot("wg", [P, S], F32)
+        nc.sync.dma_start(wg[:, half_cols(0)], wgs[:, half_cols(0)])
+        raw3a = load(nc.sync, "raw3a", [P, PACK, HEAD], F32, w3_rows[:, :, 0:HEAD])
+        nc.sync.dma_start(wg[:, half_cols(1)], wgs[:, half_cols(1)])
+        w1a = load(nc.sync, "w1a", [P, HEAD // 2], I32, w1_i32[:, 0:HEAD // 2])
+        load_scales(w1s, w1_scales)
+        raw3b = load(nc.sync, "raw3b", [P, PACK, HEAD], F32, w3_rows[:, :, HEAD:K])
         nc.sync.dma_start(idx2[:], offs2)
-        w1b = keep.tile([P, HEAD // 2], I32, name="w1b", align_bytes=64)
-        nc.sync.dma_start(w1b[:], w1_i32[:, HEAD // 2:HEAD])
-        w2b = keep.tile([P, H - HEAD], I32, name="w2b", align_bytes=64)
-        nc.sync.dma_start(w2b[:], w2_i32[:, HEAD:H])
-        w1c = keep.tile([P, K // 2], I32, name="w1c", align_bytes=64)
-        nc.sync.dma_start(w1c[:], w1_i32[:, K // 2:K])
-        raw3 = load_raw(w3_rows[:, :, K:H], K, "raw", 2)
+        w1b = load(nc.sync, "w1b", [P, HEAD // 2], I32, w1_i32[:, HEAD // 2:HEAD])
+        w2b = load(nc.sync, "w2b", [P, HEAD], I32, w2_i32[:, HEAD:K])
         nc.sync.dma_start(idx3[:], offs3)
-        g_sb = keep.tile([P, 2, PACK], F32, name="g_sb")
+        raw3c = load(nc.sync, "raw3c", [P, PACK, K], F32, w3_rows[:, :, K:H])
+        w1c = load(nc.sync, "w1c", [P, K // 2], I32, w1_i32[:, K // 2:K])
+        w2c = load(nc.sync, "w2c", [P, K], I32, w2_i32[:, K:H])
 
-        grouped0 = keep.tile([P, P, PACK], BF16, name="grouped0", align_bytes=64)
-        quantise_w3(weave(raw0, P, nc.vector.tensor_copy, grouped0)[:], 0, 1)
+        priors = {}
 
-        vs = keep.tile([P, S], U8, name="vs", align_bytes=64)
-        nc.vector.tensor_copy(vs[:], tabs[:].indirect(idx[:]))
+        def load_prior(i):
+            rows = prior[i * P:(i + 1) * P, :] if i < PACK else prior[K:H, :].rearrange("(p t) m -> t p m", t=PACK)[i - PACK]
+            priors[i] = load(nc.sync, "prior%d" % (i % 5), [P, PR], F32, rows)
 
-        def page_of(i):
-            return pages[min(i, TILES - 2) % 2]
+        load_prior(0)
+        load_prior(1)
+        wg_dealt = {}
 
-        vw = []
-        for half in range(2):
-            words = keep.tile([P, BANK], U32, name="vw%d" % half, align_bytes=64)
-            nc.vector.tensor_copy(words[:], tabw[:].bitcast(U32).indirect(idx[:, 32 * half:32 * half + 32]))
-            vw.append(words)
+        def load_weights(t):
+            wg_dealt[t] = slot("wg_dealt%d" % t, [P, S], F32)
+            for a in (0, 2, 1, 3):
+                nc.sync.dma_start(wg_dealt[t][32 * a:32 * a + 32, :], wgs.rearrange("(c t) j -> t c j", t=PACK)[t])
 
         ident = keep.tile([P, P], F32, name="ident")
         make_identity(nc, ident[:])
         pages = []
         for k in range(2):
             page = keep.tile([P, T2], F32, name="page%d" % k)
-            nc.gpsimd.memset(page[:], 0.0)
+            (nc.vector, nc.gpsimd)[k].memset(page[:], 0.0)
             pages.append(page)
 
-        w1_dealt = [lot(PACK + t, [P, 2 * P], U8, "w1_dealt") for t in range(PACK)]
-        w2_dealt = keep.tile([P, PACK, P], I32, name="w2_dealt", align_bytes=64)
-        s1_dealt = keep.tile([P, PACK, P], U8, name="s1_dealt", align_bytes=64)
-        s2_dealt = keep.tile([P, PACK, P], U8, name="s2_dealt", align_bytes=64)
+        vs = slot("vs", [P, S], U8)
+        nc.vector.tensor_copy(vs[:], tabs[:].indirect(idx[:]))
+        vw = []
+        for half in range(2):
+            words = slot("vw%d" % half, [P, BANK], U32)
+            nc.vector.tensor_copy(words[:], tabw[:].bitcast(U32).indirect(half_list(idx, half)))
+            vw.append(words)
+
+        s1_dealt = slot("s1_dealt", [P, PACK, P], U8)
+        s2_dealt = slot("s2_dealt", [P, PACK, P], U8)
         nc.gpsimd.tensor_copy(s1_dealt[:], w1s[:, K:H].rearrange("k (p t) -> k t p", t=PACK))
         nc.gpsimd.tensor_copy(s2_dealt[:], w2s[:, K:H].rearrange("k (p t) -> k t p", t=PACK))
-        nc.gpsimd.tensor_copy(w2_dealt[:], w2b[:, K - HEAD:H - HEAD].rearrange("k (p t) -> k t p", t=PACK))
-        for t in range(PACK):
-            nc.gpsimd.tensor_copy(w1_dealt[t][:].rearrange("k (p b) -> k p b", b=2),
-                                  w1c[:].bitcast(U8).rearrange("k (p t b) -> k t p b", t=PACK, b=2)[:, t, :, :])
 
-        def stationary(i):
-            codes, scales = w3q[i]
-            third = (codes.bitcast(E4M3), scales)
+        def weave(raw, tag, width):
+            woven = slot(tag, [P, width, PACK], BF16)
+            nc.scalar.copy(woven[:].rearrange("p (c i) t -> p c t i", i=4), raw.rearrange("p t (c i) -> p c t i", i=4))
+            return woven
+
+        def quantise(woven, codes, scales):
+            nc.vector.quantize_mx(out=codes.bitcast(E4M3), scales=scales, in_=woven.rearrange("p c t -> p (c t)"))
+            return codes, scales
+
+        w3q = {}
+
+        def quantise_w3(woven, first, count, codes):
+            scales = slot("w3_scales%d" % first, [P, count * P], U8)
+            quantise(woven, codes, scales[:])
+            for k in range(count):
+                w3q[first + k] = codes[:, k * P:(k + 1) * P], scales[:, k * P:(k + 1) * P]
+
+        dealt = {}
+
+        def deal_words():
+            both = slot("raw3b", [P, 3 * K // 2], I32)
+            w1_dealt = both[:, K:3 * K // 2].bitcast(U8).rearrange("k (t p b) -> k t p b", t=PACK, b=2)
+            w2_dealt = both[:, 0:K].rearrange("k (t p) -> k t p", t=PACK)
+            nc.gpsimd.tensor_copy(w1_dealt, w1c[:].bitcast(U8).rearrange("k (p t b) -> k t p b", t=PACK, b=2))
+            nc.gpsimd.tensor_copy(w2_dealt, w2c[:].rearrange("k (p t) -> k t p", t=PACK))
+            dealt[1] = both[:, K:3 * K // 2]
+            dealt[2] = both[:, 0:K]
+
+        def stationary(i, which):
+            if which == 2:
+                codes, scales = w3q[i]
+                return codes.bitcast(E4M3), scales
             if i >= PACK:
                 t = i - PACK
-                return [(w1_dealt[t][:].bitcast(E2M1), s1_dealt[:, t, :]), (w2_dealt[:, t, :].bitcast(E4M3), s2_dealt[:, t, :]), third]
+                if which == 0:
+                    return dealt[1][:, t * P // 2:(t + 1) * P // 2].bitcast(E2M1), s1_dealt[:, t, :]
+                return dealt[2][:, t * P:(t + 1) * P].bitcast(E4M3), s2_dealt[:, t, :]
             a, b, at = (w1a, w2a, i * P) if i * P < HEAD else (w1b, w2b, i * P - HEAD)
             cols = slice(i * P, (i + 1) * P)
-            return [(a[:, at // 2:(at + P) // 2].bitcast(E2M1), w1s[:, cols]), (b[:, at:at + P].bitcast(E4M3), w2s[:, cols]), third]
+            if which == 0:
+                return a[:, at // 2:(at + P) // 2].bitcast(E2M1), w1s[:, cols]
+            return b[:, at:at + P].bitcast(E4M3), w2s[:, cols]
 
-        def signature(i, which, half):
-            lhs, lhs_scale = stationary(i)[which]
-            bank = psum.tile([P, BANK], F32, name="sig", bufs=SIG)
+        def signature(i, which, half, n):
+            lhs, lhs_scale = stationary(i, which)
+            bank = bank_tile(n, [P, BANK])
             nc.tensor.matmul_mx(out=bank[:], lhsT=lhs, lhsT_scale=lhs_scale, rhs=vw[half][:].bitcast(E4M3),
-                                rhs_scale=vs[:, half * BANK:(half + 1) * BANK], start=True, stop=True)
+                                rhs_scale=vs[:, half_cols(half)], start=True, stop=True)
             return bank
 
-        def put_vector(i):
-            src = wg
-            for k, which in enumerate((2, 0, 1)):
-                part = ring.tile([P, S], F32, name="d%d" % (k + 1), bufs=3) if k < 2 else lot(8, [P, S], F32, "h")
+        joint = {}
+
+        def join_vector(i, h):
+            part = slot("h%d" % (i % 3), [P, S], F32)
+            for n, (which, src, dst) in enumerate(((1, wg, part), (2, part, part), (0, part, h))):
                 for half in range(2):
-                    cols = slice(half * BANK, (half + 1) * BANK)
-                    nc.vector.tensor_tensor(part[:, cols], signature(i, which, half)[:], src[:, cols], MULT)
-                src = part
-            nc.vector.tensor_copy(page_of(i)[:].indirect(idx2[:]), src[:])
+                    cols = half_cols(half)
+                    nc.vector.tensor_tensor(dst[:, cols], signature(i, which, half, 2 * n + half)[:], src[:, cols], MULT)
+            joint[i] = h
 
-        def put_gpsimd(i, halves, between=None):
-            page = page_of(i)
-            cols = slice(halves[0] * BANK, (halves[-1] + 1) * BANK)
-            d = [lot(1 + w // 2, [P, S], F32, "d_last") if i == TILES - 1 and w != 1 else
-                 ring.tile([P, S], F32, name="d%d" % (w + 1), bufs=3) for w in range(3)]
-            for w in (2, 1, 0):
-                for half in halves:
-                    nc.scalar.copy(d[w][:, half * BANK:(half + 1) * BANK], signature(i, w, half)[:])
-            if between is not None:
-                between()
-            h = lot(i - 1, [P, S], F32, "h")
-            nc.gpsimd.tensor_tensor(d[2][:, cols], d[2][:, cols], weights[i][:, cols], MULT)
-            nc.gpsimd.tensor_tensor(d[2][:, cols], d[2][:, cols], d[1][:, cols], MULT)
-            nc.gpsimd.tensor_tensor(h[:, cols], d[0][:, cols], d[2][:, cols], MULT)
-            return lambda: nc.vector.tensor_copy(page[:].indirect(idx2[:, 32 * halves[0]:32 * halves[-1] + 32]), h[:, cols])
+        def copy_out(i, d, banks):
+            for (which, half), n in banks:
+                nc.scalar.copy(d[which][:, half_cols(half)], signature(i, which, half, n)[:])
+            return d
 
-        squashed = keep.tile([P, PR // P, PACK, P], F32, name="squashed")
-        z1_woven = keep.tile([P, PR, PACK], BF16, name="z1_woven", align_bytes=64)
-        priors = {}
-        weights = {i: wg for i in range(PACK)}
+        def weights(i):
+            return wg[:] if i < PACK else wg_dealt[i - PACK][:]
 
-        def load_prior(i):
-            rows = prior[i * P:(i + 1) * P, :] if i < PACK else prior[K:H, :].rearrange("(p t) m -> t p m", t=PACK)[i - PACK]
-            priors[i] = ring.tile([P, PR], F32, name="prior_sb", bufs=3)
-            nc.sync.dma_start(priors[i][:], rows)
+        def scatter(i):
+            nc.vector.tensor_copy(pages[i % 2][:].indirect(idx2[:]), joint[i])
 
-        def load_weights(i):
-            weights[i] = ring.tile([P, S], F32, name="wg_dealt")
-            rows = wgs.rearrange("(p t) j -> t p j", t=PACK)[i - PACK]
-            nc.sync.dma_start(weights[i][:], rows.unsqueeze(0).to_broadcast([PACK, P // PACK, S]))
+        squashed = slot("tab", [P, PR // P, PACK, P], F32)
+        g_sb = keep.tile([P, 2, PACK], F32, name="g_sb")
+        z1 = {}
+        turns = []
 
-        def turn(terms, m0, width):
-            blocks = width // P
-            bank = psum.tile([P, blocks, P], F32, name="turned", bufs=TURN)
-            for n, src in enumerate(terms):
-                for k in range(blocks):
-                    nc.tensor.matmul(bank[:, k, :], src[:, m0 + k * P:m0 + (k + 1) * P], ident[:], is_transpose=True,
-                                     start=n == 0 and k == 0, stop=n == len(terms) - 1 and k == blocks - 1)
-            return bank
+        def turn_bank(shape):
+            turns.append(0)
+            return bank_tile(SUM_BANKS + len(turns) % 2, shape)
 
-        def squash_slot(t, y, tz, cols):
-            nc.scalar.activation(tz[:], y[:], ACT.Tanh)
-            if t == PACK - 1 and GV:
-                nc.vector.tensor_scalar(z1_woven[:, cols, t], tz[:], g_sb[:, 1, t:t + 1], None, MULT)
-            else:
-                nc.scalar.activation(z1_woven[:, cols, t], tz[:], ACT.Copy, scale=g_sb[:, 1, t:t + 1])
+        def squash_dealt(i, half, x, y, tz, spare=False):
+            cols = half_cols(half)
+            t = i - PACK
+            nc.gpsimd.tensor_tensor(y, x, priors[i][:, cols], ADD)
+            nc.scalar.activation(tz, y, ACT.Tanh)
+            if spare:
+                return lambda: nc.gpsimd.tensor_scalar(z1["woven"][:, cols, t], tz, g_sb[:, 1, t:t + 1], 0.0, MULT, ADD)
+            nc.scalar.activation(z1["woven"][:, cols, t], tz, ACT.Copy, scale=g_sb[:, 1, t:t + 1])
 
-        def fetch_whole(i):
-            x = lot(X_LOT[i], [P, PR], F32, "x")
-            nc.vector.tensor_copy(x[:], page_of(i)[:].indirect(idx3[:]))
+        waiting = []
+
+        def fetch(i, half, x):
+            cols = half_cols(half)
+            nc.vector.tensor_copy(x, pages[i % 2][:].indirect(half_list(idx3, half)))
             if i >= PACK:
-                y = lot(i - 3, [P, PR], F32, "y") if i < 6 else x
-                nc.gpsimd.tensor_tensor(y[:], x[:], priors[i][:], ADD)
-                squash_slot(i - PACK, y, ring.tile([P, PR], F32, name="planes", bufs=1), slice(0, PR))
+                waiting.append((i, half, x))
                 return
-            for m0 in (0, BANK):
-                bank = turn((priors[i], x), m0, BANK)
-                nc.scalar.activation(squashed[:, m0 // P:m0 // P + PACK, :, 32 * i:32 * i + 32],
-                                     bank[:].rearrange("m k (p t) -> m k t p", t=PACK), ACT.Tanh)
+            bank = turn_bank([P, PACK, P])
+            for n, src in enumerate((priors[i][:, cols], x)):
+                for k in range(PACK):
+                    nc.tensor.matmul(bank[:, k, :], src[:, k * P:(k + 1) * P], ident[:], is_transpose=True,
+                                     start=n == 0 and k == 0, stop=n == 1 and k == PACK - 1)
+            nc.scalar.activation(squashed[:, PACK * half:PACK * (half + 1), :, 32 * i:32 * i + 32],
+                                 bank[:].rearrange("m k (p t) -> m k t p", t=PACK), ACT.Tanh)
 
-        def weave_z0(m0, n):
-            planes = ring.tile([P, PACK, BANK], BF16, name="planes", bufs=1)
+        def weave_z0(half):
+            planes = slot("planes%d" % half, [P, PACK, BANK], BF16)
             for t in range(PACK):
-                bank = psum.tile([P, BANK], F32, name="sig", bufs=SIG)
-                for k in range(BANK // P):
-                    nc.tensor.transpose(bank[:, k * P:(k + 1) * P], squashed[:, m0 // P + k, t, :], ident[:])
+                bank = turn_bank([P, BANK])
+                for k in range(PACK):
+                    nc.tensor.transpose(bank[:, k * P:(k + 1) * P], squashed[:, PACK * half + k, t, :], ident[:])
                 nc.scalar.activation(planes[:, t, :], bank[:], ACT.Copy, scale=g_sb[:, 0, t:t + 1])
-            return weave(planes, BANK, nc.scalar.copy, lot(n, [P, BANK, PACK], BF16, "z0_woven"))
+            return weave(planes[:], "z0_woven%d" % half, BANK)
 
-        w4q = []
-        z0 = []
+        def in_order(order, first=0):
+            return [((which, half), (first + 2 * n + half) % 8) for n, which in enumerate(order) for half in range(2)]
 
-        def estimate_pass(b, banks, z_codes, z_scales):
-            codes, scales = w4q[b]
-            for n in range(N // P):
-                cols = slice(n * P, (n + 1) * P)
-                nc.tensor.matmul_mx(out=banks[n // 2][:, n % 2, :], lhsT=codes[:, cols].bitcast(E4M3), lhsT_scale=scales[:, cols],
-                                    rhs=z_codes.bitcast(E4M3), rhs_scale=z_scales,
-                                    start=b == 0 and n % 2 == 0, stop=b == 1 and n % 2 == 1)
+        def ring(i):
+            return [slot(tag, [P, S], F32)[:] for tag in ("u%d" % (i % 2), "d2_%d" % (i % 2), "d3_%d" % (i % 3))]
 
-        def estimate_open(m0, width):
-            tag, bufs = ("sig", SIG) if m0 + width < PR else ("turned", TURN)
-            banks = [psum.tile([P, 2, width], F32, name=tag, bufs=bufs) for pair in range(2)]
-            codes, scales = z0[m0 // BANK]
-            at = m0 % BANK
-            estimate_pass(0, banks, codes[:, at:at + width], scales[:, at:at + width])
-            return banks
-
-        def estimate_close(m0, width, banks, z1, both):
-            estimate_pass(1, banks, z1[0], z1[1])
-            for pair in range(2):
-                res = both[:, pair, :, :]
-                if (2 * (m0 // 256) + pair) in ONS:
-                    nc.scalar.copy(res, banks[pair][:])
-                else:
-                    nc.vector.tensor_copy(res, banks[pair][:])
-                nc.sync.dma_start(out[2 * pair * P:2 * (pair + 1) * P, m0:m0 + width].rearrange("(k p) m -> p k m", p=P), res)
-
-        AHEAD = 3
-        puts = {}
-        load_prior(0)
-        woven = weave(raw1, 3 * P, nc.scalar.copy, lot(8, [P, 3 * P, PACK], BF16, "w3_woven"))
-        quantise_w3(woven[:, 0:P, :], 1, 1)
-        quantise_w3(woven[:, P:3 * P, :], 2, 2)
-        put_vector(0)
-        late_codes = lot(8, [P, 2, 2 * P], U32, "w3_codes")
-        late = [(lot(n, [P, 2 * P, PACK], BF16, "w3_woven"), k) for k, n in enumerate((0, X_LOT[0]))]
-
-        def late_w3():
-            for grouped, k in late:
-                nc.scalar.copy(grouped[:].rearrange("k (t p) j -> k t p j", t=2),
-                               raw3[:].rearrange("k j (p t) -> k t p j", t=PACK)[:, 2 * k:2 * k + 2, :, :])
-                quantise_w3(grouped[:], PACK + 2 * k, 2, late_codes[:, k, :])
-
-        puts[1] = put_gpsimd(1, (0, 1), late_w3)
-        puts[2] = put_gpsimd(2, (0, 1))
-        w4_woven = []
-        for i in range(TILES):
-            if i + 1 < TILES:
-                load_prior(i + 1)
-            if i in (1, 2):
-                raw4 = load_raw(w4[(i - 1) * K:i * K, :].rearrange("(p j) n -> p j n", j=PACK), N, "raw", 2)
-            if i == 2:
-                nc.sync.dma_start(g_sb[:], gain.rearrange("(b p t) -> p b t", p=P, t=PACK))
-            if PACK <= i + AHEAD < TILES:
-                load_weights(i + AHEAD)
-            if i > 0:
-                puts[i]()
-            if i + AHEAD < TILES:
-                puts[i + AHEAD] = put_gpsimd(i + AHEAD, (0, 1))
-            if i in (1, 2):
-                w4_woven.append(weave(raw4, BANK, nc.scalar.copy))
-            if i == 4:
-                z0_woven = [weave_z0(0, 3), weave_z0(BANK, X_LOT[6])]
-            if i < 6:
-                fetch_whole(i)
-            if i == 6:
-                codes = lot(W4LOT, [P, 2, N], U32, "w4_codes")
-                for b in range(2):
-                    w4q.append(quantise(w4_woven[b][:], codes[:, b, :], own(N, U8, "w4_scales%d" % b)))
-                codes = lot(5, [P, 2, BANK], U32, "z0_codes")
+        def join_halves(d, v, h):
+            for which, src, dst in ((2, wg, v), (1, v, v), (0, v, h)):
                 for half in range(2):
-                    z0.append(quantise(z0_woven[half][:], codes[:, half, :], own(BANK, U8, "z0_scales%d" % half)))
-                fetch_whole(6)
+                    cols = half_cols(half)
+                    nc.gpsimd.tensor_tensor(dst[:, cols], d[which][:, cols], src[:, cols], MULT)
+
+        def join_gpsimd(i):
+            if i == 3:
+                u, d3, d2 = ring(i)
+                d = copy_out(i, [u, d2, d3], in_order((0, 2, 1)))
+                woven = slot("woven3c", [P, K, PACK], BF16)
+                for k in range(2):
+                    nc.scalar.copy(woven[:, k * HEAD:(k + 1) * HEAD, :].rearrange("k (t p) j -> k t p j", t=2),
+                                   raw3c[:].rearrange("k j (p t) -> k t p j", t=PACK)[:, 2 * k:2 * k + 2, :, :])
+                joint["late"] = lambda: late(woven, d)
+                return
+            d = copy_out(i, ring(i), in_order((0, 1, 2)))
+            nc.gpsimd.tensor_tensor(d[0], d[0], d[1], MULT)
+            if i == TILES - 1:
+                joint["last"] = d
+                return
+            v = slot("v2" if i == 2 else "h%d" % (i % 3), [P, S], F32)
+            nc.gpsimd.tensor_tensor(v[:], d[2], weights(i), MULT)
+            h = v
+            if i == 2:
+                deal_words()
+                join_gpsimd(3)
+                h = slot("raw3c", [P, S], F32)
+            nc.gpsimd.tensor_tensor(h[:], d[0], v[:], MULT)
+            joint[i] = h[:]
+
+        def late(woven, d):
+            quantise_w3(woven[:], PACK, PACK, slot("v2", [P, K], U32)[:])
+            h = slot("woven3c", [P, S], F32)
+            join_halves(d, h, h)
+            joint[3] = h[:]
+
+        quantise_w3(weave(raw3a[:], "woven3a", HEAD)[:], 0, 2, slot("w3_codes0", [P, HEAD], U32)[:])
+        quantise_w3(weave(raw3b[:], "woven3b", HEAD)[:], 2, 2, slot("w3_codes2", [P, HEAD], U32)[:])
+        early = slot("woven3b", [P, 2, S], F32)
+        join_vector(0, early[:, 0, :])
+        scatter(0)
+
+        three = slot("raw3b", [P, 3, S], F32)
+        d = copy_out(1, [three[:, which, :] for which in range(3)], in_order((2, 1, 0), 6))
+        join_halves(d, early[:, 1, :], early[:, 1, :])
+        joint[1] = early[:, 1, :]
+        join_gpsimd(2)
+
+        raw4 = [load(nc.sync, tag, [P, PACK, N], F32, w4[b * K:(b + 1) * K, :].rearrange("(p j) n -> p j n", j=PACK))
+                for b, tag in enumerate(("z0_woven0", "z1_woven"))]
+        load_weights(0)
+        load_prior(2)
+        load_weights(1)
+        load_prior(3)
+        nc.sync.dma_start(g_sb[:], gain.rearrange("(b p t) -> p b t", p=P, t=PACK))
+        load_weights(2)
+        load_weights(3)
+
+        w4_woven = []
+        z0_woven = []
+        fetch(0, 0, slot("x0", [P, BANK], F32)[:])
+        for i in range(1, TILES - 1):
+            if i == 2:
+                joint["late"]()
+            scatter(i)
+            if i == 2:
+                join_gpsimd(4)
+            if 2 <= i < TILES - 3:
+                join_gpsimd(i + 3)
+            if i < TILES - 2:
+                pair = slot("d3_%d" % ((i + 1) % 3), [P, 2, BANK], F32)
+                fetch(i - 1, 1, pair[:, 0, :])
+                if i == PACK:
+                    z0_woven.append(weave_z0(1))
+                    d = joint["last"]
+                    v = slot("planes0", [P, S], F32)
+                    h = slot("h%d" % ((TILES - 1) % 3), [P, S], F32)
+                    nc.gpsimd.tensor_tensor(v[:], d[2], weights(TILES - 1), MULT)
+                    nc.gpsimd.tensor_tensor(h[:], d[0], v[:], MULT)
+                    joint[TILES - 1] = h[:]
+                fetch(i, 0, pair[:, 1, :])
+            if i + 3 < TILES:
+                load_prior(i + 3)
+            if i in (1, 2):
+                w4_woven.append(weave(raw4[i - 1][:], "w4_woven%d" % (i - 1), N))
+            if i == 2:
+                z1["woven"] = slot("z1_woven", [P, PR, PACK], BF16)
+            if i == PACK - 1:
+                z0_woven.append(weave_z0(0))
 
         last = TILES - 1
-        chunks = [(sum(CHUNKS[:c]), width) for c, width in enumerate(CHUNKS)]
-        opened = [estimate_open(m0, width) for m0, width in chunks]
-        z1 = []
-        for half in range(2):
-            x = ring.tile([P, BANK], F32, name="planes" if half == 1 and PIN else "x_tail%d" % half, bufs=1)
-            tz = ring.tile([P, BANK], F32, name="planes" if half == 0 else "tz_tail", bufs=1)
-            mine = [(m0, width, slice(m0 % BANK, m0 % BANK + width)) for m0, width in chunks if m0 // BANK == half]
-            for m0, width, cols in mine:
-                nc.vector.tensor_tensor(x[:, cols], page_of(last)[:].indirect(idx3[:, m0 // 16:(m0 + width) // 16]),
-                                        priors[last][:, m0:m0 + width], ADD)
-            for m0, width, cols in mine:
-                squash_slot(PACK - 1, x[:, cols], tz[:, cols], slice(m0, m0 + width))
-                z1.append(quantise(z1_woven[:, m0:m0 + width, :], own(width, U32, "z1_codes%d" % m0), own(width, U8, "z1_scales%d" % m0)))
-        for c, (m0, width) in enumerate(chunks):
-            estimate_close(m0, width, opened[c], z1[c], lot(RES_LOT[c], [P, 2, 2, width], F32, "res"))
+        sums = slot("planes0", [P, 3, BANK], F32)
+        bent = slot("planes1", [P, BANK], F32)
+        for n, (i, half, x) in enumerate(waiting):
+            squash_dealt(i, half, x, sums[:, n, :], bent[:])
+        waiting.clear()
+        codes = slot("d3_0", [P, 2 * N + PR], U32)
+        z0_codes = codes[:, 2 * N:2 * N + PR]
+        z0_scales = slot("z0_scales", [P, PR], U8)
+        for half in (1, 0):
+            quantise(z0_woven[half][:], z0_codes[:, half_cols(half)], z0_scales[:, half_cols(half)])
+        w4q = [quantise(w4_woven[b][:], codes[:, b * N:(b + 1) * N], slot("w4_scales%d" % b, [P, N], U8)[:]) for b in range(2)]
+        three = slot("z0_woven1", [P, 3, BANK], F32)
+        fetch(last - 1, 0, three[:, 0, :])
+        fetch(last - 2, 1, three[:, 1, :])
+        fetch(last - 1, 1, three[:, 2, :])
+        bent = slot("planes1", [P, 3, BANK], F32)
+        gains = [squash_dealt(i, half, x, x, bent[:, n, :], half == 1) for n, (i, half, x) in enumerate(waiting)]
+        for put in gains[1:]:
+            put()
+        scatter(last)
+
+        chunks = [slice(sum(CHUNKS[:c]), sum(CHUNKS[:c + 1])) for c in range(len(CHUNKS))]
+
+        def estimate_pass(b, banks, z_codes, z_scales):
+            w_codes, w_scales = w4q[b]
+            per_bank = N // P // len(banks)
+            for n in range(N // P):
+                cols = slice(n * P, (n + 1) * P)
+                nc.tensor.matmul_mx(out=banks[n // per_bank][:, n % per_bank, :], lhsT=w_codes[:, cols].bitcast(E4M3),
+                                    lhsT_scale=w_scales[:, cols], rhs=z_codes.bitcast(E4M3), rhs_scale=z_scales,
+                                    start=b == 0 and n % per_bank == 0, stop=b == 1 and n % per_bank == per_bank - 1)
+
+        opened = []
+        for c, cols in enumerate(chunks):
+            banks = [bank_tile(n, [P, BANK // CHUNKS[c], CHUNKS[c]]) for n in range(cols.start // P, cols.stop // P)]
+            estimate_pass(0, banks, z0_codes[:, cols], z0_scales[:, cols])
+            opened.append(banks)
+
+        res = slot("tab", [P, PR // P, BANK], F32)
+        squash = {}
+        x_tail = slot("planes1", [P, 2, max(CHUNKS)], F32)
+
+        def tail_fetch(c):
+            cols = chunks[c]
+            x = x_tail[:, c % 2, 0:CHUNKS[c]]
+            nc.vector.tensor_tensor(x, pages[last % 2][:].indirect(idx3[:, cols.start // 16:cols.stop // 16]),
+                                    priors[last][:, cols], ADD)
+            squash[c] = slot("tz%d" % c, [P, CHUNKS[c]], F32)
+            nc.scalar.activation(squash[c][:], x, ACT.Tanh)
+
+        def tail_gain(c):
+            nc.vector.tensor_scalar(z1["woven"][:, chunks[c], PACK - 1], squash[c][:], g_sb[:, 1, PACK - 1:PACK], None, MULT)
+
+        def tail_close(c):
+            cols = chunks[c]
+            z_codes, z_scales = quantise(z1["woven"][:, cols, :], slot("z1_codes%d" % c, [P, CHUNKS[c]], U32)[:],
+                                         slot("z1_scales%d" % c, [P, CHUNKS[c]], U8)[:])
+            estimate_pass(1, opened[c], z_codes, z_scales)
+            for n, bank in enumerate(opened[c]):
+                rows = N // len(opened[c])
+                staged = res[:, cols.start // P + n, :].rearrange("p (k m) -> p k m", m=CHUNKS[c])
+                copy = nc.vector.tensor_copy if c == len(chunks) - 1 else nc.scalar.copy
+                copy(staged, bank[:])
+                nc.sync.dma_start(out[n * rows:(n + 1) * rows, cols].rearrange("(k p) m -> p k m", p=P), staged)
+
+        tail_fetch(0)
+        tail_fetch(1)
+        for c in range(len(chunks)):
+            tail_gain(c)
+            if c + 2 < len(chunks):
+                tail_fetch(c + 2)
+            tail_close(c)

@@ -184,10 +184,10 @@ def tile_list_semijoin_cache_kernel(tc, tab_words, tab_scales, offs, offs2, offs
 
         def join_vector(i, h):
             part = slot("h%d" % (i % 3), [P, S], F32)
-            for n, (which, src, dst) in enumerate(((1, wg, part), (2, part, part), (0, part, h))):
+            for first, which, src, dst in ((0, 1, wg, part), (2, 0, part, part), (2, 2, part, h)):
                 for half in range(2):
                     cols = half_cols(half)
-                    nc.vector.tensor_tensor(dst[:, cols], signature(i, which, half, 2 * n + half)[:], src[:, cols], MULT)
+                    nc.vector.tensor_tensor(dst[:, cols], signature(i, which, half, first + half)[:], src[:, cols], MULT)
             joint[i] = h
 
         def copy_out(i, d, banks):
@@ -221,17 +221,20 @@ def tile_list_semijoin_cache_kernel(tc, tab_words, tab_scales, offs, offs2, offs
 
         waiting = []
 
+        def turned_sum(bank, first, second):
+            for n, src in enumerate((first, second)):
+                for k in range(PACK):
+                    nc.tensor.matmul(bank[:, k, :], src[:, k * P:(k + 1) * P], ident[:], is_transpose=True,
+                                     start=n == 0 and k == 0, stop=n == 1 and k == PACK - 1)
+            return bank
+
         def fetch(i, half, x):
             cols = half_cols(half)
             nc.vector.tensor_copy(x, pages[i % 2][:].indirect(half_list(idx3, half)))
             if i >= PACK:
                 waiting.append((i, half, x))
                 return
-            bank = turn_bank([P, PACK, P])
-            for n, src in enumerate((priors[i][:, cols], x)):
-                for k in range(PACK):
-                    nc.tensor.matmul(bank[:, k, :], src[:, k * P:(k + 1) * P], ident[:], is_transpose=True,
-                                     start=n == 0 and k == 0, stop=n == 1 and k == PACK - 1)
+            bank = turned_sum(turn_bank([P, PACK, P]), priors[i][:, cols], x)
             nc.scalar.activation(squashed[:, PACK * half:PACK * (half + 1), :, 32 * i:32 * i + 32],
                                  bank[:].rearrange("m k (p t) -> m k t p", t=PACK), ACT.Tanh)
 
@@ -250,11 +253,11 @@ def tile_list_semijoin_cache_kernel(tc, tab_words, tab_scales, offs, offs2, offs
         def ring(i):
             return [slot(tag, [P, S], F32)[:] for tag in ("u%d" % (i % 2), "d2_%d" % (i % 2), "d3_%d" % (i % 3))]
 
-        def join_halves(d, v, h):
-            for which, src, dst in ((2, wg, v), (1, v, v), (0, v, h)):
+        def join_halves(order, d, h):
+            for which, src in zip(order, (wg, h, h)):
                 for half in range(2):
                     cols = half_cols(half)
-                    nc.gpsimd.tensor_tensor(dst[:, cols], d[which][:, cols], src[:, cols], MULT)
+                    nc.gpsimd.tensor_tensor(h[:, cols], d[which][:, cols], src[:, cols], MULT)
 
         def join_gpsimd(i):
             if i == 3:
@@ -284,7 +287,7 @@ def tile_list_semijoin_cache_kernel(tc, tab_words, tab_scales, offs, offs2, offs
         def late(woven, d):
             quantise_w3(woven[:], PACK, PACK, slot("v2", [P, K], U32)[:])
             h = slot("woven3c", [P, S], F32)
-            join_halves(d, h, h)
+            join_halves((2, 1, 0), d, h)
             joint[3] = h[:]
 
         quantise_w3(weave(raw3a[:], "woven3a", HEAD)[:], 0, 2, slot("w3_codes0", [P, HEAD], U32)[:])
@@ -294,8 +297,8 @@ def tile_list_semijoin_cache_kernel(tc, tab_words, tab_scales, offs, offs2, offs
         scatter(0)
 
         three = slot("raw3b", [P, 3, S], F32)
-        d = copy_out(1, [three[:, which, :] for which in range(3)], in_order((2, 1, 0), 6))
-        join_halves(d, early[:, 1, :], early[:, 1, :])
+        d = copy_out(1, [three[:, which, :] for which in range(3)], [((1, 0), 6), ((1, 1), 7), ((2, 0), 6), ((2, 1), 7), ((0, 0), 4), ((0, 1), 5)])
+        join_halves((1, 2, 0), d, early[:, 1, :])
         joint[1] = early[:, 1, :]
         join_gpsimd(2)
 

@@ -24,6 +24,8 @@ BANK = 512
 TILES = H // P
 HEAD = 2 * P
 SUM_BANKS = 6
+ON_VECTOR = ((4, 1),)
+SCALAR_GAINS = (1,)
 TAB_FIRST = 3 * T // 8
 CHUNKS = (128, 256, 256, 256, 128)
 
@@ -198,8 +200,11 @@ def tile_list_semijoin_cache_kernel(tc, tab_words, tab_scales, offs, offs2, offs
         def weights(i):
             return wg[:] if i < PACK else wg_dealt[i - PACK][:]
 
+        def page_of(i):
+            return pages[min(i, TILES - 2) % 2]
+
         def scatter(i):
-            nc.vector.tensor_copy(pages[i % 2][:].indirect(idx2[:]), joint[i])
+            nc.vector.tensor_copy(page_of(i)[:].indirect(idx2[:]), joint[i])
 
         squashed = slot("tab", [P, PR // P, PACK, P], F32)
         g_sb = keep.tile([P, 2, PACK], F32, name="g_sb")
@@ -210,13 +215,11 @@ def tile_list_semijoin_cache_kernel(tc, tab_words, tab_scales, offs, offs2, offs
             turns.append(0)
             return bank_tile(SUM_BANKS + len(turns) % 2, shape)
 
-        def squash_dealt(i, half, x, y, tz, spare=False):
+        def squash_dealt(i, half, x, y, tz):
             cols = half_cols(half)
             t = i - PACK
             nc.gpsimd.tensor_tensor(y, x, priors[i][:, cols], ADD)
             nc.scalar.activation(tz, y, ACT.Tanh)
-            if spare:
-                return lambda: nc.gpsimd.tensor_scalar(z1["woven"][:, cols, t], tz, g_sb[:, 1, t:t + 1], 0.0, MULT, ADD)
             nc.scalar.activation(z1["woven"][:, cols, t], tz, ACT.Copy, scale=g_sb[:, 1, t:t + 1])
 
         waiting = []
@@ -230,7 +233,7 @@ def tile_list_semijoin_cache_kernel(tc, tab_words, tab_scales, offs, offs2, offs
 
         def fetch(i, half, x):
             cols = half_cols(half)
-            nc.vector.tensor_copy(x, pages[i % 2][:].indirect(half_list(idx3, half)))
+            nc.vector.tensor_copy(x, page_of(i)[:].indirect(half_list(idx3, half)))
             if i >= PACK:
                 waiting.append((i, half, x))
                 return
@@ -324,7 +327,7 @@ def tile_list_semijoin_cache_kernel(tc, tab_words, tab_scales, offs, offs2, offs
             if 2 <= i < TILES - 3:
                 join_gpsimd(i + 3)
             if i < TILES - 2:
-                pair = slot("d3_%d" % ((i + 1) % 3), [P, 2, BANK], F32)
+                pair = slot("d3_%d" % ((i + 1) % 3), [P, 3 if i == TILES - 3 else 2, BANK], F32)
                 fetch(i - 1, 1, pair[:, 0, :])
                 if i == PACK:
                     z0_woven.append(weave_z0(1))
@@ -335,6 +338,8 @@ def tile_list_semijoin_cache_kernel(tc, tab_words, tab_scales, offs, offs2, offs
                     nc.gpsimd.tensor_tensor(h[:], d[0], v[:], MULT)
                     joint[TILES - 1] = h[:]
                 fetch(i, 0, pair[:, 1, :])
+                if i == TILES - 3:
+                    fetch(i, 1, pair[:, 2, :])
             if i + 3 < TILES:
                 load_prior(i + 3)
             if i in (1, 2):
@@ -345,42 +350,51 @@ def tile_list_semijoin_cache_kernel(tc, tab_words, tab_scales, offs, offs2, offs
                 z0_woven.append(weave_z0(0))
 
         last = TILES - 1
-        sums = slot("planes0", [P, 3, BANK], F32)
-        bent = slot("planes1", [P, BANK], F32)
+        sums = slot("planes0", [P, 4, BANK], F32)
+        bent = slot("planes1", [P, 2, BANK], F32)
         for n, (i, half, x) in enumerate(waiting):
-            squash_dealt(i, half, x, sums[:, n, :], bent[:])
+            squash_dealt(i, half, x, sums[:, n, :], bent[:, n % 2, :])
         waiting.clear()
-        codes = slot("d3_0", [P, 2 * N + PR], U32)
-        z0_codes = codes[:, 2 * N:2 * N + PR]
-        z0_scales = slot("z0_scales", [P, PR], U8)
-        for half in (1, 0):
-            quantise(z0_woven[half][:], z0_codes[:, half_cols(half)], z0_scales[:, half_cols(half)])
+        codes = slot("d3_0", [P, 2 * N + BANK], U32)
+        z0 = [quantise(z0_woven[0][:], codes[:, 2 * N:2 * N + BANK], slot("z0_scales0", [P, BANK], U8)[:])]
         w4q = [quantise(w4_woven[b][:], codes[:, b * N:(b + 1) * N], slot("w4_scales%d" % b, [P, N], U8)[:]) for b in range(2)]
-        three = slot("z0_woven1", [P, 3, BANK], F32)
-        fetch(last - 1, 0, three[:, 0, :])
-        fetch(last - 2, 1, three[:, 1, :])
-        fetch(last - 1, 1, three[:, 2, :])
-        bent = slot("planes1", [P, 3, BANK], F32)
-        gains = [squash_dealt(i, half, x, x, bent[:, n, :], half == 1) for n, (i, half, x) in enumerate(waiting)]
-        for put in gains[1:]:
-            put()
+        x = slot("z0_woven0", [P, PR], F32)
+        bent = slot("planes1", [P, 2, BANK], F32)
+        for half in range(2):
+            fetch(last - 1, half, x[:, half_cols(half)])
+        for i, half, x in waiting:
+            squash_dealt(i, half, x, x, bent[:, half, :])
         scatter(last)
+        z0.append(quantise(z0_woven[1][:], slot("z0_woven0", [P, BANK], U32)[:], slot("z0_scales1", [P, BANK], U8)[:]))
 
         chunks = [slice(sum(CHUNKS[:c]), sum(CHUNKS[:c + 1])) for c in range(len(CHUNKS))]
 
-        def estimate_pass(b, banks, z_codes, z_scales):
+        def estimate_pass(b, banks, pieces):
             w_codes, w_scales = w4q[b]
             per_bank = N // P // len(banks)
-            for n in range(N // P):
-                cols = slice(n * P, (n + 1) * P)
-                nc.tensor.matmul_mx(out=banks[n // per_bank][:, n % per_bank, :], lhsT=w_codes[:, cols].bitcast(E4M3),
-                                    lhsT_scale=w_scales[:, cols], rhs=z_codes.bitcast(E4M3), rhs_scale=z_scales,
-                                    start=b == 0 and n % per_bank == 0, stop=b == 1 and n % per_bank == per_bank - 1)
+            for part, (at, z_codes, z_scales) in enumerate(pieces):
+                for n in range(N // P):
+                    cols = slice(n * P, (n + 1) * P)
+                    nc.tensor.matmul_mx(out=banks[n // per_bank][:, n % per_bank, at], lhsT=w_codes[:, cols].bitcast(E4M3),
+                                        lhsT_scale=w_scales[:, cols], rhs=z_codes.bitcast(E4M3), rhs_scale=z_scales,
+                                        start=b == 0 and part == 0 and n % per_bank == 0,
+                                        stop=b == 1 and n % per_bank == per_bank - 1)
+
+        def first_pass(banks, cols):
+            pieces = []
+            for half, (z_codes, z_scales) in enumerate(z0):
+                lo, hi = max(cols.start, half * BANK), min(cols.stop, (half + 1) * BANK)
+                if lo < hi:
+                    mine = slice(lo - half * BANK, hi - half * BANK)
+                    pieces.append((slice(lo - cols.start, hi - cols.start), z_codes[:, mine], z_scales[:, mine]))
+            estimate_pass(0, banks, pieces)
 
         opened = []
         for c, cols in enumerate(chunks):
+            if c == len(chunks) - 1:
+                break
             banks = [bank_tile(n, [P, BANK // CHUNKS[c], CHUNKS[c]]) for n in range(cols.start // P, cols.stop // P)]
-            estimate_pass(0, banks, z0_codes[:, cols], z0_scales[:, cols])
+            first_pass(banks, cols)
             opened.append(banks)
 
         res = slot("tab", [P, PR // P, BANK], F32)
@@ -390,23 +404,27 @@ def tile_list_semijoin_cache_kernel(tc, tab_words, tab_scales, offs, offs2, offs
         def tail_fetch(c):
             cols = chunks[c]
             x = x_tail[:, c % 2, 0:CHUNKS[c]]
-            nc.vector.tensor_tensor(x, pages[last % 2][:].indirect(idx3[:, cols.start // 16:cols.stop // 16]),
+            nc.vector.tensor_tensor(x, page_of(last)[:].indirect(idx3[:, cols.start // 16:cols.stop // 16]),
                                     priors[last][:, cols], ADD)
             squash[c] = slot("tz%d" % c, [P, CHUNKS[c]], F32)
             nc.scalar.activation(squash[c][:], x, ACT.Tanh)
 
         def tail_gain(c):
-            nc.vector.tensor_scalar(z1["woven"][:, chunks[c], PACK - 1], squash[c][:], g_sb[:, 1, PACK - 1:PACK], None, MULT)
+            if c in SCALAR_GAINS:
+                nc.scalar.activation(z1["woven"][:, chunks[c], PACK - 1], squash[c][:], ACT.Copy, scale=g_sb[:, 1, PACK - 1:PACK])
+            else:
+                nc.vector.tensor_scalar(z1["woven"][:, chunks[c], PACK - 1], squash[c][:], g_sb[:, 1, PACK - 1:PACK], None, MULT)
 
         def tail_close(c):
             cols = chunks[c]
             z_codes, z_scales = quantise(z1["woven"][:, cols, :], slot("z1_codes%d" % c, [P, CHUNKS[c]], U32)[:],
                                          slot("z1_scales%d" % c, [P, CHUNKS[c]], U8)[:])
-            estimate_pass(1, opened[c], z_codes, z_scales)
+            estimate_pass(1, opened[c], [(slice(0, CHUNKS[c]), z_codes, z_scales)])
+            staged_all = res[:, cols.start // P:cols.stop // P, :].rearrange("p b (k m) -> p (b k) m", m=CHUNKS[c])
             for n, bank in enumerate(opened[c]):
                 rows = N // len(opened[c])
-                staged = res[:, cols.start // P + n, :].rearrange("p (k m) -> p k m", m=CHUNKS[c])
-                copy = nc.vector.tensor_copy if c == len(chunks) - 1 else nc.scalar.copy
+                staged = staged_all[:, n * rows // P:(n + 1) * rows // P, :]
+                copy = nc.vector.tensor_copy if (c, n) in ON_VECTOR else nc.scalar.copy
                 copy(staged, bank[:])
                 nc.sync.dma_start(out[n * rows:(n + 1) * rows, cols].rearrange("(k p) m -> p k m", p=P), staged)
 
@@ -417,3 +435,7 @@ def tile_list_semijoin_cache_kernel(tc, tab_words, tab_scales, offs, offs2, offs
             if c + 2 < len(chunks):
                 tail_fetch(c + 2)
             tail_close(c)
+            if c == 0:
+                cols = chunks[-1]
+                opened.append([bank_tile(n, [P, 2, CHUNKS[-1]]) for n in (7, 0)])
+                first_pass(opened[-1], cols)

@@ -75,8 +75,8 @@ def tile_list_semijoin_cache_kernel(tc, tab_words, tab_scales, offs, offs2, offs
         w2_i32 = w2_words[0].rearrange("p c i -> p (c i)").bitcast(I32)
         tab_i32 = tab_words[0].rearrange("p t i -> p (t i)").bitcast(I32)
 
-        nc.sync.dma_start(idx[:], offs)
         nc.sync.dma_start(tabw[:, 0:TAB_FIRST], tab_i32[:, 0:TAB_FIRST])
+        nc.sync.dma_start(idx[:], offs)
         load_scales(tabs, tab_scales)
         nc.sync.dma_start(tabw[:, TAB_FIRST:T], tab_i32[:, TAB_FIRST:T])
         w2a = load(nc.sync, "w2a", [P, HEAD], I32, w2_i32[:, 0:HEAD])
@@ -201,7 +201,7 @@ def tile_list_semijoin_cache_kernel(tc, tab_words, tab_scales, offs, offs2, offs
             return wg[:] if i < PACK else wg_dealt[i - PACK][:]
 
         def page_of(i):
-            return pages[min(i, TILES - 2) % 2]
+            return pages[i % 2]
 
         def scatter(i):
             nc.vector.tensor_copy(page_of(i)[:].indirect(idx2[:]), joint[i])
@@ -215,8 +215,7 @@ def tile_list_semijoin_cache_kernel(tc, tab_words, tab_scales, offs, offs2, offs
             turns.append(0)
             return bank_tile(SUM_BANKS + len(turns) % 2, shape)
 
-        def squash_dealt(i, half, x, y, tz):
-            cols = half_cols(half)
+        def squash_dealt(i, cols, x, y, tz):
             t = i - PACK
             nc.gpsimd.tensor_tensor(y, x, priors[i][:, cols], ADD)
             nc.scalar.activation(tz, y, ACT.Tanh)
@@ -231,11 +230,11 @@ def tile_list_semijoin_cache_kernel(tc, tab_words, tab_scales, offs, offs2, offs
                                      start=n == 0 and k == 0, stop=n == 1 and k == PACK - 1)
             return bank
 
-        def fetch(i, half, x):
-            cols = half_cols(half)
-            nc.vector.tensor_copy(x, page_of(i)[:].indirect(half_list(idx3, half)))
+        def fetch(i, half, x, cols=None):
+            cols = cols or half_cols(half)
+            nc.vector.tensor_copy(x, page_of(i)[:].indirect(idx3[:, cols.start // 16:cols.stop // 16]))
             if i >= PACK:
-                waiting.append((i, half, x))
+                waiting.append((i, cols, x))
                 return
             bank = turned_sum(turn_bank([P, PACK, P]), priors[i][:, cols], x)
             nc.scalar.activation(squashed[:, PACK * half:PACK * (half + 1), :, 32 * i:32 * i + 32],
@@ -267,9 +266,7 @@ def tile_list_semijoin_cache_kernel(tc, tab_words, tab_scales, offs, offs2, offs
                 u, d3, d2 = ring(i)
                 d = copy_out(i, [u, d2, d3], in_order((0, 2, 1)))
                 woven = slot("woven3c", [P, K, PACK], BF16)
-                for k in range(2):
-                    nc.scalar.copy(woven[:, k * HEAD:(k + 1) * HEAD, :].rearrange("k (t p) j -> k t p j", t=2),
-                                   raw3c[:].rearrange("k j (p t) -> k t p j", t=PACK)[:, 2 * k:2 * k + 2, :, :])
+                nc.scalar.copy(woven[:].rearrange("k (t p) j -> k p t j", t=PACK), raw3c[:].rearrange("k j (p t) -> k p t j", t=PACK))
                 joint["late"] = lambda: late(woven, d)
                 return
             d = copy_out(i, ring(i), in_order((0, 1, 2)))
@@ -315,7 +312,7 @@ def tile_list_semijoin_cache_kernel(tc, tab_words, tab_scales, offs, offs2, offs
         load_weights(2)
         load_weights(3)
 
-        w4_woven = []
+        w4_woven = slot("w4_woven", [P, 2, N, PACK], BF16)
         z0_woven = []
         fetch(0, 0, slot("x0", [P, BANK], F32)[:])
         for i in range(1, TILES - 1):
@@ -337,33 +334,38 @@ def tile_list_semijoin_cache_kernel(tc, tab_words, tab_scales, offs, offs2, offs
                     nc.gpsimd.tensor_tensor(v[:], d[2], weights(TILES - 1), MULT)
                     nc.gpsimd.tensor_tensor(h[:], d[0], v[:], MULT)
                     joint[TILES - 1] = h[:]
-                fetch(i, 0, pair[:, 1, :])
                 if i == TILES - 3:
-                    fetch(i, 1, pair[:, 2, :])
+                    fetch(i, 0, pair[:, 1:3, :].rearrange("p a m -> p (a m)")[:, 0:PR - HEAD], slice(0, PR - HEAD))
+                else:
+                    fetch(i, 0, pair[:, 1, :])
             if i + 3 < TILES:
                 load_prior(i + 3)
             if i in (1, 2):
-                w4_woven.append(weave(raw4[i - 1][:], "w4_woven%d" % (i - 1), N))
+                nc.scalar.copy(w4_woven[:, i - 1, :, :].rearrange("p (c i) t -> p c t i", i=4), raw4[i - 1][:].rearrange("p t (c i) -> p c t i", i=4))
             if i == 2:
                 z1["woven"] = slot("z1_woven", [P, PR, PACK], BF16)
             if i == PACK - 1:
                 z0_woven.append(weave_z0(0))
 
         last = TILES - 1
-        sums = slot("planes0", [P, 4, BANK], F32)
-        bent = slot("planes1", [P, 2, BANK], F32)
-        for n, (i, half, x) in enumerate(waiting):
-            squash_dealt(i, half, x, sums[:, n, :], bent[:, n % 2, :])
+        sums = slot("planes0", [P, 3, PR - HEAD], F32)
+        bent = slot("planes1", [P, 2, PR - HEAD], F32)
+        for n, (i, cols, x) in enumerate(waiting):
+            width = cols.stop - cols.start
+            squash_dealt(i, cols, x, sums[:, n, 0:width], bent[:, n % 2, 0:width])
         waiting.clear()
         codes = slot("d3_0", [P, 2 * N + BANK], U32)
         z0 = [quantise(z0_woven[0][:], codes[:, 2 * N:2 * N + BANK], slot("z0_scales0", [P, BANK], U8)[:])]
-        w4q = [quantise(w4_woven[b][:], codes[:, b * N:(b + 1) * N], slot("w4_scales%d" % b, [P, N], U8)[:]) for b in range(2)]
-        x = slot("z0_woven0", [P, PR], F32)
+        w4_scales = slot("w4_scales", [P, 2 * N], U8)
+        quantise(w4_woven[:].rearrange("p b c t -> p (b c) t"), codes[:, 0:2 * N], w4_scales[:])
+        w4q = [(codes[:, b * N:(b + 1) * N], w4_scales[:, b * N:(b + 1) * N]) for b in range(2)]
+        x = slot("z0_woven0", [P, PR + HEAD], F32)
         bent = slot("planes1", [P, 2, BANK], F32)
+        fetch(last - 2, 1, x[:, PR:PR + HEAD], slice(PR - HEAD, PR))
         for half in range(2):
             fetch(last - 1, half, x[:, half_cols(half)])
-        for i, half, x in waiting:
-            squash_dealt(i, half, x, x, bent[:, half, :])
+        for n, (i, cols, x) in enumerate(waiting):
+            squash_dealt(i, cols, x, x, bent[:, n % 2, 0:cols.stop - cols.start])
         scatter(last)
         z0.append(quantise(z0_woven[1][:], slot("z0_woven0", [P, BANK], U32)[:], slot("z0_scales1", [P, BANK], U8)[:]))
 

@@ -79,18 +79,16 @@ def tile_list_semijoin_cache_kernel(tc, tab_words, tab_scales, offs, offs2, offs
         nc.sync.dma_start(idx[:], offs)
         load_scales(tabs, tab_scales)
         nc.sync.dma_start(tabw[:, TAB_FIRST:T], tab_i32[:, TAB_FIRST:T])
-        w2a = load(nc.sync, "w2a", [P, HEAD], I32, w2_i32[:, 0:HEAD])
+        w2a = load(nc.sync, "w2a", [P, P], I32, w2_i32[:, 0:P])
         load_scales(w2s, w2_scales)
-        wg = slot("wg", [P, S], F32)
-        nc.sync.dma_start(wg[:, half_cols(0)], wgs[:, half_cols(0)])
+        wg = load(nc.sync, "wg", [P, S], F32, wgs)
         raw3a = load(nc.sync, "raw3a", [P, PACK, HEAD], F32, w3_rows[:, :, 0:HEAD])
-        nc.sync.dma_start(wg[:, half_cols(1)], wgs[:, half_cols(1)])
-        w1a = load(nc.sync, "w1a", [P, HEAD // 2], I32, w1_i32[:, 0:HEAD // 2])
+        w1a = load(nc.sync, "w1a", [P, P // 2], I32, w1_i32[:, 0:P // 2])
         load_scales(w1s, w1_scales)
+        w2b = load(nc.sync, "w2b", [P, 3 * P], I32, w2_i32[:, P:K])
         raw3b = load(nc.sync, "raw3b", [P, PACK, HEAD], F32, w3_rows[:, :, HEAD:K])
         nc.sync.dma_start(idx2[:], offs2)
-        w1b = load(nc.sync, "w1b", [P, HEAD // 2], I32, w1_i32[:, HEAD // 2:HEAD])
-        w2b = load(nc.sync, "w2b", [P, HEAD], I32, w2_i32[:, HEAD:K])
+        w1b = load(nc.sync, "w1b", [P, 3 * P // 2], I32, w1_i32[:, P // 2:K // 2])
         nc.sync.dma_start(idx3[:], offs3)
         raw3c = load(nc.sync, "raw3c", [P, PACK, K], F32, w3_rows[:, :, K:H])
         w1c = load(nc.sync, "w1c", [P, K // 2], I32, w1_i32[:, K // 2:K])
@@ -169,7 +167,7 @@ def tile_list_semijoin_cache_kernel(tc, tab_words, tab_scales, offs, offs2, offs
                 if which == 0:
                     return dealt[1][:, t * P // 2:(t + 1) * P // 2].bitcast(E2M1), s1_dealt[:, t, :]
                 return dealt[2][:, t * P:(t + 1) * P].bitcast(E4M3), s2_dealt[:, t, :]
-            a, b, at = (w1a, w2a, i * P) if i * P < HEAD else (w1b, w2b, i * P - HEAD)
+            a, b, at = (w1a, w2a, 0) if i == 0 else (w1b, w2b, (i - 1) * P)
             cols = slice(i * P, (i + 1) * P)
             if which == 0:
                 return a[:, at // 2:(at + P) // 2].bitcast(E2M1), w1s[:, cols]

@@ -79,16 +79,18 @@ def tile_list_semijoin_cache_kernel(tc, tab_words, tab_scales, offs, offs2, offs
         nc.sync.dma_start(idx[:], offs)
         load_scales(tabs, tab_scales)
         nc.sync.dma_start(tabw[:, TAB_FIRST:T], tab_i32[:, TAB_FIRST:T])
-        w2a = load(nc.sync, "w2a", [P, P], I32, w2_i32[:, 0:P])
+        w2a = load(nc.sync, "w2a", [P, HEAD], I32, w2_i32[:, 0:HEAD])
         load_scales(w2s, w2_scales)
-        wg = load(nc.sync, "wg", [P, S], F32, wgs)
+        wg = slot("wg", [P, S], F32)
+        nc.sync.dma_start(wg[:, half_cols(0)], wgs[:, half_cols(0)])
         raw3a = load(nc.sync, "raw3a", [P, PACK, HEAD], F32, w3_rows[:, :, 0:HEAD])
+        nc.sync.dma_start(wg[:, half_cols(1)], wgs[:, half_cols(1)])
         w1a = load(nc.sync, "w1a", [P, P // 2], I32, w1_i32[:, 0:P // 2])
         load_scales(w1s, w1_scales)
-        w2b = load(nc.sync, "w2b", [P, 3 * P], I32, w2_i32[:, P:K])
         raw3b = load(nc.sync, "raw3b", [P, PACK, HEAD], F32, w3_rows[:, :, HEAD:K])
         nc.sync.dma_start(idx2[:], offs2)
         w1b = load(nc.sync, "w1b", [P, 3 * P // 2], I32, w1_i32[:, P // 2:K // 2])
+        w2b = load(nc.sync, "w2b", [P, HEAD], I32, w2_i32[:, HEAD:K])
         nc.sync.dma_start(idx3[:], offs3)
         raw3c = load(nc.sync, "raw3c", [P, PACK, K], F32, w3_rows[:, :, K:H])
         w1c = load(nc.sync, "w1c", [P, K // 2], I32, w1_i32[:, K // 2:K])
@@ -167,11 +169,11 @@ def tile_list_semijoin_cache_kernel(tc, tab_words, tab_scales, offs, offs2, offs
                 if which == 0:
                     return dealt[1][:, t * P // 2:(t + 1) * P // 2].bitcast(E2M1), s1_dealt[:, t, :]
                 return dealt[2][:, t * P:(t + 1) * P].bitcast(E4M3), s2_dealt[:, t, :]
-            a, b, at = (w1a, w2a, 0) if i == 0 else (w1b, w2b, (i - 1) * P)
             cols = slice(i * P, (i + 1) * P)
             if which == 0:
-                return a[:, at // 2:(at + P) // 2].bitcast(E2M1), w1s[:, cols]
-            return b[:, at:at + P].bitcast(E4M3), w2s[:, cols]
+                words = w1a[:] if i == 0 else w1b[:, (i - 1) * P // 2:i * P // 2]
+                return words.bitcast(E2M1), w1s[:, cols]
+            return (w2a, w2b)[i // 2][:, i % 2 * P:(i % 2 + 1) * P].bitcast(E4M3), w2s[:, cols]
 
         def signature(i, which, half, n):
             lhs, lhs_scale = stationary(i, which)
@@ -288,14 +290,23 @@ def tile_list_semijoin_cache_kernel(tc, tab_words, tab_scales, offs, offs2, offs
             join_halves((2, 1, 0), d, h)
             joint[3] = h[:]
 
-        quantise_w3(weave(raw3a[:], "woven3a", HEAD)[:], 0, 2, slot("w3_codes0", [P, HEAD], U32)[:])
-        quantise_w3(weave(raw3b[:], "woven3b", HEAD)[:], 2, 2, slot("w3_codes2", [P, HEAD], U32)[:])
+        woven3 = [weave(raw[:], tag, HEAD) for raw, tag in ((raw3a, "woven3a"), (raw3b, "woven3b"))]
+        part = slot("h0", [P, S], F32)
+        for half in range(2):
+            nc.vector.tensor_tensor(part[:, half_cols(half)], signature(0, 1, half, half)[:], wg[:, half_cols(half)], MULT)
+        d1 = [signature(0, 0, half, 2 + half) for half in range(2)]
+        nc.vector.tensor_tensor(part[:, half_cols(0)], d1[0][:], part[:, half_cols(0)], MULT)
+        quantise_w3(woven3[0][:], 0, 2, slot("w1a", [P, HEAD], U32)[:])
+        nc.vector.tensor_tensor(part[:, half_cols(1)], d1[1][:], part[:, half_cols(1)], MULT)
+        quantise_w3(woven3[1][:], 2, 2, slot("w3_codes2", [P, HEAD], U32)[:])
         early = slot("woven3b", [P, 2, S], F32)
-        join_vector(0, early[:, 0, :])
+        for half in range(2):
+            nc.vector.tensor_tensor(early[:, 0, half_cols(half)], signature(0, 2, half, half)[:], part[:, half_cols(half)], MULT)
+        joint[0] = early[:, 0, :]
         scatter(0)
 
         three = slot("raw3b", [P, 3, S], F32)
-        d = copy_out(1, [three[:, which, :] for which in range(3)], [((1, 0), 6), ((1, 1), 7), ((2, 0), 6), ((2, 1), 7), ((0, 0), 4), ((0, 1), 5)])
+        d = copy_out(1, [three[:, which, :] for which in range(3)], [((1, 0), 2), ((1, 1), 3), ((2, 0), 6), ((2, 1), 7), ((0, 0), 4), ((0, 1), 5)])
         join_halves((1, 2, 0), d, early[:, 1, :])
         joint[1] = early[:, 1, :]
         join_gpsimd(2)

@@ -58,12 +58,12 @@ def tile_list_semijoin_cache_kernel(tc, tab_words, tab_scales, offs, offs2, offs
         w1s = slot("w1s", [P, H], U8)
         w2s = slot("w2s", [P, H], U8)
         nc.vector.memset(tabs[:].bitcast(I32), 0)
-        nc.gpsimd.memset(w2s[:].bitcast(I32), 0)
-        nc.vector.memset(w1s[:].bitcast(I32), 0)
+        nc.gpsimd.memset(w1s[:].bitcast(I32), 0)
+        nc.vector.memset(w2s[:].bitcast(I32), 0)
 
-        def load_scales(plane, rows):
+        def load_scales(queue, plane, rows):
             for q in range(4):
-                nc.sync.dma_start(plane[32 * q:32 * q + 4, :].bitcast(I32), rows[0, 4 * q:4 * q + 4, :].bitcast(I32))
+                queue.dma_start(plane[32 * q:32 * q + 4, :].bitcast(I32), rows[0, 4 * q:4 * q + 4, :].bitcast(I32))
 
         def load(queue, tag, shape, dtype, src):
             dst = slot(tag, shape, dtype)
@@ -77,16 +77,16 @@ def tile_list_semijoin_cache_kernel(tc, tab_words, tab_scales, offs, offs2, offs
 
         nc.sync.dma_start(tabw[:, 0:TAB_FIRST], tab_i32[:, 0:TAB_FIRST])
         nc.sync.dma_start(idx[:], offs)
-        load_scales(tabs, tab_scales)
+        load_scales(nc.sync, tabs, tab_scales)
         nc.sync.dma_start(tabw[:, TAB_FIRST:T], tab_i32[:, TAB_FIRST:T])
         w2a = load(nc.sync, "w2a", [P, HEAD], I32, w2_i32[:, 0:HEAD])
-        load_scales(w2s, w2_scales)
+        load_scales(nc.sync, w2s, w2_scales)
         wg = slot("wg", [P, S], F32)
         nc.sync.dma_start(wg[:, half_cols(0)], wgs[:, half_cols(0)])
         raw3a = load(nc.sync, "raw3a", [P, PACK, HEAD], F32, w3_rows[:, :, 0:HEAD])
         nc.sync.dma_start(wg[:, half_cols(1)], wgs[:, half_cols(1)])
         w1a = load(nc.sync, "w1a", [P, P // 2], I32, w1_i32[:, 0:P // 2])
-        load_scales(w1s, w1_scales)
+        load_scales(nc.gpsimd, w1s, w1_scales)
         raw3b = load(nc.sync, "raw3b", [P, PACK, HEAD], F32, w3_rows[:, :, HEAD:K])
         nc.sync.dma_start(idx2[:], offs2)
         w1b = load(nc.sync, "w1b", [P, 3 * P // 2], I32, w1_i32[:, P // 2:K // 2])

@@ -26,7 +26,7 @@ HEAD = 2 * P
 SUM_BANKS = 6
 ON_VECTOR = ((4, 1),)
 SCALAR_GAINS = (1,)
-TAB_FIRST = 3 * T // 8
+TAB_FIRST = T // 4
 CHUNKS = (128, 256, 256, 256, 128)
 
 

@@ -62,8 +62,8 @@ def tile_list_semijoin_cache_kernel(tc, tab_words, tab_scales, offs, offs2, offs
         nc.vector.memset(w2s[:].bitcast(I32), 0)
 
         def load_scales(queue, plane, rows):
-            for q in range(4):
-                queue.dma_start(plane[32 * q:32 * q + 4, :].bitcast(I32), rows[0, 4 * q:4 * q + 4, :].bitcast(I32))
+            for r in range(4):
+                queue.dma_start(plane[r:P:32, :].bitcast(I32), rows[0, r:16:4, :].bitcast(I32))
 
         def load(queue, tag, shape, dtype, src):
             dst = slot(tag, shape, dtype)

@@ -22,12 +22,17 @@ P = 128
 PACK = 4
 BANK = 512
 TILES = H // P
+LAST = TILES - 1
 HEAD = 2 * P
-SUM_BANKS = 6
+TABLE_FIRST = T // 4
+W2_ROWS = 4
+TURN_BANKS = (6, 7)
+PRIOR_BUFFERS = 5
+EARLY_FETCH = PR - HEAD
+CHUNKS = (128, 256, 256, 256, 128)
 ON_VECTOR = ((4, 1),)
 SCALAR_GAINS = (1,)
-TAB_FIRST = T // 4
-CHUNKS = (128, 256, 256, 256, 128)
+D1, D2, D3 = 0, 1, 2
 
 
 def tile_list_semijoin_cache_kernel(tc, tab_words, tab_scales, offs, offs2, offs3, w1_words, w1_scales,
@@ -46,95 +51,93 @@ def tile_list_semijoin_cache_kernel(tc, tab_words, tab_scales, offs, offs2, offs
         def half_cols(half):
             return slice(half * BANK, (half + 1) * BANK)
 
-        def half_list(offsets, half):
-            return offsets[:, 32 * half:32 * half + 32]
+        def entries(offsets, cols):
+            return offsets[:, cols.start // 16:cols.stop // 16]
+
+        def load(tag, shape, dtype, src):
+            dst = slot(tag, shape, dtype)
+            nc.sync.dma_start(dst[:], src)
+            return dst
+
+        def load_scales(queue, plane, rows, first):
+            for r in range(4):
+                queue.dma_start(plane[first + r:P:32, :].bitcast(I32), rows[0, r:16:4, :].bitcast(I32))
 
         idx = keep.tile([P, S // 16], U16, name="idx")
         idx2 = keep.tile([P, S // 16], U16, name="idx2")
         idx3 = keep.tile([P, PR // 16], U16, name="idx3")
-
-        tabw = slot("tab", [P, T], I32)
-        tabs = slot("tabs", [P, T], U8)
-        w1s = slot("w1s", [P, H], U8)
-        w2s = slot("w2s", [P, H], U8)
-        nc.vector.memset(tabs[:].bitcast(I32), 0)
-        nc.gpsimd.memset(w1s[:].bitcast(I32), 0)
-        nc.vector.memset(w2s[:].bitcast(I32), 0)
-
-        def load_scales(queue, plane, rows):
-            for r in range(4):
-                queue.dma_start(plane[r:P:32, :].bitcast(I32), rows[0, r:16:4, :].bitcast(I32))
-
-        def load(queue, tag, shape, dtype, src):
-            dst = slot(tag, shape, dtype)
-            queue.dma_start(dst[:], src)
-            return dst
+        table = slot("table", [P, T], I32)
+        table_scales = slot("page1", [P, T], U8)
+        w_scales = slot("w_scales", [P, H], U8)
+        nc.vector.memset(table_scales[:].bitcast(I32), 0)
+        nc.gpsimd.memset(w_scales[:].bitcast(I32), 0)
 
         w3_rows = w3.rearrange("(p j) c -> p j c", j=PACK)
         w1_i32 = w1_words[0].bitcast(I32)
         w2_i32 = w2_words[0].rearrange("p c i -> p (c i)").bitcast(I32)
-        tab_i32 = tab_words[0].rearrange("p t i -> p (t i)").bitcast(I32)
+        table_i32 = tab_words[0].rearrange("p t i -> p (t i)").bitcast(I32)
 
-        nc.sync.dma_start(tabw[:, 0:TAB_FIRST], tab_i32[:, 0:TAB_FIRST])
+        nc.sync.dma_start(table[:, 0:TABLE_FIRST], table_i32[:, 0:TABLE_FIRST])
         nc.sync.dma_start(idx[:], offs)
-        load_scales(nc.sync, tabs, tab_scales)
-        nc.sync.dma_start(tabw[:, TAB_FIRST:T], tab_i32[:, TAB_FIRST:T])
-        w2a = load(nc.sync, "w2a", [P, HEAD], I32, w2_i32[:, 0:HEAD])
-        load_scales(nc.sync, w2s, w2_scales)
+        load_scales(nc.sync, table_scales[:], tab_scales, 0)
+        nc.sync.dma_start(table[:, TABLE_FIRST:T], table_i32[:, TABLE_FIRST:T])
+        load_scales(nc.gpsimd, w_scales[:], w1_scales, 0)
+        w2a = load("w2a", [P, HEAD], I32, w2_i32[:, 0:HEAD])
+        w1a = load("w1a", [P, HEAD // 2], I32, w1_i32[:, 0:HEAD // 2])
+        load_scales(nc.sync, w_scales[:], w2_scales, W2_ROWS)
         wg = slot("wg", [P, S], F32)
         nc.sync.dma_start(wg[:, half_cols(0)], wgs[:, half_cols(0)])
-        raw3a = load(nc.sync, "raw3a", [P, PACK, HEAD], F32, w3_rows[:, :, 0:HEAD])
-        nc.sync.dma_start(wg[:, half_cols(1)], wgs[:, half_cols(1)])
-        w1a = load(nc.sync, "w1a", [P, P // 2], I32, w1_i32[:, 0:P // 2])
-        load_scales(nc.gpsimd, w1s, w1_scales)
-        raw3b = load(nc.sync, "raw3b", [P, PACK, HEAD], F32, w3_rows[:, :, HEAD:K])
+        raw3a = load("raw3a", [P, PACK, HEAD], F32, w3_rows[:, :, 0:HEAD])
         nc.sync.dma_start(idx2[:], offs2)
-        w1b = load(nc.sync, "w1b", [P, 3 * P // 2], I32, w1_i32[:, P // 2:K // 2])
-        w2b = load(nc.sync, "w2b", [P, HEAD], I32, w2_i32[:, HEAD:K])
+        nc.sync.dma_start(wg[:, half_cols(1)], wgs[:, half_cols(1)])
         nc.sync.dma_start(idx3[:], offs3)
-        raw3c = load(nc.sync, "raw3c", [P, PACK, K], F32, w3_rows[:, :, K:H])
-        w1c = load(nc.sync, "w1c", [P, K // 2], I32, w1_i32[:, K // 2:K])
-        w2c = load(nc.sync, "w2c", [P, K], I32, w2_i32[:, K:H])
+        raw3c = load("raw3c", [P, PACK, K], F32, w3_rows[:, :, K:H])
+        raw3b = load("raw3b", [P, PACK, HEAD], F32, w3_rows[:, :, HEAD:K])
+        w1b = load("w1b", [P, HEAD // 2], I32, w1_i32[:, HEAD // 2:K // 2])
+        w2b = load("w2b", [P, HEAD], I32, w2_i32[:, HEAD:K])
 
         priors = {}
 
         def load_prior(i):
             rows = prior[i * P:(i + 1) * P, :] if i < PACK else prior[K:H, :].rearrange("(p t) m -> t p m", t=PACK)[i - PACK]
-            priors[i] = load(nc.sync, "prior%d" % (i % 5), [P, PR], F32, rows)
+            priors[i] = load("prior%d" % (i % PRIOR_BUFFERS), [P, PR], F32, rows)
 
         load_prior(0)
+        w1c = load("w1c", [P, K // 2], I32, w1_i32[:, K // 2:K])
+        w2c = load("w2c", [P, K], I32, w2_i32[:, K:H])
         load_prior(1)
-        wg_dealt = {}
-
-        def load_weights(t):
-            wg_dealt[t] = slot("wg_dealt%d" % t, [P, S], F32)
+        raw4 = [load(tag, [P, PACK, N], F32, w4[b * K:(b + 1) * K, :].rearrange("(p j) n -> p j n", j=PACK))
+                for b, tag in enumerate(("z0_woven0", "z1_woven"))]
+        wg_dealt = []
+        gains = keep.tile([P, 2, PACK], F32, name="gains")
+        for t in range(PACK):
+            wg_dealt.append(slot("wg_dealt%d" % t, [P, S], F32))
             for a in (0, 2, 1, 3):
                 nc.sync.dma_start(wg_dealt[t][32 * a:32 * a + 32, :], wgs.rearrange("(c t) j -> t c j", t=PACK)[t])
+            if t < 2:
+                load_prior(2 + t)
+            if t == 1:
+                nc.sync.dma_start(gains[:], gain.rearrange("(b p t) -> p b t", p=P, t=PACK))
 
         ident = keep.tile([P, P], F32, name="ident")
         make_identity(nc, ident[:])
-        pages = []
-        for k in range(2):
-            page = keep.tile([P, T2], F32, name="page%d" % k)
-            (nc.vector, nc.gpsimd)[k].memset(page[:], 0.0)
-            pages.append(page)
+        pages = [slot("page0", [P, T2], F32)]
+        for cols in (slice(0, T2 // 2 - 1), slice(T2 // 2 - 1, T2)):
+            nc.vector.memset(pages[0][:, cols], 0.0)
 
-        vs = slot("vs", [P, S], U8)
-        nc.vector.tensor_copy(vs[:], tabs[:].indirect(idx[:]))
-        vw = []
+        v_scales = slot("v_scales", [P, S], U8)
+        nc.vector.tensor_copy(v_scales[:], table_scales[:].indirect(idx[:]))
+        v_words = []
         for half in range(2):
-            words = slot("vw%d" % half, [P, BANK], U32)
-            nc.vector.tensor_copy(words[:], tabw[:].bitcast(U32).indirect(half_list(idx, half)))
-            vw.append(words)
+            v_words.append(slot("v_words%d" % half, [P, BANK], U32))
+            nc.vector.tensor_copy(v_words[half][:], table[:].bitcast(U32).indirect(entries(idx, half_cols(half))))
+        pages.append(slot("page1", [P, T2], F32))
+        nc.gpsimd.memset(pages[1][:], 0.0)
+        scales_dealt = slot("scales_dealt", [P, PACK, P], U8)
+        nc.gpsimd.tensor_copy(scales_dealt[:], w_scales[:, K:H].rearrange("k (p t) -> k t p", t=PACK))
 
-        s1_dealt = slot("s1_dealt", [P, PACK, P], U8)
-        s2_dealt = slot("s2_dealt", [P, PACK, P], U8)
-        nc.gpsimd.tensor_copy(s1_dealt[:], w1s[:, K:H].rearrange("k (p t) -> k t p", t=PACK))
-        nc.gpsimd.tensor_copy(s2_dealt[:], w2s[:, K:H].rearrange("k (p t) -> k t p", t=PACK))
-
-        def weave(raw, tag, width):
-            woven = slot(tag, [P, width, PACK], BF16)
-            nc.scalar.copy(woven[:].rearrange("p (c i) t -> p c t i", i=4), raw.rearrange("p t (c i) -> p c t i", i=4))
+        def weave(woven, raw):
+            nc.scalar.copy(woven.rearrange("p (c i) t -> p c t i", i=4), raw.rearrange("p t (c i) -> p c t i", i=4))
             return woven
 
         def quantise(woven, codes, scales):
@@ -151,93 +154,129 @@ def tile_list_semijoin_cache_kernel(tc, tab_words, tab_scales, offs, offs2, offs
 
         dealt = {}
 
-        def deal_words():
-            both = slot("raw3b", [P, 3 * K // 2], I32)
-            w1_dealt = both[:, K:3 * K // 2].bitcast(U8).rearrange("k (t p b) -> k t p b", t=PACK, b=2)
-            w2_dealt = both[:, 0:K].rearrange("k (t p) -> k t p", t=PACK)
-            nc.gpsimd.tensor_copy(w1_dealt, w1c[:].bitcast(U8).rearrange("k (p t b) -> k t p b", t=PACK, b=2))
-            nc.gpsimd.tensor_copy(w2_dealt, w2c[:].rearrange("k (p t) -> k t p", t=PACK))
-            dealt[1] = both[:, K:3 * K // 2]
-            dealt[2] = both[:, 0:K]
-
         def stationary(i, which):
-            if which == 2:
+            if which == D3:
                 codes, scales = w3q[i]
                 return codes.bitcast(E4M3), scales
             if i >= PACK:
                 t = i - PACK
-                if which == 0:
-                    return dealt[1][:, t * P // 2:(t + 1) * P // 2].bitcast(E2M1), s1_dealt[:, t, :]
-                return dealt[2][:, t * P:(t + 1) * P].bitcast(E4M3), s2_dealt[:, t, :]
+                if which == D1:
+                    return dealt[D1][:, t, :].bitcast(E2M1), scales_dealt[:, t, :]
+                return dealt[D2][:, t, :].bitcast(E4M3), scales_dealt[W2_ROWS:P, t, :]
             cols = slice(i * P, (i + 1) * P)
-            if which == 0:
-                words = w1a[:] if i == 0 else w1b[:, (i - 1) * P // 2:i * P // 2]
-                return words.bitcast(E2M1), w1s[:, cols]
-            return (w2a, w2b)[i // 2][:, i % 2 * P:(i % 2 + 1) * P].bitcast(E4M3), w2s[:, cols]
+            if which == D1:
+                return (w1a, w1b)[i // 2][:, i % 2 * P // 2:(i % 2 + 1) * P // 2].bitcast(E2M1), w_scales[:, cols]
+            return (w2a, w2b)[i // 2][:, i % 2 * P:(i % 2 + 1) * P].bitcast(E4M3), w_scales[W2_ROWS:P, cols]
 
         def signature(i, which, half, n):
             lhs, lhs_scale = stationary(i, which)
             bank = bank_tile(n, [P, BANK])
-            nc.tensor.matmul_mx(out=bank[:], lhsT=lhs, lhsT_scale=lhs_scale, rhs=vw[half][:].bitcast(E4M3),
-                                rhs_scale=vs[:, half_cols(half)], start=True, stop=True)
+            nc.tensor.matmul_mx(out=bank[:], lhsT=lhs, lhsT_scale=lhs_scale, rhs=v_words[half][:].bitcast(E4M3),
+                                rhs_scale=v_scales[:, half_cols(half)], start=True, stop=True)
             return bank
+
+        def copy_out(i, which, dst, first):
+            for half in range(2):
+                nc.scalar.copy(dst[:, half_cols(half)], signature(i, which, half, first + half)[:])
+            return dst
 
         joint = {}
 
-        def join_vector(i, h):
-            part = slot("h%d" % (i % 3), [P, S], F32)
-            for first, which, src, dst in ((0, 1, wg, part), (2, 0, part, part), (2, 2, part, h)):
-                for half in range(2):
-                    cols = half_cols(half)
-                    nc.vector.tensor_tensor(dst[:, cols], signature(i, which, half, first + half)[:], src[:, cols], MULT)
-            joint[i] = h
-
-        def copy_out(i, d, banks):
-            for (which, half), n in banks:
-                nc.scalar.copy(d[which][:, half_cols(half)], signature(i, which, half, n)[:])
-            return d
-
-        def weights(i):
-            return wg[:] if i < PACK else wg_dealt[i - PACK][:]
-
-        def page_of(i):
-            return pages[i % 2]
-
         def scatter(i):
-            nc.vector.tensor_copy(page_of(i)[:].indirect(idx2[:]), joint[i])
+            nc.vector.tensor_copy(pages[i % 2][:].indirect(idx2[:]), joint[i])
 
-        squashed = slot("tab", [P, PR // P, PACK, P], F32)
-        g_sb = keep.tile([P, 2, PACK], F32, name="g_sb")
-        z1 = {}
+        woven3a = weave(slot("woven3a", [P, HEAD, PACK], BF16)[:], raw3a[:])
+        h0 = slot("h0", [P, S], F32)
+
+        def join_vector(which, half, bank, src):
+            cols = half_cols(half)
+            nc.vector.tensor_tensor(h0[:, cols], signature(0, which, half, bank)[:], src[:, cols], MULT)
+
+        join_vector(D2, 0, 0, wg)
+        join_vector(D1, 0, 2, h0)
+        join_vector(D2, 1, 1, wg)
+        quantise_w3(woven3a, 0, 2, slot("w3_codes0", [P, HEAD], U32)[:])
+        join_vector(D1, 1, 3, h0)
+        join_vector(D3, 0, 4, h0)
+        join_vector(D3, 1, 5, h0)
+        joint[0] = h0[:]
+        scatter(0)
+        x0 = slot("x0", [P, BANK], F32)
+        nc.vector.tensor_copy(x0[:], pages[0][:].indirect(entries(idx3, half_cols(0))))
+
+        h1 = slot("h1", [P, S], F32)
+
+        def join_half(which, half, d, bank, src):
+            nc.scalar.copy(d, signature(1, which, half, bank)[:])
+            nc.gpsimd.tensor_tensor(h1[:, half_cols(half)], d, src[:, half_cols(half)], MULT)
+
+        early = slot("raw3a", [P, 2, BANK], F32)
+        join_half(D2, 0, early[:, 0, :], 0, wg)
+        join_half(D2, 1, slot("one_d2", [P, BANK], F32)[:], 1, wg)
+        join_half(D1, 0, early[:, 1, :], 2, h1)
+        join_half(D1, 1, slot("one_d1", [P, BANK], F32)[:], 3, h1)
+        join_half(D3, 0, slot("one_d3", [P, BANK], F32)[:], 6, h1)
+        woven3c = slot("woven3c", [P, K, PACK], BF16)
+        nc.scalar.copy(woven3c[:].rearrange("k (t p) j -> k p t j", t=PACK), raw3c[:].rearrange("k j (p t) -> k p t j", t=PACK))
+        woven3b = weave(slot("woven3b", [P, HEAD, PACK], BF16)[:], raw3b[:])
+        join_half(D3, 1, slot("raw3c", [P, BANK], F32)[:], 7, h1)
+        joint[1] = h1[:]
+        codes3 = slot("raw3c", [P, HEAD + K], U32)
+        quantise_w3(woven3b, 2, 2, codes3[:, 0:HEAD])
+        quantise_w3(woven3c[:], PACK, PACK, codes3[:, HEAD:HEAD + K])
+
+        def deal_words():
+            dealt[D1] = slot("w1_dealt", [P, PACK, P], U16)
+            dealt[D2] = slot("w2_dealt", [P, PACK, P], U32)
+            nc.scalar.copy(dealt[D1][:].rearrange("k t p -> k p t"), w1c[:].bitcast(U16).rearrange("k (p t) -> k p t", t=PACK))
+            nc.scalar.copy(dealt[D2][:].rearrange("k t p -> k p t"), w2c[:].bitcast(U32).rearrange("k (p t) -> k p t", t=PACK))
+
+        held = {}
+
+        def join(i):
+            if i == 2:
+                behind = slot("raw3b", [P, 2, S], F32)
+                d1 = copy_out(i, D1, behind[:, 0, :], 0)
+                d2 = copy_out(i, D2, behind[:, 1, :], 2)
+            else:
+                d1 = copy_out(i, D1, slot("u%d" % (i % 2), [P, S], F32), 0)
+                d2 = copy_out(i, D2, slot("d2_%d" % (i % 2), [P, S], F32), 2)
+            d3 = copy_out(i, D3, slot("d3_%d" % (i % 3), [P, S], F32), 4)
+            u = slot("woven3c", [P, S], F32) if i == 2 else d1
+            nc.gpsimd.tensor_tensor(u[:], d1[:], d2[:], MULT)
+            held[i] = u, d3
+            if i < LAST:
+                finish(i, slot("h%d" % (i % 3), [P, S], F32), None)
+
+        def finish(i, h, v):
+            u, d3 = held[i]
+            v = v or h
+            nc.gpsimd.tensor_tensor(v[:], d3[:], wg[:] if i < PACK else wg_dealt[i - PACK][:], MULT)
+            nc.gpsimd.tensor_tensor(h[:], u[:], v[:], MULT)
+            joint[i] = h[:]
+
+        squashed = slot("table", [P, PR // P, PACK, P], F32)
         turns = []
 
         def turn_bank(shape):
             turns.append(0)
-            return bank_tile(SUM_BANKS + len(turns) % 2, shape)
-
-        def squash_dealt(i, cols, x, y, tz):
-            t = i - PACK
-            nc.gpsimd.tensor_tensor(y, x, priors[i][:, cols], ADD)
-            nc.scalar.activation(tz, y, ACT.Tanh)
-            nc.scalar.activation(z1["woven"][:, cols, t], tz, ACT.Copy, scale=g_sb[:, 1, t:t + 1])
+            return bank_tile(TURN_BANKS[len(turns) % 2], shape)
 
         waiting = []
 
-        def turned_sum(bank, first, second):
-            for n, src in enumerate((first, second)):
+        def fetch(i, cols, x):
+            nc.vector.tensor_copy(x, pages[i % 2][:].indirect(entries(idx3, cols)))
+            if i >= PACK:
+                waiting.append((i, cols, x))
+            else:
+                squash_turned(i, cols, x, turn_bank([P, PACK, P]))
+
+        def squash_turned(i, cols, x, bank):
+            for n, src in enumerate((priors[i][:, cols], x)):
                 for k in range(PACK):
                     nc.tensor.matmul(bank[:, k, :], src[:, k * P:(k + 1) * P], ident[:], is_transpose=True,
                                      start=n == 0 and k == 0, stop=n == 1 and k == PACK - 1)
-            return bank
-
-        def fetch(i, half, x, cols=None):
-            cols = cols or half_cols(half)
-            nc.vector.tensor_copy(x, page_of(i)[:].indirect(idx3[:, cols.start // 16:cols.stop // 16]))
-            if i >= PACK:
-                waiting.append((i, cols, x))
-                return
-            bank = turned_sum(turn_bank([P, PACK, P]), priors[i][:, cols], x)
-            nc.scalar.activation(squashed[:, PACK * half:PACK * (half + 1), :, 32 * i:32 * i + 32],
+            nc.scalar.activation(squashed[:, cols.start // P:cols.stop // P, :, 32 * i:32 * i + 32],
                                  bank[:].rearrange("m k (p t) -> m k t p", t=PACK), ACT.Tanh)
 
         def weave_z0(half):
@@ -246,137 +285,63 @@ def tile_list_semijoin_cache_kernel(tc, tab_words, tab_scales, offs, offs2, offs
                 bank = turn_bank([P, BANK])
                 for k in range(PACK):
                     nc.tensor.transpose(bank[:, k * P:(k + 1) * P], squashed[:, PACK * half + k, t, :], ident[:])
-                nc.scalar.activation(planes[:, t, :], bank[:], ACT.Copy, scale=g_sb[:, 0, t:t + 1])
-            return weave(planes[:], "z0_woven%d" % half, BANK)
+                nc.scalar.activation(planes[:, t, :], bank[:], ACT.Copy, scale=gains[:, 0, t:t + 1])
+            return weave(slot("z0_woven%d" % half, [P, BANK, PACK], BF16)[:], planes[:])
 
-        def in_order(order, first=0):
-            return [((which, half), (first + 2 * n + half) % 8) for n, which in enumerate(order) for half in range(2)]
-
-        def ring(i):
-            return [slot(tag, [P, S], F32)[:] for tag in ("u%d" % (i % 2), "d2_%d" % (i % 2), "d3_%d" % (i % 3))]
-
-        def join_halves(order, d, h):
-            for which, src in zip(order, (wg, h, h)):
-                for half in range(2):
-                    cols = half_cols(half)
-                    nc.gpsimd.tensor_tensor(h[:, cols], d[which][:, cols], src[:, cols], MULT)
-
-        def join_gpsimd(i):
-            if i == 3:
-                u, d3, d2 = ring(i)
-                d = copy_out(i, [u, d2, d3], in_order((0, 2, 1)))
-                woven = slot("woven3c", [P, K, PACK], BF16)
-                nc.scalar.copy(woven[:].rearrange("k (t p) j -> k p t j", t=PACK), raw3c[:].rearrange("k j (p t) -> k p t j", t=PACK))
-                joint["late"] = lambda: late(woven, d)
-                return
-            d = copy_out(i, ring(i), in_order((0, 1, 2)))
-            nc.gpsimd.tensor_tensor(d[0], d[0], d[1], MULT)
-            if i == TILES - 1:
-                joint["last"] = d
-                return
-            v = slot("v2" if i == 2 else "h%d" % (i % 3), [P, S], F32)
-            nc.gpsimd.tensor_tensor(v[:], d[2], weights(i), MULT)
-            h = v
-            if i == 2:
-                deal_words()
-                join_gpsimd(3)
-                h = slot("raw3c", [P, S], F32)
-            nc.gpsimd.tensor_tensor(h[:], d[0], v[:], MULT)
-            joint[i] = h[:]
-
-        def late(woven, d):
-            quantise_w3(woven[:], PACK, PACK, slot("v2", [P, K], U32)[:])
-            h = slot("woven3c", [P, S], F32)
-            join_halves((2, 1, 0), d, h)
-            joint[3] = h[:]
-
-        woven3 = [weave(raw[:], tag, HEAD) for raw, tag in ((raw3a, "woven3a"), (raw3b, "woven3b"))]
-        part = slot("h0", [P, S], F32)
-        for half in range(2):
-            nc.vector.tensor_tensor(part[:, half_cols(half)], signature(0, 1, half, half)[:], wg[:, half_cols(half)], MULT)
-        d1 = [signature(0, 0, half, 2 + half) for half in range(2)]
-        nc.vector.tensor_tensor(part[:, half_cols(0)], d1[0][:], part[:, half_cols(0)], MULT)
-        quantise_w3(woven3[0][:], 0, 2, slot("w1a", [P, HEAD], U32)[:])
-        nc.vector.tensor_tensor(part[:, half_cols(1)], d1[1][:], part[:, half_cols(1)], MULT)
-        quantise_w3(woven3[1][:], 2, 2, slot("w3_codes2", [P, HEAD], U32)[:])
-        early = slot("woven3b", [P, 2, S], F32)
-        for half in range(2):
-            nc.vector.tensor_tensor(early[:, 0, half_cols(half)], signature(0, 2, half, half)[:], part[:, half_cols(half)], MULT)
-        joint[0] = early[:, 0, :]
-        scatter(0)
-
-        three = slot("raw3b", [P, 3, S], F32)
-        d = copy_out(1, [three[:, which, :] for which in range(3)], [((1, 0), 2), ((1, 1), 3), ((2, 0), 6), ((2, 1), 7), ((0, 0), 4), ((0, 1), 5)])
-        join_halves((1, 2, 0), d, early[:, 1, :])
-        joint[1] = early[:, 1, :]
-        join_gpsimd(2)
-
-        raw4 = [load(nc.sync, tag, [P, PACK, N], F32, w4[b * K:(b + 1) * K, :].rearrange("(p j) n -> p j n", j=PACK))
-                for b, tag in enumerate(("z0_woven0", "z1_woven"))]
-        load_weights(0)
-        load_prior(2)
-        load_weights(1)
-        load_prior(3)
-        nc.sync.dma_start(g_sb[:], gain.rearrange("(b p t) -> p b t", p=P, t=PACK))
-        load_weights(2)
-        load_weights(3)
-
+        join(2)
+        squash_turned(0, half_cols(0), x0[:], bank_tile(5, [P, PACK, P]))
+        deal_words()
+        join(3)
         w4_woven = slot("w4_woven", [P, 2, N, PACK], BF16)
         z0_woven = []
-        fetch(0, 0, slot("x0", [P, BANK], F32)[:])
-        for i in range(1, TILES - 1):
-            if i == 2:
-                joint["late"]()
+        z1_woven = None
+        for i in range(1, LAST):
             scatter(i)
-            if i == 2:
-                join_gpsimd(4)
-            if 2 <= i < TILES - 3:
-                join_gpsimd(i + 3)
-            if i < TILES - 2:
-                pair = slot("d3_%d" % ((i + 1) % 3), [P, 3 if i == TILES - 3 else 2, BANK], F32)
-                fetch(i - 1, 1, pair[:, 0, :])
+            if i + 3 <= LAST:
+                join(i + 3)
+            if i < LAST - 1:
+                ahead = EARLY_FETCH if i == LAST - 2 else BANK
+                x = slot("d3_%d" % ((i + 1) % 3), [P, BANK + ahead], F32)
+                fetch(i - 1, half_cols(1), x[:, 0:BANK])
                 if i == PACK:
                     z0_woven.append(weave_z0(1))
-                    d = joint["last"]
-                    v = slot("planes0", [P, S], F32)
-                    h = slot("h%d" % ((TILES - 1) % 3), [P, S], F32)
-                    nc.gpsimd.tensor_tensor(v[:], d[2], weights(TILES - 1), MULT)
-                    nc.gpsimd.tensor_tensor(h[:], d[0], v[:], MULT)
-                    joint[TILES - 1] = h[:]
-                if i == TILES - 3:
-                    fetch(i, 0, pair[:, 1:3, :].rearrange("p a m -> p (a m)")[:, 0:PR - HEAD], slice(0, PR - HEAD))
-                else:
-                    fetch(i, 0, pair[:, 1, :])
-            if i + 3 < TILES:
+                    finish(LAST, slot("h%d" % (LAST % 3), [P, S], F32), slot("planes0", [P, S], F32))
+                fetch(i, slice(0, ahead), x[:, BANK:BANK + ahead])
+            if i + 3 <= LAST:
                 load_prior(i + 3)
             if i in (1, 2):
-                nc.scalar.copy(w4_woven[:, i - 1, :, :].rearrange("p (c i) t -> p c t i", i=4), raw4[i - 1][:].rearrange("p t (c i) -> p c t i", i=4))
+                weave(w4_woven[:, i - 1, :, :], raw4[i - 1][:])
             if i == 2:
-                z1["woven"] = slot("z1_woven", [P, PR, PACK], BF16)
+                z1_woven = slot("z1_woven", [P, PR, PACK], BF16)
             if i == PACK - 1:
                 z0_woven.append(weave_z0(0))
 
-        last = TILES - 1
-        sums = slot("planes0", [P, 3, PR - HEAD], F32)
-        bent = slot("planes1", [P, 2, PR - HEAD], F32)
+        def squash_dealt(i, cols, x, y, bent):
+            t = i - PACK
+            nc.gpsimd.tensor_tensor(y, x, priors[i][:, cols], ADD)
+            nc.scalar.activation(bent, y, ACT.Tanh)
+            nc.scalar.activation(z1_woven[:, cols, t], bent, ACT.Copy, scale=gains[:, 1, t:t + 1])
+
+        sums = slot("planes0", [P, 3, EARLY_FETCH], F32)
+        bent = slot("planes1", [P, 2, EARLY_FETCH], F32)
         for n, (i, cols, x) in enumerate(waiting):
             width = cols.stop - cols.start
             squash_dealt(i, cols, x, sums[:, n, 0:width], bent[:, n % 2, 0:width])
         waiting.clear()
         codes = slot("d3_0", [P, 2 * N + BANK], U32)
-        z0 = [quantise(z0_woven[0][:], codes[:, 2 * N:2 * N + BANK], slot("z0_scales0", [P, BANK], U8)[:])]
+        z0 = [quantise(z0_woven[0], codes[:, 2 * N:2 * N + BANK], slot("z0_scales0", [P, BANK], U8)[:])]
         w4_scales = slot("w4_scales", [P, 2 * N], U8)
         quantise(w4_woven[:].rearrange("p b c t -> p (b c) t"), codes[:, 0:2 * N], w4_scales[:])
         w4q = [(codes[:, b * N:(b + 1) * N], w4_scales[:, b * N:(b + 1) * N]) for b in range(2)]
         x = slot("z0_woven0", [P, PR + HEAD], F32)
         bent = slot("planes1", [P, 2, BANK], F32)
-        fetch(last - 2, 1, x[:, PR:PR + HEAD], slice(PR - HEAD, PR))
+        fetch(LAST - 2, slice(EARLY_FETCH, PR), x[:, PR:PR + HEAD])
         for half in range(2):
-            fetch(last - 1, half, x[:, half_cols(half)])
+            fetch(LAST - 1, half_cols(half), x[:, half_cols(half)])
         for n, (i, cols, x) in enumerate(waiting):
             squash_dealt(i, cols, x, x, bent[:, n % 2, 0:cols.stop - cols.start])
-        scatter(last)
-        z0.append(quantise(z0_woven[1][:], slot("z0_woven0", [P, BANK], U32)[:], slot("z0_scales1", [P, BANK], U8)[:]))
+        scatter(LAST)
+        z0.append(quantise(z0_woven[1], slot("z0_woven0", [P, BANK], U32)[:], slot("z0_scales1", [P, BANK], U8)[:]))
 
         chunks = [slice(sum(CHUNKS[:c]), sum(CHUNKS[:c + 1])) for c in range(len(CHUNKS))]
 
@@ -408,27 +373,27 @@ def tile_list_semijoin_cache_kernel(tc, tab_words, tab_scales, offs, offs2, offs
             first_pass(banks, cols)
             opened.append(banks)
 
-        res = slot("tab", [P, PR // P, BANK], F32)
+        res = slot("table", [P, PR // P, BANK], F32)
         squash = {}
         x_tail = slot("planes1", [P, 2, max(CHUNKS)], F32)
 
         def tail_fetch(c):
             cols = chunks[c]
             x = x_tail[:, c % 2, 0:CHUNKS[c]]
-            nc.vector.tensor_tensor(x, page_of(last)[:].indirect(idx3[:, cols.start // 16:cols.stop // 16]),
-                                    priors[last][:, cols], ADD)
+            nc.vector.tensor_tensor(x, pages[LAST % 2][:].indirect(idx3[:, cols.start // 16:cols.stop // 16]),
+                                    priors[LAST][:, cols], ADD)
             squash[c] = slot("tz%d" % c, [P, CHUNKS[c]], F32)
             nc.scalar.activation(squash[c][:], x, ACT.Tanh)
 
         def tail_gain(c):
             if c in SCALAR_GAINS:
-                nc.scalar.activation(z1["woven"][:, chunks[c], PACK - 1], squash[c][:], ACT.Copy, scale=g_sb[:, 1, PACK - 1:PACK])
+                nc.scalar.activation(z1_woven[:, chunks[c], PACK - 1], squash[c][:], ACT.Copy, scale=gains[:, 1, PACK - 1:PACK])
             else:
-                nc.vector.tensor_scalar(z1["woven"][:, chunks[c], PACK - 1], squash[c][:], g_sb[:, 1, PACK - 1:PACK], None, MULT)
+                nc.vector.tensor_scalar(z1_woven[:, chunks[c], PACK - 1], squash[c][:], gains[:, 1, PACK - 1:PACK], None, MULT)
 
         def tail_close(c):
             cols = chunks[c]
-            z_codes, z_scales = quantise(z1["woven"][:, cols, :], slot("z1_codes%d" % c, [P, CHUNKS[c]], U32)[:],
+            z_codes, z_scales = quantise(z1_woven[:, cols, :], slot("z1_codes%d" % c, [P, CHUNKS[c]], U32)[:],
                                          slot("z1_scales%d" % c, [P, CHUNKS[c]], U8)[:])
             estimate_pass(1, opened[c], [(slice(0, CHUNKS[c]), z_codes, z_scales)])
             staged_all = res[:, cols.start // P:cols.stop // P, :].rearrange("p b (k m) -> p (b k) m", m=CHUNKS[c])

@@ -30,6 +30,7 @@ TURN_BANKS = (6, 7)
 PRIOR_BUFFERS = 5
 EARLY_FETCH = PR - HEAD
 CHUNKS = (128, 256, 256, 256, 128)
+BANKS = ((0,), (1, 2), (3, 4), (5, 6), (7, 0))
 ON_VECTOR = ((4, 1),)
 SCALAR_GAINS = (1,)
 D1, D2, D3 = 0, 1, 2
@@ -68,9 +69,10 @@ def tile_list_semijoin_cache_kernel(tc, tab_words, tab_scales, offs, offs2, offs
         idx3 = keep.tile([P, PR // 16], U16, name="idx3")
         table = slot("table", [P, T], I32)
         table_scales = slot("page1", [P, T], U8)
-        w_scales = slot("w_scales", [P, H], U8)
+        w_scales = slot("w_scales", [P, 2, H], U8)
         nc.vector.memset(table_scales[:].bitcast(I32), 0)
-        nc.gpsimd.memset(w_scales[:].bitcast(I32), 0)
+        nc.gpsimd.memset(w_scales[:, D2, :].bitcast(I32), 0)
+        nc.vector.memset(w_scales[:, D1, :].bitcast(I32), 0)
 
         w3_rows = w3.rearrange("(p j) c -> p j c", j=PACK)
         w1_i32 = w1_words[0].bitcast(I32)
@@ -81,20 +83,21 @@ def tile_list_semijoin_cache_kernel(tc, tab_words, tab_scales, offs, offs2, offs
         nc.sync.dma_start(idx[:], offs)
         load_scales(nc.sync, table_scales[:], tab_scales, 0)
         nc.sync.dma_start(table[:, TABLE_FIRST:T], table_i32[:, TABLE_FIRST:T])
-        load_scales(nc.gpsimd, w_scales[:], w1_scales, 0)
-        w2a = load("w2a", [P, HEAD], I32, w2_i32[:, 0:HEAD])
+        load_scales(nc.gpsimd, w_scales[:, D2, :], w2_scales, W2_ROWS)
         w1a = load("w1a", [P, HEAD // 2], I32, w1_i32[:, 0:HEAD // 2])
-        load_scales(nc.sync, w_scales[:], w2_scales, W2_ROWS)
+        load_scales(nc.sync, w_scales[:, D1, :], w1_scales, 0)
         wg = slot("wg", [P, S], F32)
         nc.sync.dma_start(wg[:, half_cols(0)], wgs[:, half_cols(0)])
-        raw3a = load("raw3a", [P, PACK, HEAD], F32, w3_rows[:, :, 0:HEAD])
-        nc.sync.dma_start(idx2[:], offs2)
+        raw30 = load("raw30", [P, PACK, P], F32, w3_rows[:, :, 0:P])
         nc.sync.dma_start(wg[:, half_cols(1)], wgs[:, half_cols(1)])
+        w2a = load("w2a", [P, P], I32, w2_i32[:, 0:P])
+        raw31 = load("raw31", [P, PACK, P], F32, w3_rows[:, :, P:HEAD])
+        nc.sync.dma_start(idx2[:], offs2)
+        w2b = load("w2b", [P, 3 * P], I32, w2_i32[:, P:K])
         nc.sync.dma_start(idx3[:], offs3)
         raw3c = load("raw3c", [P, PACK, K], F32, w3_rows[:, :, K:H])
         raw3b = load("raw3b", [P, PACK, HEAD], F32, w3_rows[:, :, HEAD:K])
         w1b = load("w1b", [P, HEAD // 2], I32, w1_i32[:, HEAD // 2:K // 2])
-        w2b = load("w2b", [P, HEAD], I32, w2_i32[:, HEAD:K])
 
         priors = {}
 
@@ -122,8 +125,7 @@ def tile_list_semijoin_cache_kernel(tc, tab_words, tab_scales, offs, offs2, offs
         ident = keep.tile([P, P], F32, name="ident")
         make_identity(nc, ident[:])
         pages = [slot("page0", [P, T2], F32)]
-        for cols in (slice(0, T2 // 2 - 1), slice(T2 // 2 - 1, T2)):
-            nc.vector.memset(pages[0][:, cols], 0.0)
+        nc.vector.memset(pages[0][:], 0.0)
 
         v_scales = slot("v_scales", [P, S], U8)
         nc.vector.tensor_copy(v_scales[:], table_scales[:].indirect(idx[:]))
@@ -133,8 +135,8 @@ def tile_list_semijoin_cache_kernel(tc, tab_words, tab_scales, offs, offs2, offs
             nc.vector.tensor_copy(v_words[half][:], table[:].bitcast(U32).indirect(entries(idx, half_cols(half))))
         pages.append(slot("page1", [P, T2], F32))
         nc.gpsimd.memset(pages[1][:], 0.0)
-        scales_dealt = slot("scales_dealt", [P, PACK, P], U8)
-        nc.gpsimd.tensor_copy(scales_dealt[:], w_scales[:, K:H].rearrange("k (p t) -> k t p", t=PACK))
+        scales_dealt = slot("scales_dealt", [P, 2, PACK, P], U8)
+        nc.gpsimd.tensor_copy(scales_dealt[:], w_scales[:, :, K:H].rearrange("k w (p t) -> k w t p", t=PACK))
 
         def weave(woven, raw):
             nc.scalar.copy(woven.rearrange("p (c i) t -> p c t i", i=4), raw.rearrange("p t (c i) -> p c t i", i=4))
@@ -161,12 +163,13 @@ def tile_list_semijoin_cache_kernel(tc, tab_words, tab_scales, offs, offs2, offs
             if i >= PACK:
                 t = i - PACK
                 if which == D1:
-                    return dealt[D1][:, t, :].bitcast(E2M1), scales_dealt[:, t, :]
-                return dealt[D2][:, t, :].bitcast(E4M3), scales_dealt[W2_ROWS:P, t, :]
+                    return dealt[D1][:, t, :].bitcast(E2M1), scales_dealt[:, D1, t, :]
+                return dealt[D2][:, t, :].bitcast(E4M3), scales_dealt[W2_ROWS:P, D2, t, :]
             cols = slice(i * P, (i + 1) * P)
             if which == D1:
-                return (w1a, w1b)[i // 2][:, i % 2 * P // 2:(i % 2 + 1) * P // 2].bitcast(E2M1), w_scales[:, cols]
-            return (w2a, w2b)[i // 2][:, i % 2 * P:(i % 2 + 1) * P].bitcast(E4M3), w_scales[W2_ROWS:P, cols]
+                return (w1a, w1b)[i // 2][:, i % 2 * P // 2:(i % 2 + 1) * P // 2].bitcast(E2M1), w_scales[:, D1, cols]
+            words = w2a[:] if i == 0 else w2b[:, (i - 1) * P:i * P]
+            return words.bitcast(E4M3), w_scales[W2_ROWS:P, D2, cols]
 
         def signature(i, which, half, n):
             lhs, lhs_scale = stationary(i, which)
@@ -185,42 +188,44 @@ def tile_list_semijoin_cache_kernel(tc, tab_words, tab_scales, offs, offs2, offs
         def scatter(i):
             nc.vector.tensor_copy(pages[i % 2][:].indirect(idx2[:]), joint[i])
 
-        woven3a = weave(slot("woven3a", [P, HEAD, PACK], BF16)[:], raw3a[:])
+        woven30 = weave(slot("woven30", [P, P, PACK], BF16)[:], raw30[:])
+        woven31 = weave(slot("woven31", [P, P, PACK], BF16)[:], raw31[:])
         h0 = slot("h0", [P, S], F32)
 
-        def join_vector(which, half, bank, src):
+        def join_vector(bank, half, src, dst=h0):
             cols = half_cols(half)
-            nc.vector.tensor_tensor(h0[:, cols], signature(0, which, half, bank)[:], src[:, cols], MULT)
+            nc.vector.tensor_tensor(dst[:, cols], bank[:], src[:, cols], MULT)
 
-        join_vector(D2, 0, 0, wg)
-        join_vector(D1, 0, 2, h0)
-        join_vector(D2, 1, 1, wg)
-        quantise_w3(woven3a, 0, 2, slot("w3_codes0", [P, HEAD], U32)[:])
-        join_vector(D1, 1, 3, h0)
-        join_vector(D3, 0, 4, h0)
-        join_vector(D3, 1, 5, h0)
-        joint[0] = h0[:]
+        for half in range(2):
+            join_vector(signature(0, D1, half, half), half, wg)
+        second = [signature(0, D2, half, 2 + half) for half in range(2)]
+        join_vector(second[0], 0, h0)
+        quantise_w3(woven30, 0, 1, slot("w2a", [P, P], U32)[:])
+        join_vector(second[1], 1, h0)
+        quantise_w3(woven31, 1, 1, slot("w3_codes1", [P, P], U32)[:])
+        first_two = slot("woven31", [P, 2, S], F32)
+        for half in range(2):
+            join_vector(signature(0, D3, half, half), half, h0, first_two[:, 0, :])
+        joint[0] = first_two[:, 0, :]
         scatter(0)
         x0 = slot("x0", [P, BANK], F32)
         nc.vector.tensor_copy(x0[:], pages[0][:].indirect(entries(idx3, half_cols(0))))
 
-        h1 = slot("h1", [P, S], F32)
+        h1 = first_two[:, 1, :]
 
         def join_half(which, half, d, bank, src):
             nc.scalar.copy(d, signature(1, which, half, bank)[:])
             nc.gpsimd.tensor_tensor(h1[:, half_cols(half)], d, src[:, half_cols(half)], MULT)
 
-        early = slot("raw3a", [P, 2, BANK], F32)
-        join_half(D2, 0, early[:, 0, :], 0, wg)
-        join_half(D2, 1, slot("one_d2", [P, BANK], F32)[:], 1, wg)
-        join_half(D1, 0, early[:, 1, :], 2, h1)
-        join_half(D1, 1, slot("one_d1", [P, BANK], F32)[:], 3, h1)
-        join_half(D3, 0, slot("one_d3", [P, BANK], F32)[:], 6, h1)
+        for which, first, src in ((D1, 2, wg), (D3, 6, h1)):
+            for half in range(2):
+                join_half(which, half, slot("one%d_%d" % (which, half), [P, BANK], F32)[:], first + half, src)
+        join_half(D2, 0, slot("raw30", [P, BANK], F32)[:], 0, h1)
         woven3c = slot("woven3c", [P, K, PACK], BF16)
         nc.scalar.copy(woven3c[:].rearrange("k (t p) j -> k p t j", t=PACK), raw3c[:].rearrange("k j (p t) -> k p t j", t=PACK))
         woven3b = weave(slot("woven3b", [P, HEAD, PACK], BF16)[:], raw3b[:])
-        join_half(D3, 1, slot("raw3c", [P, BANK], F32)[:], 7, h1)
-        joint[1] = h1[:]
+        join_half(D2, 1, slot("raw3c", [P, BANK], F32)[:], 1, h1)
+        joint[1] = h1
         codes3 = slot("raw3c", [P, HEAD + K], U32)
         quantise_w3(woven3b, 2, 2, codes3[:, 0:HEAD])
         quantise_w3(woven3c[:], PACK, PACK, codes3[:, HEAD:HEAD + K])
@@ -316,11 +321,14 @@ def tile_list_semijoin_cache_kernel(tc, tab_words, tab_scales, offs, offs2, offs
             if i == PACK - 1:
                 z0_woven.append(weave_z0(0))
 
-        def squash_dealt(i, cols, x, y, bent):
+        def bend(i, cols, y, bent):
             t = i - PACK
-            nc.gpsimd.tensor_tensor(y, x, priors[i][:, cols], ADD)
             nc.scalar.activation(bent, y, ACT.Tanh)
             nc.scalar.activation(z1_woven[:, cols, t], bent, ACT.Copy, scale=gains[:, 1, t:t + 1])
+
+        def squash_dealt(i, cols, x, y, bent):
+            nc.gpsimd.tensor_tensor(y, x, priors[i][:, cols], ADD)
+            bend(i, cols, y, bent)
 
         sums = slot("planes0", [P, 3, EARLY_FETCH], F32)
         bent = slot("planes1", [P, 2, EARLY_FETCH], F32)
@@ -329,61 +337,69 @@ def tile_list_semijoin_cache_kernel(tc, tab_words, tab_scales, offs, offs2, offs
             squash_dealt(i, cols, x, sums[:, n, 0:width], bent[:, n % 2, 0:width])
         waiting.clear()
         codes = slot("d3_0", [P, 2 * N + BANK], U32)
-        z0 = [quantise(z0_woven[0], codes[:, 2 * N:2 * N + BANK], slot("z0_scales0", [P, BANK], U8)[:])]
+        z0 = {(0, BANK): quantise(z0_woven[0], codes[:, 2 * N:2 * N + BANK], slot("z0_scales0", [P, BANK], U8)[:])}
         w4_scales = slot("w4_scales", [P, 2 * N], U8)
         quantise(w4_woven[:].rearrange("p b c t -> p (b c) t"), codes[:, 0:2 * N], w4_scales[:])
         w4q = [(codes[:, b * N:(b + 1) * N], w4_scales[:, b * N:(b + 1) * N]) for b in range(2)]
         x = slot("z0_woven0", [P, PR + HEAD], F32)
         bent = slot("planes1", [P, 2, BANK], F32)
-        fetch(LAST - 2, slice(EARLY_FETCH, PR), x[:, PR:PR + HEAD])
-        for half in range(2):
-            fetch(LAST - 1, half_cols(half), x[:, half_cols(half)])
-        for n, (i, cols, x) in enumerate(waiting):
-            squash_dealt(i, cols, x, x, bent[:, n % 2, 0:cols.stop - cols.start])
-        scatter(LAST)
-        z0.append(quantise(z0_woven[1], slot("z0_woven0", [P, BANK], U32)[:], slot("z0_scales1", [P, BANK], U8)[:]))
+        late = [(LAST - 2, slice(EARLY_FETCH, PR), x[:, PR:PR + HEAD])] + [(LAST - 1, half_cols(half), x[:, half_cols(half)]) for half in range(2)]
+        for i, cols, y in late:
+            nc.vector.tensor_tensor(y, pages[i % 2][:].indirect(entries(idx3, cols)), priors[i][:, cols], ADD)
+        for n, (i, cols, y) in enumerate(late):
+            bend(i, cols, y, bent[:, n % 2, 0:cols.stop - cols.start])
+        def quantise_z0(cols, tag):
+            mine = slice(cols.start - BANK, cols.stop - BANK)
+            width = cols.stop - cols.start
+            z0[cols.start, cols.stop] = quantise(z0_woven[1][:, mine, :], slot(tag, [P, width], U32)[:],
+                                                 slot("z0_scales%d" % cols.start, [P, width], U8)[:])
 
         chunks = [slice(sum(CHUNKS[:c]), sum(CHUNKS[:c + 1])) for c in range(len(CHUNKS))]
 
         def estimate_pass(b, banks, pieces):
-            w_codes, w_scales = w4q[b]
+            w_codes, w_scales4 = w4q[b]
             per_bank = N // P // len(banks)
-            for part, (at, z_codes, z_scales) in enumerate(pieces):
-                for n in range(N // P):
+            steps = [(part, n) for part in range(len(pieces)) for n in range(N // P)]
+            if b == 1:
+                steps = [(part, n) for n in range(N // P) for part in range(len(pieces))]
+            for part, n in steps:
+                if True:
+                    at, z_codes, z_scales = pieces[part]
                     cols = slice(n * P, (n + 1) * P)
                     nc.tensor.matmul_mx(out=banks[n // per_bank][:, n % per_bank, at], lhsT=w_codes[:, cols].bitcast(E4M3),
-                                        lhsT_scale=w_scales[:, cols], rhs=z_codes.bitcast(E4M3), rhs_scale=z_scales,
+                                        lhsT_scale=w_scales4[:, cols], rhs=z_codes.bitcast(E4M3), rhs_scale=z_scales,
                                         start=b == 0 and part == 0 and n % per_bank == 0,
-                                        stop=b == 1 and n % per_bank == per_bank - 1)
+                                        stop=b == 1 and part == len(pieces) - 1 and n % per_bank == per_bank - 1)
 
-        def first_pass(banks, cols):
+        opened = {}
+
+        def first_pass(c):
+            cols = chunks[c]
+            opened[c] = [bank_tile(n, [P, N // P // len(BANKS[c]), CHUNKS[c]]) for n in BANKS[c]]
             pieces = []
-            for half, (z_codes, z_scales) in enumerate(z0):
-                lo, hi = max(cols.start, half * BANK), min(cols.stop, (half + 1) * BANK)
-                if lo < hi:
-                    mine = slice(lo - half * BANK, hi - half * BANK)
-                    pieces.append((slice(lo - cols.start, hi - cols.start), z_codes[:, mine], z_scales[:, mine]))
-            estimate_pass(0, banks, pieces)
+            for (first, stop), (z_codes, z_scales) in z0.items():
+                lo, hi = max(cols.start, first), min(cols.stop, stop)
+                while lo < hi:
+                    end = lo + HEAD if hi - lo == HEAD + P else hi
+                    mine = slice(lo - first, end - first)
+                    pieces.append((slice(lo - cols.start, end - cols.start), z_codes[:, mine], z_scales[:, mine]))
+                    lo = end
+            estimate_pass(0, opened[c], pieces)
 
-        opened = []
-        for c, cols in enumerate(chunks):
-            if c == len(chunks) - 1:
-                break
-            banks = [bank_tile(n, [P, BANK // CHUNKS[c], CHUNKS[c]]) for n in range(cols.start // P, cols.stop // P)]
-            first_pass(banks, cols)
-            opened.append(banks)
-
-        res = slot("table", [P, PR // P, BANK], F32)
+        res = slot("table", [P, N // P * PR], F32)
         squash = {}
+        fetched = {}
         x_tail = slot("planes1", [P, 2, max(CHUNKS)], F32)
 
         def tail_fetch(c):
             cols = chunks[c]
             x = x_tail[:, c % 2, 0:CHUNKS[c]]
-            nc.vector.tensor_tensor(x, pages[LAST % 2][:].indirect(idx3[:, cols.start // 16:cols.stop // 16]),
-                                    priors[LAST][:, cols], ADD)
+            nc.vector.tensor_tensor(x, pages[LAST % 2][:].indirect(entries(idx3, cols)), priors[LAST][:, cols], ADD)
+            fetched[c] = x
+
+        def tail_tanh(c):
             squash[c] = slot("tz%d" % c, [P, CHUNKS[c]], F32)
-            nc.scalar.activation(squash[c][:], x, ACT.Tanh)
+            nc.scalar.activation(squash[c][:], fetched[c], ACT.Tanh)
 
         def tail_gain(c):
             if c in SCALAR_GAINS:
@@ -395,23 +411,50 @@ def tile_list_semijoin_cache_kernel(tc, tab_words, tab_scales, offs, offs2, offs
             cols = chunks[c]
             z_codes, z_scales = quantise(z1_woven[:, cols, :], slot("z1_codes%d" % c, [P, CHUNKS[c]], U32)[:],
                                          slot("z1_scales%d" % c, [P, CHUNKS[c]], U8)[:])
-            estimate_pass(1, opened[c], [(slice(0, CHUNKS[c]), z_codes, z_scales)])
-            staged_all = res[:, cols.start // P:cols.stop // P, :].rearrange("p b (k m) -> p (b k) m", m=CHUNKS[c])
+            cuts = [slice(0, HEAD), slice(HEAD, CHUNKS[c])] if CHUNKS[c] > HEAD and CHUNKS[c] < BANK else [slice(0, CHUNKS[c])]
+            estimate_pass(1, opened[c], [(at, z_codes[:, at], z_scales[:, at]) for at in cuts])
+
+        def tail_store(c, only=None):
+            cols = chunks[c]
+            staged_all = res[:, N // P * cols.start:N // P * cols.stop].rearrange("p (k m) -> p k m", m=CHUNKS[c])
             for n, bank in enumerate(opened[c]):
+                if only is not None and n != only:
+                    continue
                 rows = N // len(opened[c])
                 staged = staged_all[:, n * rows // P:(n + 1) * rows // P, :]
                 copy = nc.vector.tensor_copy if (c, n) in ON_VECTOR else nc.scalar.copy
                 copy(staged, bank[:])
                 nc.sync.dma_start(out[n * rows:(n + 1) * rows, cols].rearrange("(k p) m -> p k m", p=P), staged)
 
+        scatter(LAST)
+        quantise_z0(slice(BANK, PR), "z0_woven0")
+        first_pass(0)
+        first_pass(1)
+        first_pass(2)
+        first_pass(3)
         tail_fetch(0)
+        tail_tanh(0)
         tail_fetch(1)
-        for c in range(len(chunks)):
-            tail_gain(c)
-            if c + 2 < len(chunks):
-                tail_fetch(c + 2)
-            tail_close(c)
-            if c == 0:
-                cols = chunks[-1]
-                opened.append([bank_tile(n, [P, 2, CHUNKS[-1]]) for n in (7, 0)])
-                first_pass(opened[-1], cols)
+        tail_tanh(1)
+        tail_gain(0)
+        tail_fetch(2)
+        tail_tanh(2)
+        tail_close(0)
+        tail_store(0)
+        first_pass(4)
+        tail_gain(1)
+        tail_fetch(3)
+        tail_tanh(3)
+        tail_close(1)
+        tail_store(1)
+        tail_gain(2)
+        tail_fetch(4)
+        tail_tanh(4)
+        tail_close(2)
+        tail_store(2)
+        tail_gain(3)
+        tail_close(3)
+        tail_store(3)
+        tail_gain(4)
+        tail_close(4)
+        tail_store(4)

@@ -70,7 +70,8 @@ def tile_list_semijoin_cache_kernel(tc, tab_words, tab_scales, offs, offs2, offs
         table = slot("table", [P, T], I32)
         table_scales = slot("page1", [P, T], U8)
         w_scales = slot("w_scales", [P, 2, H], U8)
-        nc.vector.memset(table_scales[:].bitcast(I32), 0)
+        nc.gpsimd.memset(table_scales[:, 0:T // 2].bitcast(I32), 0)
+        nc.vector.memset(table_scales[:, T // 2:T].bitcast(I32), 0)
         nc.gpsimd.memset(w_scales[:, D2, :].bitcast(I32), 0)
         nc.vector.memset(w_scales[:, D1, :].bitcast(I32), 0)
 
@@ -321,10 +322,15 @@ def tile_list_semijoin_cache_kernel(tc, tab_words, tab_scales, offs, offs2, offs
             if i == PACK - 1:
                 z0_woven.append(weave_z0(0))
 
+        z1_planes = slot("raw3b", [P, PACK - 1, PR], BF16)
+
         def bend(i, cols, y, bent):
             t = i - PACK
             nc.scalar.activation(bent, y, ACT.Tanh)
-            nc.scalar.activation(z1_woven[:, cols, t], bent, ACT.Copy, scale=gains[:, 1, t:t + 1])
+            nc.scalar.activation(z1_planes[:, t, cols], bent, ACT.Copy, scale=gains[:, 1, t:t + 1])
+            if i == LAST - 1:
+                nc.scalar.copy(z1_woven[:, cols, 0:PACK - 1].rearrange("p (c i) t -> p c t i", i=4),
+                               z1_planes[:, :, cols].rearrange("p t (c i) -> p c t i", i=4))
 
         def squash_dealt(i, cols, x, y, bent):
             nc.gpsimd.tensor_tensor(y, x, priors[i][:, cols], ADD)
@@ -339,13 +345,13 @@ def tile_list_semijoin_cache_kernel(tc, tab_words, tab_scales, offs, offs2, offs
         codes = slot("d3_0", [P, 2 * N + BANK], U32)
         z0 = {(0, BANK): quantise(z0_woven[0], codes[:, 2 * N:2 * N + BANK], slot("z0_scales0", [P, BANK], U8)[:])}
         w4_scales = slot("w4_scales", [P, 2 * N], U8)
-        quantise(w4_woven[:].rearrange("p b c t -> p (b c) t"), codes[:, 0:2 * N], w4_scales[:])
-        w4q = [(codes[:, b * N:(b + 1) * N], w4_scales[:, b * N:(b + 1) * N]) for b in range(2)]
+        w4q = [quantise(w4_woven[:, 0, :, :], codes[:, 0:N], w4_scales[:, 0:N])]
         x = slot("z0_woven0", [P, PR + HEAD], F32)
         bent = slot("planes1", [P, 2, BANK], F32)
         late = [(LAST - 2, slice(EARLY_FETCH, PR), x[:, PR:PR + HEAD])] + [(LAST - 1, half_cols(half), x[:, half_cols(half)]) for half in range(2)]
         for i, cols, y in late:
             nc.vector.tensor_tensor(y, pages[i % 2][:].indirect(entries(idx3, cols)), priors[i][:, cols], ADD)
+        w4q.append(quantise(w4_woven[:, 1, :, :], codes[:, N:2 * N], w4_scales[:, N:2 * N]))
         for n, (i, cols, y) in enumerate(late):
             bend(i, cols, y, bent[:, n % 2, 0:cols.stop - cols.start])
         def quantise_z0(cols, tag):

@@ -29,9 +29,9 @@ W2_ROWS = 4
 TURN_BANKS = (6, 7)
 PRIOR_BUFFERS = 5
 EARLY_FETCH = PR - HEAD
-CHUNKS = (128, 256, 256, 256, 128)
-BANKS = ((0,), (1, 2), (3, 4), (5, 6), (7, 0))
-ON_VECTOR = ((4, 1),)
+CHUNKS = (128, 256, 384, 256)
+BANKS = ((0, 1), (2, 3), (4, 5, 6, 7), (0, 1))
+ON_VECTOR = ((3, 1),)
 SCALAR_GAINS = (1,)
 D1, D2, D3 = 0, 1, 2
 
@@ -433,11 +433,10 @@ def tile_list_semijoin_cache_kernel(tc, tab_words, tab_scales, offs, offs2, offs
                 nc.sync.dma_start(out[n * rows:(n + 1) * rows, cols].rearrange("(k p) m -> p k m", p=P), staged)
 
         scatter(LAST)
-        quantise_z0(slice(BANK, PR), "z0_woven0")
+        quantise_z0(slice(BANK, BANK + HEAD), "z0_woven0")
         first_pass(0)
         first_pass(1)
         first_pass(2)
-        first_pass(3)
         tail_fetch(0)
         tail_tanh(0)
         tail_fetch(1)
@@ -447,20 +446,16 @@ def tile_list_semijoin_cache_kernel(tc, tab_words, tab_scales, offs, offs2, offs
         tail_tanh(2)
         tail_close(0)
         tail_store(0)
-        first_pass(4)
         tail_gain(1)
         tail_fetch(3)
         tail_tanh(3)
         tail_close(1)
-        tail_store(1)
         tail_gain(2)
-        tail_fetch(4)
-        tail_tanh(4)
+        tail_store(1)
         tail_close(2)
+        quantise_z0(slice(BANK + HEAD, PR), "tz1")
+        first_pass(3)
         tail_store(2)
         tail_gain(3)
         tail_close(3)
         tail_store(3)
-        tail_gain(4)
-        tail_close(4)
-        tail_store(4)

@@ -187,7 +187,10 @@ def tile_list_semijoin_cache_kernel(tc, tab_words, tab_scales, offs, offs2, offs
         joint = {}
 
         def scatter(i):
-            nc.vector.tensor_copy(pages[i % 2][:].indirect(idx2[:]), joint[i])
+            if i == LAST:
+                nc.vector.tensor_tensor(pages[i % 2][:].indirect(idx2[:]), joint[i], wg_dealt[i - PACK][:], MULT)
+            else:
+                nc.vector.tensor_copy(pages[i % 2][:].indirect(idx2[:]), joint[i])
 
         woven30 = weave(slot("woven30", [P, P, PACK], BF16)[:], raw30[:])
         woven31 = weave(slot("woven31", [P, P, PACK], BF16)[:], raw31[:])
@@ -237,8 +240,6 @@ def tile_list_semijoin_cache_kernel(tc, tab_words, tab_scales, offs, offs2, offs
             nc.scalar.copy(dealt[D1][:].rearrange("k t p -> k p t"), w1c[:].bitcast(U16).rearrange("k (p t) -> k p t", t=PACK))
             nc.scalar.copy(dealt[D2][:].rearrange("k t p -> k p t"), w2c[:].bitcast(U32).rearrange("k (p t) -> k p t", t=PACK))
 
-        held = {}
-
         def join(i):
             if i == 2:
                 behind = slot("raw3b", [P, 2, S], F32)
@@ -250,15 +251,12 @@ def tile_list_semijoin_cache_kernel(tc, tab_words, tab_scales, offs, offs2, offs
             d3 = copy_out(i, D3, slot("d3_%d" % (i % 3), [P, S], F32), 4)
             u = slot("woven3c", [P, S], F32) if i == 2 else d1
             nc.gpsimd.tensor_tensor(u[:], d1[:], d2[:], MULT)
-            held[i] = u, d3
-            if i < LAST:
-                finish(i, slot("h%d" % (i % 3), [P, S], F32), None)
-
-        def finish(i, h, v):
-            u, d3 = held[i]
-            v = v or h
-            nc.gpsimd.tensor_tensor(v[:], d3[:], wg[:] if i < PACK else wg_dealt[i - PACK][:], MULT)
-            nc.gpsimd.tensor_tensor(h[:], u[:], v[:], MULT)
+            h = slot("h%d" % (i % 3), [P, S], F32)
+            if i == LAST:
+                nc.gpsimd.tensor_tensor(h[:], u[:], d3[:], MULT)
+            else:
+                nc.gpsimd.tensor_tensor(h[:], d3[:], wg[:] if i < PACK else wg_dealt[i - PACK][:], MULT)
+                nc.gpsimd.tensor_tensor(h[:], u[:], h[:], MULT)
             joint[i] = h[:]
 
         squashed = slot("table", [P, PR // P, PACK, P], F32)
@@ -311,7 +309,6 @@ def tile_list_semijoin_cache_kernel(tc, tab_words, tab_scales, offs, offs2, offs
                 fetch(i - 1, half_cols(1), x[:, 0:BANK])
                 if i == PACK:
                     z0_woven.append(weave_z0(1))
-                    finish(LAST, slot("h%d" % (LAST % 3), [P, S], F32), slot("planes0", [P, S], F32))
                 fetch(i, slice(0, ahead), x[:, BANK:BANK + ahead])
             if i + 3 <= LAST:
                 load_prior(i + 3)
@@ -336,7 +333,7 @@ def tile_list_semijoin_cache_kernel(tc, tab_words, tab_scales, offs, offs2, offs
             nc.gpsimd.tensor_tensor(y, x, priors[i][:, cols], ADD)
             bend(i, cols, y, bent)
 
-        sums = slot("planes0", [P, 3, EARLY_FETCH], F32)
+        sums = slot("u%d" % (LAST % 2), [P, 3, EARLY_FETCH], F32)
         bent = slot("planes1", [P, 2, EARLY_FETCH], F32)
         for n, (i, cols, x) in enumerate(waiting):
             width = cols.stop - cols.start

@@ -32,6 +32,7 @@ EARLY_FETCH = PR - HEAD
 CHUNKS = (128, 256, 384, 256)
 BANKS = ((0, 1), (2, 3), (4, 5, 6, 7), (0, 1))
 ON_VECTOR = ((3, 1),)
+STORE_BANKS = (1, 1, 1, 1)
 SCALAR_GAINS = (1,)
 D1, D2, D3 = 0, 1, 2
 
@@ -339,22 +340,22 @@ def tile_list_semijoin_cache_kernel(tc, tab_words, tab_scales, offs, offs2, offs
             width = cols.stop - cols.start
             squash_dealt(i, cols, x, sums[:, n, 0:width], bent[:, n % 2, 0:width])
         waiting.clear()
-        codes = slot("d3_0", [P, 2 * N + BANK], U32)
-        z0 = {(0, BANK): quantise(z0_woven[0], codes[:, 2 * N:2 * N + BANK], slot("z0_scales0", [P, BANK], U8)[:])}
-        w4_scales = slot("w4_scales", [P, 2 * N], U8)
-        w4q = [quantise(w4_woven[:, 0, :, :], codes[:, 0:N], w4_scales[:, 0:N])]
-        x = slot("z0_woven0", [P, PR + HEAD], F32)
+        x = slot("d3_0", [P, PR + HEAD], F32)
         bent = slot("planes1", [P, 2, BANK], F32)
         late = [(LAST - 2, slice(EARLY_FETCH, PR), x[:, PR:PR + HEAD])] + [(LAST - 1, half_cols(half), x[:, half_cols(half)]) for half in range(2)]
         for i, cols, y in late:
             nc.vector.tensor_tensor(y, pages[i % 2][:].indirect(entries(idx3, cols)), priors[i][:, cols], ADD)
+        codes = slot("prior%d" % ((LAST - 2) % PRIOR_BUFFERS), [P, 2 * N + 128], U32)
+        z0 = {(0, 128): quantise(z0_woven[0][:, 0:128, :], codes[:, 2 * N:2 * N + 128], slot("z0_scales0", [P, 128], U8)[:])}
+        w4_scales = slot("w4_scales", [P, 2 * N], U8)
+        w4q = [quantise(w4_woven[:, 0, :, :], codes[:, 0:N], w4_scales[:, 0:N])]
         w4q.append(quantise(w4_woven[:, 1, :, :], codes[:, N:2 * N], w4_scales[:, N:2 * N]))
         for n, (i, cols, y) in enumerate(late):
             bend(i, cols, y, bent[:, n % 2, 0:cols.stop - cols.start])
         def quantise_z0(cols, tag):
-            mine = slice(cols.start - BANK, cols.stop - BANK)
+            mine = slice(cols.start % BANK, (cols.stop - 1) % BANK + 1)
             width = cols.stop - cols.start
-            z0[cols.start, cols.stop] = quantise(z0_woven[1][:, mine, :], slot(tag, [P, width], U32)[:],
+            z0[cols.start, cols.stop] = quantise(z0_woven[cols.start // BANK][:, mine, :], slot(tag, [P, width], U32)[:],
                                                  slot("z0_scales%d" % cols.start, [P, width], U8)[:])
 
         chunks = [slice(sum(CHUNKS[:c]), sum(CHUNKS[:c + 1])) for c in range(len(CHUNKS))]
@@ -427,13 +428,15 @@ def tile_list_semijoin_cache_kernel(tc, tab_words, tab_scales, offs, offs2, offs
                 staged = staged_all[:, n * rows // P:(n + 1) * rows // P, :]
                 copy = nc.vector.tensor_copy if (c, n) in ON_VECTOR else nc.scalar.copy
                 copy(staged, bank[:])
-                nc.sync.dma_start(out[n * rows:(n + 1) * rows, cols].rearrange("(k p) m -> p k m", p=P), staged)
+                group = STORE_BANKS[c]
+                if n % group == group - 1:
+                    lo, hi = (n + 1 - group) * rows, (n + 1) * rows
+                    nc.sync.dma_start(out[lo:hi, cols].rearrange("(k p) m -> p k m", p=P), staged_all[:, lo // P:hi // P, :])
 
-        scatter(LAST)
-        quantise_z0(slice(BANK, BANK + HEAD), "z0_woven0")
         first_pass(0)
+        scatter(LAST)
+        quantise_z0(slice(128, 384), "d3_0")
         first_pass(1)
-        first_pass(2)
         tail_fetch(0)
         tail_tanh(0)
         tail_fetch(1)
@@ -448,9 +451,12 @@ def tile_list_semijoin_cache_kernel(tc, tab_words, tab_scales, offs, offs2, offs
         tail_tanh(3)
         tail_close(1)
         tail_gain(2)
+        quantise_z0(slice(384, 512), "tz0")
+        quantise_z0(slice(512, 768), "tz1")
+        first_pass(2)
         tail_store(1)
         tail_close(2)
-        quantise_z0(slice(BANK + HEAD, PR), "tz1")
+        quantise_z0(slice(768, 1024), "tz2")
         first_pass(3)
         tail_store(2)
         tail_gain(3)

@@ -28,13 +28,16 @@ TABLE_FIRST = T // 4
 W2_ROWS = 4
 TURN_BANKS = (6, 7)
 PRIOR_BUFFERS = 5
-EARLY_FETCH = PR - HEAD
+EARLY_FETCH = HEAD
 CHUNKS = (128, 256, 384, 256)
 BANKS = ((0, 1), (2, 3), (4, 5, 6, 7), (0, 1))
 ON_VECTOR = ((3, 1),)
 STORE_BANKS = (1, 1, 1, 1)
 SCALAR_GAINS = (1,)
 D1, D2, D3 = 0, 1, 2
+D3_TAGS = {2: "d3_2", 3: "d3_2", 4: "d3_0", 5: "d3_2", 6: "d3_0", 7: "d3_1"}
+D2_TAGS = {2: "d2_0", 3: "raw3c", 4: "d2_1", 5: "raw3c", 6: "d2_1", 7: "d2_0"}
+D1_TAGS = {2: "d1_0", 3: "d1_0", 4: "d1_1", 5: "d1_1", 6: "woven3b", 7: "raw3a"}
 
 
 def tile_list_semijoin_cache_kernel(tc, tab_words, tab_scales, offs, offs2, offs3, w1_words, w1_scales,
@@ -69,11 +72,11 @@ def tile_list_semijoin_cache_kernel(tc, tab_words, tab_scales, offs, offs2, offs
         idx2 = keep.tile([P, S // 16], U16, name="idx2")
         idx3 = keep.tile([P, PR // 16], U16, name="idx3")
         table = slot("table", [P, T], I32)
-        table_scales = slot("page1", [P, T], U8)
+        table_scales = slot("table_scales", [P, T], U8)
         w_scales = slot("w_scales", [P, 2, H], U8)
+        nc.gpsimd.memset(w_scales[:, D2, :].bitcast(I32), 0)
         nc.gpsimd.memset(table_scales[:, 0:T // 2].bitcast(I32), 0)
         nc.vector.memset(table_scales[:, T // 2:T].bitcast(I32), 0)
-        nc.gpsimd.memset(w_scales[:, D2, :].bitcast(I32), 0)
         nc.vector.memset(w_scales[:, D1, :].bitcast(I32), 0)
 
         w3_rows = w3.rearrange("(p j) c -> p j c", j=PACK)
@@ -88,18 +91,16 @@ def tile_list_semijoin_cache_kernel(tc, tab_words, tab_scales, offs, offs2, offs
         load_scales(nc.gpsimd, w_scales[:, D2, :], w2_scales, W2_ROWS)
         w1a = load("w1a", [P, HEAD // 2], I32, w1_i32[:, 0:HEAD // 2])
         load_scales(nc.sync, w_scales[:, D1, :], w1_scales, 0)
+        w2a = load("w2a", [P, HEAD], I32, w2_i32[:, 0:HEAD])
+        raw3a = load("raw3a", [P, PACK, HEAD], F32, w3_rows[:, :, 0:HEAD])
         wg = slot("wg", [P, S], F32)
         nc.sync.dma_start(wg[:, half_cols(0)], wgs[:, half_cols(0)])
-        raw30 = load("raw30", [P, PACK, P], F32, w3_rows[:, :, 0:P])
         nc.sync.dma_start(wg[:, half_cols(1)], wgs[:, half_cols(1)])
-        w2a = load("w2a", [P, P], I32, w2_i32[:, 0:P])
-        raw31 = load("raw31", [P, PACK, P], F32, w3_rows[:, :, P:HEAD])
         nc.sync.dma_start(idx2[:], offs2)
-        w2b = load("w2b", [P, 3 * P], I32, w2_i32[:, P:K])
-        nc.sync.dma_start(idx3[:], offs3)
-        raw3c = load("raw3c", [P, PACK, K], F32, w3_rows[:, :, K:H])
         raw3b = load("raw3b", [P, PACK, HEAD], F32, w3_rows[:, :, HEAD:K])
         w1b = load("w1b", [P, HEAD // 2], I32, w1_i32[:, HEAD // 2:K // 2])
+        w2b = load("w2b", [P, HEAD], I32, w2_i32[:, HEAD:K])
+        nc.sync.dma_start(idx3[:], offs3)
 
         priors = {}
 
@@ -107,27 +108,31 @@ def tile_list_semijoin_cache_kernel(tc, tab_words, tab_scales, offs, offs2, offs
             rows = prior[i * P:(i + 1) * P, :] if i < PACK else prior[K:H, :].rearrange("(p t) m -> t p m", t=PACK)[i - PACK]
             priors[i] = load("prior%d" % (i % PRIOR_BUFFERS), [P, PR], F32, rows)
 
-        load_prior(0)
+        raw3c = load("raw3c", [P, PACK, K], F32, w3_rows[:, :, K:H])
         w1c = load("w1c", [P, K // 2], I32, w1_i32[:, K // 2:K])
         w2c = load("w2c", [P, K], I32, w2_i32[:, K:H])
-        load_prior(1)
-        raw4 = [load(tag, [P, PACK, N], F32, w4[b * K:(b + 1) * K, :].rearrange("(p j) n -> p j n", j=PACK))
-                for b, tag in enumerate(("z0_woven0", "z1_woven"))]
         wg_dealt = []
-        gains = keep.tile([P, 2, PACK], F32, name="gains")
-        for t in range(PACK):
+
+        def load_dealt_wgs(t):
             wg_dealt.append(slot("wg_dealt%d" % t, [P, S], F32))
             for a in (0, 2, 1, 3):
                 nc.sync.dma_start(wg_dealt[t][32 * a:32 * a + 32, :], wgs.rearrange("(c t) j -> t c j", t=PACK)[t])
-            if t < 2:
-                load_prior(2 + t)
-            if t == 1:
-                nc.sync.dma_start(gains[:], gain.rearrange("(b p t) -> p b t", p=P, t=PACK))
+
+        for t in range(PACK - 1):
+            load_prior(t)
+            load_dealt_wgs(t)
+        gains = keep.tile([P, 2, PACK], F32, name="gains")
+        nc.sync.dma_start(gains[:], gain.rearrange("(b p t) -> p b t", p=P, t=PACK))
+        load_prior(PACK - 1)
+        raw4 = [load(tag, [P, PACK, N], F32, w4[b * K:(b + 1) * K, :].rearrange("(p j) n -> p j n", j=PACK))
+                for b, tag in enumerate(("raw4a", "z1_woven"))]
+        load_dealt_wgs(PACK - 1)
 
         ident = keep.tile([P, P], F32, name="ident")
         make_identity(nc, ident[:])
-        pages = [slot("page0", [P, T2], F32)]
+        pages = [slot("page%d" % n, [P, T2], F32) for n in range(2)]
         nc.vector.memset(pages[0][:], 0.0)
+        nc.gpsimd.memset(pages[1][:], 0.0)
 
         v_scales = slot("v_scales", [P, S], U8)
         nc.vector.tensor_copy(v_scales[:], table_scales[:].indirect(idx[:]))
@@ -135,10 +140,8 @@ def tile_list_semijoin_cache_kernel(tc, tab_words, tab_scales, offs, offs2, offs
         for half in range(2):
             v_words.append(slot("v_words%d" % half, [P, BANK], U32))
             nc.vector.tensor_copy(v_words[half][:], table[:].bitcast(U32).indirect(entries(idx, half_cols(half))))
-        pages.append(slot("page1", [P, T2], F32))
-        nc.gpsimd.memset(pages[1][:], 0.0)
         scales_dealt = slot("scales_dealt", [P, 2, PACK, P], U8)
-        nc.gpsimd.tensor_copy(scales_dealt[:], w_scales[:, :, K:H].rearrange("k w (p t) -> k w t p", t=PACK))
+        nc.vector.tensor_copy(scales_dealt[:], w_scales[:, :, K:H].rearrange("k w (p t) -> k w t p", t=PACK))
 
         def weave(woven, raw):
             nc.scalar.copy(woven.rearrange("p (c i) t -> p c t i", i=4), raw.rearrange("p t (c i) -> p c t i", i=4))
@@ -150,9 +153,10 @@ def tile_list_semijoin_cache_kernel(tc, tab_words, tab_scales, offs, offs2, offs
 
         w3q = {}
 
-        def quantise_w3(woven, first, count, codes):
+        def quantise_w3(woven, first, count, tag):
+            codes = slot(tag, [P, count * P], U32)
             scales = slot("w3_scales%d" % first, [P, count * P], U8)
-            quantise(woven, codes, scales[:])
+            quantise(woven, codes[:], scales[:])
             for k in range(count):
                 w3q[first + k] = codes[:, k * P:(k + 1) * P], scales[:, k * P:(k + 1) * P]
 
@@ -170,8 +174,7 @@ def tile_list_semijoin_cache_kernel(tc, tab_words, tab_scales, offs, offs2, offs
             cols = slice(i * P, (i + 1) * P)
             if which == D1:
                 return (w1a, w1b)[i // 2][:, i % 2 * P // 2:(i % 2 + 1) * P // 2].bitcast(E2M1), w_scales[:, D1, cols]
-            words = w2a[:] if i == 0 else w2b[:, (i - 1) * P:i * P]
-            return words.bitcast(E4M3), w_scales[W2_ROWS:P, D2, cols]
+            return (w2a, w2b)[i // 2][:, i % 2 * P:(i % 2 + 1) * P].bitcast(E4M3), w_scales[W2_ROWS:P, D2, cols]
 
         def signature(i, which, half, n):
             lhs, lhs_scale = stationary(i, which)
@@ -180,60 +183,65 @@ def tile_list_semijoin_cache_kernel(tc, tab_words, tab_scales, offs, offs2, offs
                                 rhs_scale=v_scales[:, half_cols(half)], start=True, stop=True)
             return bank
 
+        def copy_half(i, which, half, dst, n):
+            nc.scalar.copy(dst, signature(i, which, half, n)[:])
+            return dst
+
         def copy_out(i, which, dst, first):
             for half in range(2):
-                nc.scalar.copy(dst[:, half_cols(half)], signature(i, which, half, first + half)[:])
-            return dst
+                copy_half(i, which, half, dst[:, half_cols(half)], first + half)
+            return dst[:]
 
         joint = {}
 
-        def scatter(i):
+        def scatter(i, cols=slice(0, S)):
+            page = pages[i % 2][:].indirect(entries(idx2, cols))
             if i == LAST:
-                nc.vector.tensor_tensor(pages[i % 2][:].indirect(idx2[:]), joint[i], wg_dealt[i - PACK][:], MULT)
+                nc.vector.tensor_tensor(page, joint[i][:, cols], wg_dealt[i - PACK][:, cols], MULT)
             else:
-                nc.vector.tensor_copy(pages[i % 2][:].indirect(idx2[:]), joint[i])
+                nc.vector.tensor_copy(page, joint[i][:, cols])
 
-        woven30 = weave(slot("woven30", [P, P, PACK], BF16)[:], raw30[:])
-        woven31 = weave(slot("woven31", [P, P, PACK], BF16)[:], raw31[:])
-        h0 = slot("h0", [P, S], F32)
+        def multiply(h, u, v, a, b, c, d):
+            nc.gpsimd.tensor_tensor(u, a, b, MULT)
+            nc.gpsimd.tensor_tensor(v, c, d, MULT)
+            nc.gpsimd.tensor_tensor(h, u, v, MULT)
 
-        def join_vector(bank, half, src, dst=h0):
-            cols = half_cols(half)
-            nc.vector.tensor_tensor(dst[:, cols], bank[:], src[:, cols], MULT)
-
-        for half in range(2):
-            join_vector(signature(0, D1, half, half), half, wg)
-        second = [signature(0, D2, half, 2 + half) for half in range(2)]
-        join_vector(second[0], 0, h0)
-        quantise_w3(woven30, 0, 1, slot("w2a", [P, P], U32)[:])
-        join_vector(second[1], 1, h0)
-        quantise_w3(woven31, 1, 1, slot("w3_codes1", [P, P], U32)[:])
-        first_two = slot("woven31", [P, 2, S], F32)
-        for half in range(2):
-            join_vector(signature(0, D3, half, half), half, h0, first_two[:, 0, :])
-        joint[0] = first_two[:, 0, :]
-        scatter(0)
-        x0 = slot("x0", [P, BANK], F32)
-        nc.vector.tensor_copy(x0[:], pages[0][:].indirect(entries(idx3, half_cols(0))))
-
-        h1 = first_two[:, 1, :]
-
-        def join_half(which, half, d, bank, src):
-            nc.scalar.copy(d, signature(1, which, half, bank)[:])
-            nc.gpsimd.tensor_tensor(h1[:, half_cols(half)], d, src[:, half_cols(half)], MULT)
-
-        for which, first, src in ((D1, 2, wg), (D3, 6, h1)):
-            for half in range(2):
-                join_half(which, half, slot("one%d_%d" % (which, half), [P, BANK], F32)[:], first + half, src)
-        join_half(D2, 0, slot("raw30", [P, BANK], F32)[:], 0, h1)
-        woven3c = slot("woven3c", [P, K, PACK], BF16)
-        nc.scalar.copy(woven3c[:].rearrange("k (t p) j -> k p t j", t=PACK), raw3c[:].rearrange("k j (p t) -> k p t j", t=PACK))
+        first, second = half_cols(0), half_cols(1)
+        joint[0] = slot("h0", [P, S], F32)
+        joint[1] = slot("h1", [P, S], F32)
+        woven3a = weave(slot("woven3a", [P, HEAD, PACK], BF16)[:], raw3a[:])
+        behind_weave = slot("raw3a", [P, 2, S], F32)
+        ones = [behind_weave[:, D1, :], behind_weave[:, D2, :], slot("d3_1", [P, BANK], F32)]
+        h0 = joint[0][:, first]
+        nc.vector.tensor_tensor(h0, signature(0, D1, 0, 0)[:], wg[:, first], MULT)
+        copy_half(1, D1, 0, ones[D1][:, first], 3)
+        quantise_w3(woven3a, 0, 2, "w3_codes0")
+        nc.vector.tensor_tensor(h0, signature(0, D2, 0, 1)[:], h0, MULT)
+        copy_half(1, D2, 0, ones[D2][:, first], 4)
+        nc.vector.tensor_tensor(h0, signature(0, D3, 0, 2)[:], h0, MULT)
+        copy_half(1, D3, 0, ones[D3][:, first], 5)
+        scatter(0, first)
+        weighted = slot("weighted0", [P, BANK], F32)
+        bank = signature(0, D1, 1, 6)
+        for at in (0, HEAD):
+            nc.vector.tensor_tensor(weighted[:, at:at + HEAD], bank[:, at:at + HEAD], wg[:, BANK + at:BANK + at + HEAD], MULT)
+        multiply(joint[1][:, first], slot("woven3a", [P, BANK], F32)[:], slot("v_half", [P, BANK], F32)[:],
+                 ones[D1][:, first], wg[:, first], ones[D2][:, first], ones[D3][:, first])
         woven3b = weave(slot("woven3b", [P, HEAD, PACK], BF16)[:], raw3b[:])
-        join_half(D2, 1, slot("raw3c", [P, BANK], F32)[:], 1, h1)
-        joint[1] = h1
-        codes3 = slot("raw3c", [P, HEAD + K], U32)
-        quantise_w3(woven3b, 2, 2, codes3[:, 0:HEAD])
-        quantise_w3(woven3c[:], PACK, PACK, codes3[:, HEAD:HEAD + K])
+        zeros = {which: copy_half(0, which, 1, slot(tag, [P, BANK], F32)[:], n)
+                 for which, tag, n in ((D3, "d3_0", 3), (D2, "raw3b", 5))}
+        scatter(1, first)
+        u = slot("woven3a", [P, BANK], F32)
+        nc.gpsimd.tensor_tensor(u[:], zeros[D2], zeros[D3], MULT)
+        nc.gpsimd.tensor_tensor(joint[0][:, second], u[:], weighted[:], MULT)
+        for which, n in ((D1, 5), (D2, 2)):
+            copy_half(1, which, 1, ones[which][:, second], n)
+        quantise_w3(woven3b, 2, 2, "woven3a")
+        scatter(0, second)
+        pair = slot("woven3b", [P, 2, BANK], F32)
+        copy_half(1, D3, 1, pair[:, 1, :], 7)
+        multiply(joint[1][:, second], pair[:, 0, :], slot("h2", [P, BANK], F32)[:],
+                 ones[D1][:, second], ones[D2][:, second], pair[:, 1, :], wg[:, second])
 
         def deal_words():
             dealt[D1] = slot("w1_dealt", [P, PACK, P], U16)
@@ -242,23 +250,34 @@ def tile_list_semijoin_cache_kernel(tc, tab_words, tab_scales, offs, offs2, offs
             nc.scalar.copy(dealt[D2][:].rearrange("k t p -> k p t"), w2c[:].bitcast(U32).rearrange("k (p t) -> k p t", t=PACK))
 
         def join(i):
+            d1 = copy_out(i, D1, slot(D1_TAGS[i], [P, S], F32), 0)
+            d2 = copy_out(i, D2, slot(D2_TAGS[i], [P, S], F32), 2)
+            d3 = slot(D3_TAGS[i], [P, S], F32)
+            v = None
             if i == 2:
-                behind = slot("raw3b", [P, 2, S], F32)
-                d1 = copy_out(i, D1, behind[:, 0, :], 0)
-                d2 = copy_out(i, D2, behind[:, 1, :], 2)
+                v = slot("weighted0", [P, BANK], F32)
+                bank = signature(i, D3, 0, 4)
+                nc.scalar.copy(d3[:, HEAD:BANK], bank[:, HEAD:BANK])
+                nc.vector.tensor_tensor(v[:, 0:HEAD], bank[:, 0:HEAD], wg[:, 0:HEAD], MULT)
+                copy_half(i, D3, 1, d3[:, second], 5)
             else:
-                d1 = copy_out(i, D1, slot("u%d" % (i % 2), [P, S], F32), 0)
-                d2 = copy_out(i, D2, slot("d2_%d" % (i % 2), [P, S], F32), 2)
-            d3 = copy_out(i, D3, slot("d3_%d" % (i % 3), [P, S], F32), 4)
-            u = slot("woven3c", [P, S], F32) if i == 2 else d1
-            nc.gpsimd.tensor_tensor(u[:], d1[:], d2[:], MULT)
+                copy_out(i, D3, d3, 4)
+            u = slot({2: "woven3b", PACK: "raw3a"}[i], [P, S], F32)[:] if i in (2, PACK) else d1
             h = slot("h%d" % (i % 3), [P, S], F32)
+            joint[i] = h
+            nc.gpsimd.tensor_tensor(u, d1, d2, MULT)
             if i == LAST:
-                nc.gpsimd.tensor_tensor(h[:], u[:], d3[:], MULT)
+                nc.gpsimd.tensor_tensor(h[:], u, d3[:], MULT)
+                return
+            weight = wg if i < PACK else wg_dealt[i - PACK]
+            if v is None:
+                v = h
+                nc.gpsimd.tensor_tensor(v[:, first], d3[:, first], weight[:, first], MULT)
             else:
-                nc.gpsimd.tensor_tensor(h[:], d3[:], wg[:] if i < PACK else wg_dealt[i - PACK][:], MULT)
-                nc.gpsimd.tensor_tensor(h[:], u[:], h[:], MULT)
-            joint[i] = h[:]
+                nc.gpsimd.tensor_tensor(v[:, HEAD:BANK], d3[:, HEAD:BANK], weight[:, HEAD:BANK], MULT)
+            nc.gpsimd.tensor_tensor(h[:, second], d3[:, second], weight[:, second], MULT)
+            nc.gpsimd.tensor_tensor(h[:, first], u[:, first], v[:, first], MULT)
+            nc.gpsimd.tensor_tensor(h[:, second], u[:, second], h[:, second], MULT)
 
         squashed = slot("table", [P, PR // P, PACK, P], F32)
         turns = []
@@ -269,15 +288,19 @@ def tile_list_semijoin_cache_kernel(tc, tab_words, tab_scales, offs, offs2, offs
 
         waiting = []
 
-        def fetch(i, cols, x):
+        def gather(i, cols, x):
             nc.vector.tensor_copy(x, pages[i % 2][:].indirect(entries(idx3, cols)))
+
+        def fetch(i, cols, x):
+            gather(i, cols, x)
             if i >= PACK:
                 waiting.append((i, cols, x))
             else:
-                squash_turned(i, cols, x, turn_bank([P, PACK, P]))
+                for at in range(0, cols.stop - cols.start, BANK):
+                    squash_turned(i, slice(cols.start + at, cols.start + at + BANK), x[:, at:at + BANK], turn_bank([P, PACK, P]))
 
         def squash_turned(i, cols, x, bank):
-            for n, src in enumerate((priors[i][:, cols], x)):
+            for n, src in enumerate((x, priors[i][:, cols])):
                 for k in range(PACK):
                     nc.tensor.matmul(bank[:, k, :], src[:, k * P:(k + 1) * P], ident[:], is_transpose=True,
                                      start=n == 0 and k == 0, stop=n == 1 and k == PACK - 1)
@@ -294,33 +317,39 @@ def tile_list_semijoin_cache_kernel(tc, tab_words, tab_scales, offs, offs2, offs
             return weave(slot("z0_woven%d" % half, [P, BANK, PACK], BF16)[:], planes[:])
 
         join(2)
-        squash_turned(0, half_cols(0), x0[:], bank_tile(5, [P, PACK, P]))
+        woven3c = slot("raw3a", [P, K, PACK], BF16)
+        nc.scalar.copy(woven3c[:].rearrange("k (t p) j -> k p t j", t=PACK), raw3c[:].rearrange("k j (p t) -> k p t j", t=PACK))
         deal_words()
+        fetch(0, first, slot("table_scales", [P, BANK], F32)[:])
+        scatter(1, second)
+        x = slot("d2_0", [P, BANK + PR], F32)
         join(3)
-        w4_woven = slot("w4_woven", [P, 2, N, PACK], BF16)
+        fetch(0, second, x[:, 0:BANK])
+        fetch(1, slice(0, PR), x[:, BANK:BANK + PR])
         z0_woven = []
-        z1_woven = None
-        for i in range(1, LAST):
+        for i in range(2, LAST):
             scatter(i)
-            if i + 3 <= LAST:
-                join(i + 3)
-            if i < LAST - 1:
-                ahead = EARLY_FETCH if i == LAST - 2 else BANK
-                x = slot("d3_%d" % ((i + 1) % 3), [P, BANK + ahead], F32)
-                fetch(i - 1, half_cols(1), x[:, 0:BANK])
+            ahead = EARLY_FETCH if i == LAST - 2 else BANK
+            x = slot(D3_TAGS[i + 1], [P, BANK + ahead], F32) if i < LAST - 1 else None
+            if i == 2:
+                gather(i, first, x[:, 0:BANK])
+                quantise_w3(woven3c[:], PACK, PACK, "d1_0")
+                join(i + 2)
+                squash_turned(i, first, x[:, 0:BANK], turn_bank([P, PACK, P]))
+            elif i < LAST - 1:
+                join(i + 2)
+                fetch(i - 1, second, x[:, 0:BANK])
                 if i == PACK:
                     z0_woven.append(weave_z0(1))
                 fetch(i, slice(0, ahead), x[:, BANK:BANK + ahead])
-            if i + 3 <= LAST:
-                load_prior(i + 3)
-            if i in (1, 2):
-                weave(w4_woven[:, i - 1, :, :], raw4[i - 1][:])
-            if i == 2:
-                z1_woven = slot("z1_woven", [P, PR, PACK], BF16)
+            if i + 2 <= LAST:
+                load_prior(i + 2)
             if i == PACK - 1:
                 z0_woven.append(weave_z0(0))
 
-        z1_planes = slot("raw3b", [P, PACK - 1, PR], BF16)
+        w4_woven = [weave(slot("v_words%d" % b, [P, N, PACK], BF16)[:], raw4[b][:]) for b in range(2)]
+        z1_woven = slot("z1_woven", [P, PR, PACK], BF16)
+        z1_planes = slot("raw3c", [P, PACK - 1, PR], BF16)
 
         def bend(i, cols, y, bent):
             t = i - PACK
@@ -334,22 +363,22 @@ def tile_list_semijoin_cache_kernel(tc, tab_words, tab_scales, offs, offs2, offs
             nc.gpsimd.tensor_tensor(y, x, priors[i][:, cols], ADD)
             bend(i, cols, y, bent)
 
-        sums = slot("u%d" % (LAST % 2), [P, 3, EARLY_FETCH], F32)
-        bent = slot("planes1", [P, 2, EARLY_FETCH], F32)
+        sums = slot("raw3a", [P, 3, BANK], F32)
+        bent = slot("planes1", [P, 2, BANK], F32)
         for n, (i, cols, x) in enumerate(waiting):
             width = cols.stop - cols.start
             squash_dealt(i, cols, x, sums[:, n, 0:width], bent[:, n % 2, 0:width])
         waiting.clear()
-        x = slot("d3_0", [P, PR + HEAD], F32)
-        bent = slot("planes1", [P, 2, BANK], F32)
-        late = [(LAST - 2, slice(EARLY_FETCH, PR), x[:, PR:PR + HEAD])] + [(LAST - 1, half_cols(half), x[:, half_cols(half)]) for half in range(2)]
+        x = slot("d3_0", [P, 2 * PR - EARLY_FETCH], F32)
+        bent = slot("planes1", [P, 2, PR - EARLY_FETCH], F32)
+        late = [(LAST - 2, slice(EARLY_FETCH, PR), x[:, PR:2 * PR - EARLY_FETCH])] + [(LAST - 1, half_cols(half), x[:, half_cols(half)]) for half in range(2)]
         for i, cols, y in late:
             nc.vector.tensor_tensor(y, pages[i % 2][:].indirect(entries(idx3, cols)), priors[i][:, cols], ADD)
         codes = slot("prior%d" % ((LAST - 2) % PRIOR_BUFFERS), [P, 2 * N + 128], U32)
         z0 = {(0, 128): quantise(z0_woven[0][:, 0:128, :], codes[:, 2 * N:2 * N + 128], slot("z0_scales0", [P, 128], U8)[:])}
         w4_scales = slot("w4_scales", [P, 2 * N], U8)
-        w4q = [quantise(w4_woven[:, 0, :, :], codes[:, 0:N], w4_scales[:, 0:N])]
-        w4q.append(quantise(w4_woven[:, 1, :, :], codes[:, N:2 * N], w4_scales[:, N:2 * N]))
+        w4q = [quantise(w4_woven[0], codes[:, 0:N], w4_scales[:, 0:N])]
+        w4q.append(quantise(w4_woven[1], codes[:, N:2 * N], w4_scales[:, N:2 * N]))
         for n, (i, cols, y) in enumerate(late):
             bend(i, cols, y, bent[:, n % 2, 0:cols.stop - cols.start])
         def quantise_z0(cols, tag):

@@ -36,7 +36,7 @@ STORE_BANKS = (1, 1, 1, 1)
 SCALAR_GAINS = (1,)
 D1, D2, D3 = 0, 1, 2
 D3_TAGS = {2: "d3_2", 3: "d3_2", 4: "d3_0", 5: "d3_2", 6: "d3_0", 7: "d3_1"}
-D2_TAGS = {2: "d2_0", 3: "raw3c", 4: "d2_1", 5: "raw3c", 6: "d2_1", 7: "d2_0"}
+D2_TAGS = {2: "d2_0", 3: "d2_1", 4: "raw3c", 5: "d2_1", 6: "raw3c", 7: "d2_0"}
 D1_TAGS = {2: "d1_0", 3: "d1_0", 4: "d1_1", 5: "d1_1", 6: "woven3b", 7: "raw3a"}
 
 
@@ -87,17 +87,18 @@ def tile_list_semijoin_cache_kernel(tc, tab_words, tab_scales, offs, offs2, offs
         nc.sync.dma_start(table[:, 0:TABLE_FIRST], table_i32[:, 0:TABLE_FIRST])
         nc.sync.dma_start(idx[:], offs)
         load_scales(nc.sync, table_scales[:], tab_scales, 0)
+        w1a = load("w1a", [P, HEAD // 2], I32, w1_i32[:, 0:HEAD // 2])
         nc.sync.dma_start(table[:, TABLE_FIRST:T], table_i32[:, TABLE_FIRST:T])
         load_scales(nc.gpsimd, w_scales[:, D2, :], w2_scales, W2_ROWS)
-        w1a = load("w1a", [P, HEAD // 2], I32, w1_i32[:, 0:HEAD // 2])
         load_scales(nc.sync, w_scales[:, D1, :], w1_scales, 0)
-        w2a = load("w2a", [P, HEAD], I32, w2_i32[:, 0:HEAD])
         raw3a = load("raw3a", [P, PACK, HEAD], F32, w3_rows[:, :, 0:HEAD])
         wg = slot("wg", [P, S], F32)
         nc.sync.dma_start(wg[:, half_cols(0)], wgs[:, half_cols(0)])
+        w2a = load("w2a", [P, HEAD], I32, w2_i32[:, 0:HEAD])
         nc.sync.dma_start(wg[:, half_cols(1)], wgs[:, half_cols(1)])
         nc.sync.dma_start(idx2[:], offs2)
         raw3b = load("raw3b", [P, PACK, HEAD], F32, w3_rows[:, :, HEAD:K])
+        raw3c = load("raw3c", [P, PACK, K], F32, w3_rows[:, :, K:H])
         w1b = load("w1b", [P, HEAD // 2], I32, w1_i32[:, HEAD // 2:K // 2])
         w2b = load("w2b", [P, HEAD], I32, w2_i32[:, HEAD:K])
         nc.sync.dma_start(idx3[:], offs3)
@@ -108,7 +109,6 @@ def tile_list_semijoin_cache_kernel(tc, tab_words, tab_scales, offs, offs2, offs
             rows = prior[i * P:(i + 1) * P, :] if i < PACK else prior[K:H, :].rearrange("(p t) m -> t p m", t=PACK)[i - PACK]
             priors[i] = load("prior%d" % (i % PRIOR_BUFFERS), [P, PR], F32, rows)
 
-        raw3c = load("raw3c", [P, PACK, K], F32, w3_rows[:, :, K:H])
         w1c = load("w1c", [P, K // 2], I32, w1_i32[:, K // 2:K])
         w2c = load("w2c", [P, K], I32, w2_i32[:, K:H])
         wg_dealt = []
@@ -141,7 +141,8 @@ def tile_list_semijoin_cache_kernel(tc, tab_words, tab_scales, offs, offs2, offs
             v_words.append(slot("v_words%d" % half, [P, BANK], U32))
             nc.vector.tensor_copy(v_words[half][:], table[:].bitcast(U32).indirect(entries(idx, half_cols(half))))
         scales_dealt = slot("scales_dealt", [P, 2, PACK, P], U8)
-        nc.vector.tensor_copy(scales_dealt[:], w_scales[:, :, K:H].rearrange("k w (p t) -> k w t p", t=PACK))
+        for which in (D2, D1):
+            nc.gpsimd.tensor_copy(scales_dealt[:, which, :, :], w_scales[:, which, K:H].rearrange("k (p t) -> k t p", t=PACK))
 
         def weave(woven, raw):
             nc.scalar.copy(woven.rearrange("p (c i) t -> p c t i", i=4), raw.rearrange("p t (c i) -> p c t i", i=4))
@@ -210,7 +211,7 @@ def tile_list_semijoin_cache_kernel(tc, tab_words, tab_scales, offs, offs2, offs
         joint[0] = slot("h0", [P, S], F32)
         joint[1] = slot("h1", [P, S], F32)
         woven3a = weave(slot("woven3a", [P, HEAD, PACK], BF16)[:], raw3a[:])
-        behind_weave = slot("raw3a", [P, 2, S], F32)
+        behind_weave = slot("raw3a", [P, 2, BANK], F32)
         ones = [behind_weave[:, D1, :], behind_weave[:, D2, :], slot("d3_1", [P, BANK], F32)]
         h0 = joint[0][:, first]
         nc.vector.tensor_tensor(h0, signature(0, D1, 0, 0)[:], wg[:, first], MULT)
@@ -231,17 +232,21 @@ def tile_list_semijoin_cache_kernel(tc, tab_words, tab_scales, offs, offs2, offs
         zeros = {which: copy_half(0, which, 1, slot(tag, [P, BANK], F32)[:], n)
                  for which, tag, n in ((D3, "d3_0", 3), (D2, "raw3b", 5))}
         scatter(1, first)
+        woven3c = slot("woven3c", [P, K, PACK], BF16)
+        nc.scalar.copy(woven3c[:].rearrange("k (t p) j -> k p t j", t=PACK), raw3c[:].rearrange("k j (p t) -> k p t j", t=PACK))
         u = slot("woven3a", [P, BANK], F32)
         nc.gpsimd.tensor_tensor(u[:], zeros[D2], zeros[D3], MULT)
+        behind_weave = slot("raw3c", [P, 2, S], F32)
+        joint[0] = behind_weave[:, 0, :]
         nc.gpsimd.tensor_tensor(joint[0][:, second], u[:], weighted[:], MULT)
-        for which, n in ((D1, 5), (D2, 2)):
-            copy_half(1, which, 1, ones[which][:, second], n)
+        ones = [copy_half(1, which, 1, behind_weave[:, 1, half_cols(which)], n) for which, n in ((D1, 5), (D2, 2))]
+        quantise_w3(woven3c[:], PACK, PACK, "weighted0")
         quantise_w3(woven3b, 2, 2, "woven3a")
         scatter(0, second)
         pair = slot("woven3b", [P, 2, BANK], F32)
         copy_half(1, D3, 1, pair[:, 1, :], 7)
         multiply(joint[1][:, second], pair[:, 0, :], slot("h2", [P, BANK], F32)[:],
-                 ones[D1][:, second], ones[D2][:, second], pair[:, 1, :], wg[:, second])
+                 ones[D1], ones[D2], pair[:, 1, :], wg[:, second])
 
         def deal_words():
             dealt[D1] = slot("w1_dealt", [P, PACK, P], U16)
@@ -255,7 +260,7 @@ def tile_list_semijoin_cache_kernel(tc, tab_words, tab_scales, offs, offs2, offs
             d3 = slot(D3_TAGS[i], [P, S], F32)
             v = None
             if i == 2:
-                v = slot("weighted0", [P, BANK], F32)
+                v = slot("d3_1", [P, BANK], F32)
                 bank = signature(i, D3, 0, 4)
                 nc.scalar.copy(d3[:, HEAD:BANK], bank[:, HEAD:BANK])
                 nc.vector.tensor_tensor(v[:, 0:HEAD], bank[:, 0:HEAD], wg[:, 0:HEAD], MULT)
@@ -317,8 +322,6 @@ def tile_list_semijoin_cache_kernel(tc, tab_words, tab_scales, offs, offs2, offs
             return weave(slot("z0_woven%d" % half, [P, BANK, PACK], BF16)[:], planes[:])
 
         join(2)
-        woven3c = slot("raw3a", [P, K, PACK], BF16)
-        nc.scalar.copy(woven3c[:].rearrange("k (t p) j -> k p t j", t=PACK), raw3c[:].rearrange("k j (p t) -> k p t j", t=PACK))
         deal_words()
         fetch(0, first, slot("table_scales", [P, BANK], F32)[:])
         scatter(1, second)
@@ -333,7 +336,6 @@ def tile_list_semijoin_cache_kernel(tc, tab_words, tab_scales, offs, offs2, offs
             x = slot(D3_TAGS[i + 1], [P, BANK + ahead], F32) if i < LAST - 1 else None
             if i == 2:
                 gather(i, first, x[:, 0:BANK])
-                quantise_w3(woven3c[:], PACK, PACK, "d1_0")
                 join(i + 2)
                 squash_turned(i, first, x[:, 0:BANK], turn_bank([P, PACK, P]))
             elif i < LAST - 1:

@@ -35,7 +35,7 @@ ON_VECTOR = ((3, 1),)
 STORE_BANKS = (1, 1, 1, 1)
 SCALAR_GAINS = (1,)
 D1, D2, D3 = 0, 1, 2
-D3_TAGS = {2: "d3_2", 3: "d3_2", 4: "d3_0", 5: "d3_2", 6: "d3_0", 7: "d3_1"}
+D3_TAGS = {2: "d3_2", 3: "d3_2", 4: "d3_0", 5: "d3_2", 6: "d3_0", 7: "d3_7"}
 D2_TAGS = {2: "d2_0", 3: "d2_1", 4: "raw3c", 5: "d2_1", 6: "raw3c", 7: "d2_0"}
 D1_TAGS = {2: "d1_0", 3: "d1_0", 4: "d1_1", 5: "d1_1", 6: "woven3b", 7: "raw3a"}
 
@@ -78,6 +78,10 @@ def tile_list_semijoin_cache_kernel(tc, tab_words, tab_scales, offs, offs2, offs
         nc.gpsimd.memset(table_scales[:, 0:T // 2].bitcast(I32), 0)
         nc.vector.memset(table_scales[:, T // 2:T].bitcast(I32), 0)
         nc.vector.memset(w_scales[:, D1, :].bitcast(I32), 0)
+
+        preload = keep.tile([P, 2], F32, name="preload")
+        nc.vector.memset(preload[:, 0:1], 0.0)
+        nc.scalar.activation(preload[:, 1:2], preload[:, 0:1], ACT.Tanh)
 
         w3_rows = w3.rearrange("(p j) c -> p j c", j=PACK)
         w1_i32 = w1_words[0].bitcast(I32)
@@ -140,9 +144,13 @@ def tile_list_semijoin_cache_kernel(tc, tab_words, tab_scales, offs, offs2, offs
         for half in range(2):
             v_words.append(slot("v_words%d" % half, [P, BANK], U32))
             nc.vector.tensor_copy(v_words[half][:], table[:].bitcast(U32).indirect(entries(idx, half_cols(half))))
-        scales_dealt = slot("scales_dealt", [P, 2, PACK, P], U8)
-        for which in (D2, D1):
-            nc.gpsimd.tensor_copy(scales_dealt[:, which, :, :], w_scales[:, which, K:H].rearrange("k (p t) -> k t p", t=PACK))
+        scales_dealt = {}
+
+        def deal_scales(which, tag):
+            scales_dealt[which] = slot(tag, [P, PACK, P], U8)
+            nc.gpsimd.tensor_copy(scales_dealt[which][:], w_scales[:, which, K:H].rearrange("k (p t) -> k t p", t=PACK))
+
+        deal_scales(D1, "w1_scales_dealt")
 
         def weave(woven, raw):
             nc.scalar.copy(woven.rearrange("p (c i) t -> p c t i", i=4), raw.rearrange("p t (c i) -> p c t i", i=4))
@@ -170,8 +178,8 @@ def tile_list_semijoin_cache_kernel(tc, tab_words, tab_scales, offs, offs2, offs
             if i >= PACK:
                 t = i - PACK
                 if which == D1:
-                    return dealt[D1][:, t, :].bitcast(E2M1), scales_dealt[:, D1, t, :]
-                return dealt[D2][:, t, :].bitcast(E4M3), scales_dealt[W2_ROWS:P, D2, t, :]
+                    return dealt[D1][:, t, :].bitcast(E2M1), scales_dealt[D1][:, t, :]
+                return dealt[D2][:, t, :].bitcast(E4M3), scales_dealt[D2][W2_ROWS:P, t, :]
             cols = slice(i * P, (i + 1) * P)
             if which == D1:
                 return (w1a, w1b)[i // 2][:, i % 2 * P // 2:(i % 2 + 1) * P // 2].bitcast(E2M1), w_scales[:, D1, cols]
@@ -322,6 +330,7 @@ def tile_list_semijoin_cache_kernel(tc, tab_words, tab_scales, offs, offs2, offs
             return weave(slot("z0_woven%d" % half, [P, BANK, PACK], BF16)[:], planes[:])
 
         join(2)
+        deal_scales(D2, "d3_1")
         deal_words()
         fetch(0, first, slot("table_scales", [P, BANK], F32)[:])
         scatter(1, second)

@@ -35,8 +35,10 @@ ON_VECTOR = ((3, 1),)
 STORE_BANKS = (1, 1, 1, 1)
 SCALAR_GAINS = (1,)
 D1, D2, D3 = 0, 1, 2
-D3_TAGS = {2: "d3_2", 3: "d3_2", 4: "d3_0", 5: "d3_2", 6: "d3_0", 7: "d3_7"}
+D3_TAGS = {2: "d3_2", 3: "d3_2", 4: "d3_0", 5: "d3_2", 6: "d3_0", 7: "d3_1"}
 D2_TAGS = {2: "d2_0", 3: "d2_1", 4: "raw3c", 5: "d2_1", 6: "raw3c", 7: "d2_0"}
+VECTOR_SHARE = {2: BANK}
+V_TAGS = {2: "d3_1", 4: "woven3b"}
 D1_TAGS = {2: "d1_0", 3: "d1_0", 4: "d1_1", 5: "d1_1", 6: "woven3b", 7: "raw3a"}
 
 
@@ -150,6 +152,7 @@ def tile_list_semijoin_cache_kernel(tc, tab_words, tab_scales, offs, offs2, offs
             scales_dealt[which] = slot(tag, [P, PACK, P], U8)
             nc.gpsimd.tensor_copy(scales_dealt[which][:], w_scales[:, which, K:H].rearrange("k (p t) -> k t p", t=PACK))
 
+        deal_scales(D2, "w2_scales_dealt")
         deal_scales(D1, "w1_scales_dealt")
 
         def weave(woven, raw):
@@ -266,12 +269,15 @@ def tile_list_semijoin_cache_kernel(tc, tab_words, tab_scales, offs, offs2, offs
             d1 = copy_out(i, D1, slot(D1_TAGS[i], [P, S], F32), 0)
             d2 = copy_out(i, D2, slot(D2_TAGS[i], [P, S], F32), 2)
             d3 = slot(D3_TAGS[i], [P, S], F32)
+            weight = wg if i < PACK else wg_dealt[i - PACK]
+            done = VECTOR_SHARE.get(i, 0)
             v = None
-            if i == 2:
-                v = slot("d3_1", [P, BANK], F32)
+            if done:
+                v = slot(V_TAGS[i], [P, BANK], F32)
                 bank = signature(i, D3, 0, 4)
-                nc.scalar.copy(d3[:, HEAD:BANK], bank[:, HEAD:BANK])
-                nc.vector.tensor_tensor(v[:, 0:HEAD], bank[:, 0:HEAD], wg[:, 0:HEAD], MULT)
+                if done < BANK:
+                    nc.scalar.copy(d3[:, done:BANK], bank[:, done:BANK])
+                nc.vector.tensor_tensor(v[:, 0:done], bank[:, 0:done], weight[:, 0:done], MULT)
                 copy_half(i, D3, 1, d3[:, second], 5)
             else:
                 copy_out(i, D3, d3, 4)
@@ -282,12 +288,10 @@ def tile_list_semijoin_cache_kernel(tc, tab_words, tab_scales, offs, offs2, offs
             if i == LAST:
                 nc.gpsimd.tensor_tensor(h[:], u, d3[:], MULT)
                 return
-            weight = wg if i < PACK else wg_dealt[i - PACK]
             if v is None:
                 v = h
-                nc.gpsimd.tensor_tensor(v[:, first], d3[:, first], weight[:, first], MULT)
-            else:
-                nc.gpsimd.tensor_tensor(v[:, HEAD:BANK], d3[:, HEAD:BANK], weight[:, HEAD:BANK], MULT)
+            if done < BANK:
+                nc.gpsimd.tensor_tensor(v[:, done:BANK], d3[:, done:BANK], weight[:, done:BANK], MULT)
             nc.gpsimd.tensor_tensor(h[:, second], d3[:, second], weight[:, second], MULT)
             nc.gpsimd.tensor_tensor(h[:, first], u[:, first], v[:, first], MULT)
             nc.gpsimd.tensor_tensor(h[:, second], u[:, second], h[:, second], MULT)
@@ -312,13 +316,29 @@ def tile_list_semijoin_cache_kernel(tc, tab_words, tab_scales, offs, offs2, offs
                 for at in range(0, cols.stop - cols.start, BANK):
                     squash_turned(i, slice(cols.start + at, cols.start + at + BANK), x[:, at:at + BANK], turn_bank([P, PACK, P]))
 
-        def squash_turned(i, cols, x, bank):
-            for n, src in enumerate((x, priors[i][:, cols])):
+        def add_turned(bank, x, y):
+            for n, src in enumerate((x, y)):
                 for k in range(PACK):
                     nc.tensor.matmul(bank[:, k, :], src[:, k * P:(k + 1) * P], ident[:], is_transpose=True,
                                      start=n == 0 and k == 0, stop=n == 1 and k == PACK - 1)
+
+        def squash_turned(i, cols, x, bank):
+            add_turned(bank, x, priors[i][:, cols])
             nc.scalar.activation(squashed[:, cols.start // P:cols.stop // P, :, 32 * i:32 * i + 32],
                                  bank[:].rearrange("m k (p t) -> m k t p", t=PACK), ACT.Tanh)
+
+        def squash_dealt_turned(i, cols, x):
+            bank = turn_bank([P, PACK, P])
+            add_turned(bank, x, priors[i][:, cols])
+            bent = slot("bent", [P, PACK, P], F32)
+            nc.scalar.activation(bent[:], bank[:], ACT.Tanh)
+            for n in range(2):
+                bank = bank_tile(n, [P, 2, P])
+                for k in range(2):
+                    nc.tensor.transpose(bank[:, k, :], bent[:, 2 * n + k, :], ident[:])
+                at = cols.start + n * HEAD
+                nc.scalar.activation(z1_planes[:, i - PACK, at:at + HEAD], bank[:].rearrange("p k m -> p (k m)"), ACT.Copy,
+                                     scale=gains[:, 1, i - PACK:i - PACK + 1])
 
         def weave_z0(half):
             planes = slot("planes%d" % half, [P, PACK, BANK], BF16)
@@ -330,7 +350,6 @@ def tile_list_semijoin_cache_kernel(tc, tab_words, tab_scales, offs, offs2, offs
             return weave(slot("z0_woven%d" % half, [P, BANK, PACK], BF16)[:], planes[:])
 
         join(2)
-        deal_scales(D2, "d3_1")
         deal_words()
         fetch(0, first, slot("table_scales", [P, BANK], F32)[:])
         scatter(1, second)
@@ -339,6 +358,7 @@ def tile_list_semijoin_cache_kernel(tc, tab_words, tab_scales, offs, offs2, offs
         fetch(0, second, x[:, 0:BANK])
         fetch(1, slice(0, PR), x[:, BANK:BANK + PR])
         z0_woven = []
+        z1_planes = slot("z1_planes", [P, PACK - 1, PR], BF16)
         for i in range(2, LAST):
             scatter(i)
             ahead = EARLY_FETCH if i == LAST - 2 else BANK
@@ -349,6 +369,8 @@ def tile_list_semijoin_cache_kernel(tc, tab_words, tab_scales, offs, offs2, offs
                 squash_turned(i, first, x[:, 0:BANK], turn_bank([P, PACK, P]))
             elif i < LAST - 1:
                 join(i + 2)
+                if i + 2 == LAST:
+                    squash_dealt_turned(*waiting.pop())
                 fetch(i - 1, second, x[:, 0:BANK])
                 if i == PACK:
                     z0_woven.append(weave_z0(1))
@@ -360,7 +382,6 @@ def tile_list_semijoin_cache_kernel(tc, tab_words, tab_scales, offs, offs2, offs
 
         w4_woven = [weave(slot("v_words%d" % b, [P, N, PACK], BF16)[:], raw4[b][:]) for b in range(2)]
         z1_woven = slot("z1_woven", [P, PR, PACK], BF16)
-        z1_planes = slot("raw3c", [P, PACK - 1, PR], BF16)
 
         def bend(i, cols, y, bent):
             t = i - PACK

@@ -37,8 +37,8 @@ SCALAR_GAINS = (1,)
 D1, D2, D3 = 0, 1, 2
 D3_TAGS = {2: "d3_2", 3: "d3_2", 4: "d3_0", 5: "d3_2", 6: "d3_0", 7: "d3_1"}
 D2_TAGS = {2: "d2_0", 3: "d2_1", 4: "raw3c", 5: "d2_1", 6: "raw3c", 7: "d2_0"}
-VECTOR_SHARE = {2: BANK}
-V_TAGS = {2: "d3_1", 4: "woven3b"}
+VECTOR_SHARE = {3: HEAD}
+V_TAGS = {3: "woven3c"}
 D1_TAGS = {2: "d1_0", 3: "d1_0", 4: "d1_1", 5: "d1_1", 6: "woven3b", 7: "raw3a"}
 
 
@@ -250,14 +250,16 @@ def tile_list_semijoin_cache_kernel(tc, tab_words, tab_scales, offs, offs2, offs
         behind_weave = slot("raw3c", [P, 2, S], F32)
         joint[0] = behind_weave[:, 0, :]
         nc.gpsimd.tensor_tensor(joint[0][:, second], u[:], weighted[:], MULT)
-        ones = [copy_half(1, which, 1, behind_weave[:, 1, half_cols(which)], n) for which, n in ((D1, 5), (D2, 2))]
+        early = {2: [copy_out(2, which, slot(tag, [P, S], F32), 2 * which) for which, tag in ((D1, D1_TAGS[2]), (D2, D2_TAGS[2]))]}
+        ones = [copy_half(1, which, 1, behind_weave[:, 1, half_cols(which)], 2 * which + 1) for which in (D1, D2)]
         quantise_w3(woven3c[:], PACK, PACK, "weighted0")
         quantise_w3(woven3b, 2, 2, "woven3a")
         scatter(0, second)
-        pair = slot("woven3b", [P, 2, BANK], F32)
-        copy_half(1, D3, 1, pair[:, 1, :], 7)
-        multiply(joint[1][:, second], pair[:, 0, :], slot("h2", [P, BANK], F32)[:],
-                 ones[D1], ones[D2], pair[:, 1, :], wg[:, second])
+        weighted = slot("woven3c", [P, BANK], F32)
+        nc.vector.tensor_tensor(weighted[:], signature(1, D3, 1, 7)[:], wg[:, second], MULT)
+        behind_window = slot("woven3b", [P, BANK + S], F32)
+        nc.gpsimd.tensor_tensor(behind_window[:, 0:BANK], ones[D1], ones[D2], MULT)
+        nc.gpsimd.tensor_tensor(joint[1][:, second], behind_window[:, 0:BANK], weighted[:], MULT)
 
         def deal_words():
             dealt[D1] = slot("w1_dealt", [P, PACK, P], U16)
@@ -266,8 +268,7 @@ def tile_list_semijoin_cache_kernel(tc, tab_words, tab_scales, offs, offs2, offs
             nc.scalar.copy(dealt[D2][:].rearrange("k t p -> k p t"), w2c[:].bitcast(U32).rearrange("k (p t) -> k p t", t=PACK))
 
         def join(i):
-            d1 = copy_out(i, D1, slot(D1_TAGS[i], [P, S], F32), 0)
-            d2 = copy_out(i, D2, slot(D2_TAGS[i], [P, S], F32), 2)
+            d1, d2 = early.get(i) or [copy_out(i, which, slot(tags[i], [P, S], F32), 2 * which) for which, tags in ((D1, D1_TAGS), (D2, D2_TAGS))]
             d3 = slot(D3_TAGS[i], [P, S], F32)
             weight = wg if i < PACK else wg_dealt[i - PACK]
             done = VECTOR_SHARE.get(i, 0)
@@ -275,13 +276,15 @@ def tile_list_semijoin_cache_kernel(tc, tab_words, tab_scales, offs, offs2, offs
             if done:
                 v = slot(V_TAGS[i], [P, BANK], F32)
                 bank = signature(i, D3, 0, 4)
-                if done < BANK:
-                    nc.scalar.copy(d3[:, done:BANK], bank[:, done:BANK])
                 nc.vector.tensor_tensor(v[:, 0:done], bank[:, 0:done], weight[:, 0:done], MULT)
+                nc.scalar.copy(d3[:, done:BANK], bank[:, done:BANK])
                 copy_half(i, D3, 1, d3[:, second], 5)
+            elif i == 2:
+                for half in range(2):
+                    copy_half(i, D3, half, d3[:, half_cols(half)], 2 * half + 1)
             else:
                 copy_out(i, D3, d3, 4)
-            u = slot({2: "woven3b", PACK: "raw3a"}[i], [P, S], F32)[:] if i in (2, PACK) else d1
+            u = behind_window[:, BANK:BANK + S] if i == 2 else slot("raw3a", [P, S], F32)[:] if i == PACK else d1
             h = slot("h%d" % (i % 3), [P, S], F32)
             joint[i] = h
             nc.gpsimd.tensor_tensor(u, d1, d2, MULT)
@@ -290,11 +293,11 @@ def tile_list_semijoin_cache_kernel(tc, tab_words, tab_scales, offs, offs2, offs
                 return
             if v is None:
                 v = h
-            if done < BANK:
-                nc.gpsimd.tensor_tensor(v[:, done:BANK], d3[:, done:BANK], weight[:, done:BANK], MULT)
-            nc.gpsimd.tensor_tensor(h[:, second], d3[:, second], weight[:, second], MULT)
-            nc.gpsimd.tensor_tensor(h[:, first], u[:, first], v[:, first], MULT)
-            nc.gpsimd.tensor_tensor(h[:, second], u[:, second], h[:, second], MULT)
+            cut = HEAD if i == 2 else BANK
+            nc.gpsimd.tensor_tensor(v[:, done:cut], d3[:, done:cut], weight[:, done:cut], MULT)
+            nc.gpsimd.tensor_tensor(h[:, cut:S], d3[:, cut:S], weight[:, cut:S], MULT)
+            nc.gpsimd.tensor_tensor(h[:, 0:cut], u[:, 0:cut], v[:, 0:cut], MULT)
+            nc.gpsimd.tensor_tensor(h[:, cut:S], u[:, cut:S], h[:, cut:S], MULT)
 
         squashed = slot("table", [P, PR // P, PACK, P], F32)
         turns = []
@@ -351,12 +354,15 @@ def tile_list_semijoin_cache_kernel(tc, tab_words, tab_scales, offs, offs2, offs
 
         join(2)
         deal_words()
-        fetch(0, first, slot("table_scales", [P, BANK], F32)[:])
+        fetched = [slot("table_scales", [P, PR], F32)]
+        gather(0, slice(0, PR), fetched[0][:])
         scatter(1, second)
-        x = slot("d2_0", [P, BANK + PR], F32)
+        fetched.append(slot("d2_0", [P, PR], F32))
         join(3)
-        fetch(0, second, x[:, 0:BANK])
-        fetch(1, slice(0, PR), x[:, BANK:BANK + PR])
+        gather(1, slice(0, PR), fetched[1][:])
+        for i, x in enumerate(fetched):
+            for half in range(2):
+                squash_turned(i, half_cols(half), x[:, half_cols(half)], bank_tile(4 * i + half, [P, PACK, P]))
         z0_woven = []
         z1_planes = slot("z1_planes", [P, PACK - 1, PR], BF16)
         for i in range(2, LAST):

@@ -28,7 +28,7 @@ TABLE_FIRST = T // 4
 W2_ROWS = 4
 TURN_BANKS = (6, 7)
 PRIOR_BUFFERS = 5
-EARLY_FETCH = HEAD
+EARLY_FETCH = BANK
 CHUNKS = (128, 256, 384, 256)
 BANKS = ((0, 1), (2, 3), (4, 5, 6, 7), (0, 1))
 ON_VECTOR = ((3, 1),)
@@ -293,7 +293,7 @@ def tile_list_semijoin_cache_kernel(tc, tab_words, tab_scales, offs, offs2, offs
                 return
             if v is None:
                 v = h
-            cut = HEAD if i == 2 else BANK
+            cut = P if i == 2 else BANK
             nc.gpsimd.tensor_tensor(v[:, done:cut], d3[:, done:cut], weight[:, done:cut], MULT)
             nc.gpsimd.tensor_tensor(h[:, cut:S], d3[:, cut:S], weight[:, cut:S], MULT)
             nc.gpsimd.tensor_tensor(h[:, 0:cut], u[:, 0:cut], v[:, 0:cut], MULT)

@@ -28,7 +28,7 @@ TABLE_FIRST = T // 4
 W2_ROWS = 4
 TURN_BANKS = (6, 7)
 PRIOR_BUFFERS = 5
-EARLY_FETCH = BANK
+EARLY_FETCH = HEAD
 CHUNKS = (128, 256, 384, 256)
 BANKS = ((0, 1), (2, 3), (4, 5, 6, 7), (0, 1))
 ON_VECTOR = ((3, 1),)
@@ -381,6 +381,8 @@ def tile_list_semijoin_cache_kernel(tc, tab_words, tab_scales, offs, offs2, offs
                 if i == PACK:
                     z0_woven.append(weave_z0(1))
                 fetch(i, slice(0, ahead), x[:, BANK:BANK + ahead])
+                if i + 2 == LAST:
+                    squash_dealt_turned(*waiting.pop(0))
             if i + 2 <= LAST:
                 load_prior(i + 2)
             if i == PACK - 1:

@@ -20,9 +20,11 @@ ACT = mybir.ActivationFunctionType
 
 P = 128
 PACK = 4
+QUADRANT = 32
+SCALE_ROWS = K // 32
+GROUP = 16
 BANK = 512
-TILES = H // P
-LAST = TILES - 1
+LAST = H // P - 1
 HEAD = 2 * P
 TABLE_FIRST = T // 4
 W2_ROWS = 4
@@ -31,15 +33,12 @@ PRIOR_BUFFERS = 5
 EARLY_FETCH = HEAD
 CHUNKS = (128, 256, 384, 256)
 BANKS = ((0, 1), (2, 3), (4, 5, 6, 7), (0, 1))
-ON_VECTOR = ((3, 1),)
-STORE_BANKS = (1, 1, 1, 1)
-SCALAR_GAINS = (1,)
+ON_VECTOR = (3, 1)
+SCALAR_GAINS = (0, 1)
 D1, D2, D3 = 0, 1, 2
-D3_TAGS = {2: "d3_2", 3: "d3_2", 4: "d3_0", 5: "d3_2", 6: "d3_0", 7: "d3_1"}
-D2_TAGS = {2: "d2_0", 3: "d2_1", 4: "raw3c", 5: "d2_1", 6: "raw3c", 7: "d2_0"}
-VECTOR_SHARE = {3: HEAD}
-V_TAGS = {3: "woven3c"}
 D1_TAGS = {2: "d1_0", 3: "d1_0", 4: "d1_1", 5: "d1_1", 6: "woven3b", 7: "raw3a"}
+D2_TAGS = {2: "d2_0", 3: "d2_1", 4: "raw3c", 5: "d2_1", 6: "raw3c", 7: "d2_0"}
+D3_TAGS = {2: "d3_2", 3: "d3_2", 4: "d3_0", 5: "d3_2", 6: "d3_0", 7: "d3_1"}
 
 
 def tile_list_semijoin_cache_kernel(tc, tab_words, tab_scales, offs, offs2, offs3, w1_words, w1_scales,
@@ -59,7 +58,7 @@ def tile_list_semijoin_cache_kernel(tc, tab_words, tab_scales, offs, offs2, offs
             return slice(half * BANK, (half + 1) * BANK)
 
         def entries(offsets, cols):
-            return offsets[:, cols.start // 16:cols.stop // 16]
+            return offsets[:, cols.start // GROUP:cols.stop // GROUP]
 
         def load(tag, shape, dtype, src):
             dst = slot(tag, shape, dtype)
@@ -67,12 +66,12 @@ def tile_list_semijoin_cache_kernel(tc, tab_words, tab_scales, offs, offs2, offs
             return dst
 
         def load_scales(queue, plane, rows, first):
-            for r in range(4):
-                queue.dma_start(plane[first + r:P:32, :].bitcast(I32), rows[0, r:16:4, :].bitcast(I32))
+            for r in range(PACK):
+                queue.dma_start(plane[first + r:P:QUADRANT, :].bitcast(I32), rows[0, r:SCALE_ROWS:PACK, :].bitcast(I32))
 
-        idx = keep.tile([P, S // 16], U16, name="idx")
-        idx2 = keep.tile([P, S // 16], U16, name="idx2")
-        idx3 = keep.tile([P, PR // 16], U16, name="idx3")
+        idx = keep.tile([P, S // GROUP], U16, name="idx")
+        idx2 = keep.tile([P, S // GROUP], U16, name="idx2")
+        idx3 = keep.tile([P, PR // GROUP], U16, name="idx3")
         table = slot("table", [P, T], I32)
         table_scales = slot("table_scales", [P, T], U8)
         w_scales = slot("w_scales", [P, 2, H], U8)
@@ -122,7 +121,7 @@ def tile_list_semijoin_cache_kernel(tc, tab_words, tab_scales, offs, offs2, offs
         def load_dealt_wgs(t):
             wg_dealt.append(slot("wg_dealt%d" % t, [P, S], F32))
             for a in (0, 2, 1, 3):
-                nc.sync.dma_start(wg_dealt[t][32 * a:32 * a + 32, :], wgs.rearrange("(c t) j -> t c j", t=PACK)[t])
+                nc.sync.dma_start(wg_dealt[t][QUADRANT * a:QUADRANT * (a + 1), :], wgs.rearrange("(c t) j -> t c j", t=PACK)[t])
 
         for t in range(PACK - 1):
             load_prior(t)
@@ -147,13 +146,9 @@ def tile_list_semijoin_cache_kernel(tc, tab_words, tab_scales, offs, offs2, offs
             v_words.append(slot("v_words%d" % half, [P, BANK], U32))
             nc.vector.tensor_copy(v_words[half][:], table[:].bitcast(U32).indirect(entries(idx, half_cols(half))))
         scales_dealt = {}
-
-        def deal_scales(which, tag):
+        for which, tag in ((D2, "w2_scales_dealt"), (D1, "w1_scales_dealt")):
             scales_dealt[which] = slot(tag, [P, PACK, P], U8)
             nc.gpsimd.tensor_copy(scales_dealt[which][:], w_scales[:, which, K:H].rearrange("k (p t) -> k t p", t=PACK))
-
-        deal_scales(D2, "w2_scales_dealt")
-        deal_scales(D1, "w1_scales_dealt")
 
         def weave(woven, raw):
             nc.scalar.copy(woven.rearrange("p (c i) t -> p c t i", i=4), raw.rearrange("p t (c i) -> p c t i", i=4))
@@ -213,11 +208,6 @@ def tile_list_semijoin_cache_kernel(tc, tab_words, tab_scales, offs, offs2, offs
             else:
                 nc.vector.tensor_copy(page, joint[i][:, cols])
 
-        def multiply(h, u, v, a, b, c, d):
-            nc.gpsimd.tensor_tensor(u, a, b, MULT)
-            nc.gpsimd.tensor_tensor(v, c, d, MULT)
-            nc.gpsimd.tensor_tensor(h, u, v, MULT)
-
         first, second = half_cols(0), half_cols(1)
         joint[0] = slot("h0", [P, S], F32)
         joint[1] = slot("h1", [P, S], F32)
@@ -237,29 +227,32 @@ def tile_list_semijoin_cache_kernel(tc, tab_words, tab_scales, offs, offs2, offs
         bank = signature(0, D1, 1, 6)
         for at in (0, HEAD):
             nc.vector.tensor_tensor(weighted[:, at:at + HEAD], bank[:, at:at + HEAD], wg[:, BANK + at:BANK + at + HEAD], MULT)
-        multiply(joint[1][:, first], slot("woven3a", [P, BANK], F32)[:], slot("v_half", [P, BANK], F32)[:],
-                 ones[D1][:, first], wg[:, first], ones[D2][:, first], ones[D3][:, first])
+        u = slot("woven3a", [P, BANK], F32)
+        v = slot("v_half", [P, BANK], F32)
+        nc.gpsimd.tensor_tensor(u[:], ones[D1][:, first], wg[:, first], MULT)
+        nc.gpsimd.tensor_tensor(v[:], ones[D2][:, first], ones[D3][:, first], MULT)
+        nc.gpsimd.tensor_tensor(joint[1][:, first], u[:], v[:], MULT)
         woven3b = weave(slot("woven3b", [P, HEAD, PACK], BF16)[:], raw3b[:])
         zeros = {which: copy_half(0, which, 1, slot(tag, [P, BANK], F32)[:], n)
-                 for which, tag, n in ((D3, "d3_0", 3), (D2, "raw3b", 5))}
+                 for which, tag, n in ((D3, "d3_0", 3), (D2, "d2_0", 5))}
         scatter(1, first)
         woven3c = slot("woven3c", [P, K, PACK], BF16)
-        nc.scalar.copy(woven3c[:].rearrange("k (t p) j -> k p t j", t=PACK), raw3c[:].rearrange("k j (p t) -> k p t j", t=PACK))
+        nc.scalar.copy(woven3c[:].rearrange("k (t p) j -> k p j t", t=PACK), raw3c[:].rearrange("k j (p t) -> k p j t", t=PACK))
         u = slot("woven3a", [P, BANK], F32)
         nc.gpsimd.tensor_tensor(u[:], zeros[D2], zeros[D3], MULT)
-        behind_weave = slot("raw3c", [P, 2, S], F32)
-        joint[0] = behind_weave[:, 0, :]
+        behind_last_weave = slot("raw3c", [P, 2, S], F32)
+        joint[0] = behind_last_weave[:, 0, :]
         nc.gpsimd.tensor_tensor(joint[0][:, second], u[:], weighted[:], MULT)
-        early = {2: [copy_out(2, which, slot(tag, [P, S], F32), 2 * which) for which, tag in ((D1, D1_TAGS[2]), (D2, D2_TAGS[2]))]}
-        ones = [copy_half(1, which, 1, behind_weave[:, 1, half_cols(which)], 2 * which + 1) for which in (D1, D2)]
+        twos = [copy_out(2, which, slot(tags[2], [P, S], F32), 2 * which) for which, tags in ((D1, D1_TAGS), (D2, D2_TAGS))]
+        late_ones = [copy_half(1, which, 1, behind_last_weave[:, 1, half_cols(which)], 2 * which + 1) for which in (D1, D2)]
         quantise_w3(woven3c[:], PACK, PACK, "weighted0")
         quantise_w3(woven3b, 2, 2, "woven3a")
         scatter(0, second)
-        weighted = slot("woven3c", [P, BANK], F32)
-        nc.vector.tensor_tensor(weighted[:], signature(1, D3, 1, 7)[:], wg[:, second], MULT)
+        weighted_one = slot("woven3c", [P, BANK], F32)
+        nc.vector.tensor_tensor(weighted_one[:], signature(1, D3, 1, 7)[:], wg[:, second], MULT)
         behind_window = slot("woven3b", [P, BANK + S], F32)
-        nc.gpsimd.tensor_tensor(behind_window[:, 0:BANK], ones[D1], ones[D2], MULT)
-        nc.gpsimd.tensor_tensor(joint[1][:, second], behind_window[:, 0:BANK], weighted[:], MULT)
+        nc.gpsimd.tensor_tensor(behind_window[:, 0:BANK], late_ones[D1], late_ones[D2], MULT)
+        nc.gpsimd.tensor_tensor(joint[1][:, second], behind_window[:, 0:BANK], weighted_one[:], MULT)
 
         def deal_words():
             dealt[D1] = slot("w1_dealt", [P, PACK, P], U16)
@@ -268,20 +261,21 @@ def tile_list_semijoin_cache_kernel(tc, tab_words, tab_scales, offs, offs2, offs
             nc.scalar.copy(dealt[D2][:].rearrange("k t p -> k p t"), w2c[:].bitcast(U32).rearrange("k (p t) -> k p t", t=PACK))
 
         def join(i):
-            d1, d2 = early.get(i) or [copy_out(i, which, slot(tags[i], [P, S], F32), 2 * which) for which, tags in ((D1, D1_TAGS), (D2, D2_TAGS))]
+            d1, d2 = twos if i == 2 else [copy_out(i, which, slot(tags[i], [P, S], F32), 2 * which)
+                                          for which, tags in ((D1, D1_TAGS), (D2, D2_TAGS))]
             d3 = slot(D3_TAGS[i], [P, S], F32)
             weight = wg if i < PACK else wg_dealt[i - PACK]
-            done = VECTOR_SHARE.get(i, 0)
-            v = None
-            if done:
-                v = slot(V_TAGS[i], [P, BANK], F32)
+            done = 0
+            if i == 2:
+                for half in range(2):
+                    copy_half(i, D3, half, d3[:, half_cols(half)], 2 * half + 1)
+            elif i == 3:
+                done = HEAD
+                v = slot("woven3c", [P, BANK], F32)
                 bank = signature(i, D3, 0, 4)
                 nc.vector.tensor_tensor(v[:, 0:done], bank[:, 0:done], weight[:, 0:done], MULT)
                 nc.scalar.copy(d3[:, done:BANK], bank[:, done:BANK])
                 copy_half(i, D3, 1, d3[:, second], 5)
-            elif i == 2:
-                for half in range(2):
-                    copy_half(i, D3, half, d3[:, half_cols(half)], 2 * half + 1)
             else:
                 copy_out(i, D3, d3, 4)
             u = behind_window[:, BANK:BANK + S] if i == 2 else slot("raw3a", [P, S], F32)[:] if i == PACK else d1
@@ -291,7 +285,7 @@ def tile_list_semijoin_cache_kernel(tc, tab_words, tab_scales, offs, offs2, offs
             if i == LAST:
                 nc.gpsimd.tensor_tensor(h[:], u, d3[:], MULT)
                 return
-            if v is None:
+            if not done:
                 v = h
             cut = P if i == 2 else BANK
             nc.gpsimd.tensor_tensor(v[:, done:cut], d3[:, done:cut], weight[:, done:cut], MULT)
@@ -316,8 +310,7 @@ def tile_list_semijoin_cache_kernel(tc, tab_words, tab_scales, offs, offs2, offs
             if i >= PACK:
                 waiting.append((i, cols, x))
             else:
-                for at in range(0, cols.stop - cols.start, BANK):
-                    squash_turned(i, slice(cols.start + at, cols.start + at + BANK), x[:, at:at + BANK], turn_bank([P, PACK, P]))
+                squash_turned(i, cols, x, turn_bank([P, PACK, P]))
 
         def add_turned(bank, x, y):
             for n, src in enumerate((x, y)):
@@ -327,7 +320,7 @@ def tile_list_semijoin_cache_kernel(tc, tab_words, tab_scales, offs, offs2, offs
 
         def squash_turned(i, cols, x, bank):
             add_turned(bank, x, priors[i][:, cols])
-            nc.scalar.activation(squashed[:, cols.start // P:cols.stop // P, :, 32 * i:32 * i + 32],
+            nc.scalar.activation(squashed[:, cols.start // P:cols.stop // P, :, QUADRANT * i:QUADRANT * (i + 1)],
                                  bank[:].rearrange("m k (p t) -> m k t p", t=PACK), ACT.Tanh)
 
         def squash_dealt_turned(i, cols, x):
@@ -399,28 +392,23 @@ def tile_list_semijoin_cache_kernel(tc, tab_words, tab_scales, offs, offs2, offs
                 nc.scalar.copy(z1_woven[:, cols, 0:PACK - 1].rearrange("p (c i) t -> p c t i", i=4),
                                z1_planes[:, :, cols].rearrange("p t (c i) -> p c t i", i=4))
 
-        def squash_dealt(i, cols, x, y, bent):
-            nc.gpsimd.tensor_tensor(y, x, priors[i][:, cols], ADD)
-            bend(i, cols, y, bent)
-
+        i, cols, x = waiting.pop()
         sums = slot("raw3a", [P, 3, BANK], F32)
         bent = slot("planes1", [P, 2, BANK], F32)
-        for n, (i, cols, x) in enumerate(waiting):
-            width = cols.stop - cols.start
-            squash_dealt(i, cols, x, sums[:, n, 0:width], bent[:, n % 2, 0:width])
-        waiting.clear()
+        nc.gpsimd.tensor_tensor(sums[:, 0, cols], x, priors[i][:, cols], ADD)
+        bend(i, cols, sums[:, 0, cols], bent[:, 0, cols])
         x = slot("d3_0", [P, 2 * PR - EARLY_FETCH], F32)
         bent = slot("planes1", [P, 2, PR - EARLY_FETCH], F32)
-        late = [(LAST - 2, slice(EARLY_FETCH, PR), x[:, PR:2 * PR - EARLY_FETCH])] + [(LAST - 1, half_cols(half), x[:, half_cols(half)]) for half in range(2)]
+        late = [(LAST - 2, slice(EARLY_FETCH, PR), x[:, PR:2 * PR - EARLY_FETCH])]
+        late.extend((LAST - 1, half_cols(half), x[:, half_cols(half)]) for half in range(2))
         for i, cols, y in late:
             nc.vector.tensor_tensor(y, pages[i % 2][:].indirect(entries(idx3, cols)), priors[i][:, cols], ADD)
-        codes = slot("prior%d" % ((LAST - 2) % PRIOR_BUFFERS), [P, 2 * N + 128], U32)
-        z0 = {(0, 128): quantise(z0_woven[0][:, 0:128, :], codes[:, 2 * N:2 * N + 128], slot("z0_scales0", [P, 128], U8)[:])}
-        w4_scales = slot("w4_scales", [P, 2 * N], U8)
-        w4q = [quantise(w4_woven[0], codes[:, 0:N], w4_scales[:, 0:N])]
-        w4q.append(quantise(w4_woven[1], codes[:, N:2 * N], w4_scales[:, N:2 * N]))
         for n, (i, cols, y) in enumerate(late):
             bend(i, cols, y, bent[:, n % 2, 0:cols.stop - cols.start])
+
+        z0 = {}
+        w4q = []
+
         def quantise_z0(cols, tag):
             mine = slice(cols.start % BANK, (cols.stop - 1) % BANK + 1)
             width = cols.stop - cols.start
@@ -436,13 +424,12 @@ def tile_list_semijoin_cache_kernel(tc, tab_words, tab_scales, offs, offs2, offs
             if b == 1:
                 steps = [(part, n) for n in range(N // P) for part in range(len(pieces))]
             for part, n in steps:
-                if True:
-                    at, z_codes, z_scales = pieces[part]
-                    cols = slice(n * P, (n + 1) * P)
-                    nc.tensor.matmul_mx(out=banks[n // per_bank][:, n % per_bank, at], lhsT=w_codes[:, cols].bitcast(E4M3),
-                                        lhsT_scale=w_scales4[:, cols], rhs=z_codes.bitcast(E4M3), rhs_scale=z_scales,
-                                        start=b == 0 and part == 0 and n % per_bank == 0,
-                                        stop=b == 1 and part == len(pieces) - 1 and n % per_bank == per_bank - 1)
+                at, z_codes, z_scales = pieces[part]
+                cols = slice(n * P, (n + 1) * P)
+                nc.tensor.matmul_mx(out=banks[n // per_bank][:, n % per_bank, at], lhsT=w_codes[:, cols].bitcast(E4M3),
+                                    lhsT_scale=w_scales4[:, cols], rhs=z_codes.bitcast(E4M3), rhs_scale=z_scales,
+                                    start=b == 0 and part == 0 and n % per_bank == 0,
+                                    stop=b == 1 and part == len(pieces) - 1 and n % per_bank == per_bank - 1)
 
         opened = {}
 
@@ -450,29 +437,25 @@ def tile_list_semijoin_cache_kernel(tc, tab_words, tab_scales, offs, offs2, offs
             cols = chunks[c]
             opened[c] = [bank_tile(n, [P, N // P // len(BANKS[c]), CHUNKS[c]]) for n in BANKS[c]]
             pieces = []
-            for (first, stop), (z_codes, z_scales) in z0.items():
-                lo, hi = max(cols.start, first), min(cols.stop, stop)
-                while lo < hi:
-                    end = lo + HEAD if hi - lo == HEAD + P else hi
-                    mine = slice(lo - first, end - first)
-                    pieces.append((slice(lo - cols.start, end - cols.start), z_codes[:, mine], z_scales[:, mine]))
-                    lo = end
+            for (start, stop), (z_codes, z_scales) in z0.items():
+                if cols.start <= start and stop <= cols.stop:
+                    pieces.append((slice(start - cols.start, stop - cols.start), z_codes, z_scales))
             estimate_pass(0, opened[c], pieces)
 
         res = slot("table", [P, N // P * PR], F32)
         squash = {}
-        fetched = {}
+        probed = {}
         x_tail = slot("planes1", [P, 2, max(CHUNKS)], F32)
 
         def tail_fetch(c):
             cols = chunks[c]
             x = x_tail[:, c % 2, 0:CHUNKS[c]]
             nc.vector.tensor_tensor(x, pages[LAST % 2][:].indirect(entries(idx3, cols)), priors[LAST][:, cols], ADD)
-            fetched[c] = x
+            probed[c] = x
 
         def tail_tanh(c):
             squash[c] = slot("tz%d" % c, [P, CHUNKS[c]], F32)
-            nc.scalar.activation(squash[c][:], fetched[c], ACT.Tanh)
+            nc.scalar.activation(squash[c][:], probed[c], ACT.Tanh)
 
         def tail_gain(c):
             if c in SCALAR_GAINS:
@@ -484,48 +467,49 @@ def tile_list_semijoin_cache_kernel(tc, tab_words, tab_scales, offs, offs2, offs
             cols = chunks[c]
             z_codes, z_scales = quantise(z1_woven[:, cols, :], slot("z1_codes%d" % c, [P, CHUNKS[c]], U32)[:],
                                          slot("z1_scales%d" % c, [P, CHUNKS[c]], U8)[:])
-            cuts = [slice(0, HEAD), slice(HEAD, CHUNKS[c])] if CHUNKS[c] > HEAD and CHUNKS[c] < BANK else [slice(0, CHUNKS[c])]
+            cuts = [slice(0, HEAD), slice(HEAD, CHUNKS[c])] if CHUNKS[c] > HEAD else [slice(0, CHUNKS[c])]
             estimate_pass(1, opened[c], [(at, z_codes[:, at], z_scales[:, at]) for at in cuts])
 
-        def tail_store(c, only=None):
+        def tail_store(c):
             cols = chunks[c]
-            staged_all = res[:, N // P * cols.start:N // P * cols.stop].rearrange("p (k m) -> p k m", m=CHUNKS[c])
+            staged = res[:, N // P * cols.start:N // P * cols.stop].rearrange("p (k m) -> p k m", m=CHUNKS[c])
+            blocks = N // P // len(opened[c])
             for n, bank in enumerate(opened[c]):
-                if only is not None and n != only:
-                    continue
-                rows = N // len(opened[c])
-                staged = staged_all[:, n * rows // P:(n + 1) * rows // P, :]
-                copy = nc.vector.tensor_copy if (c, n) in ON_VECTOR else nc.scalar.copy
-                copy(staged, bank[:])
-                group = STORE_BANKS[c]
-                if n % group == group - 1:
-                    lo, hi = (n + 1 - group) * rows, (n + 1) * rows
-                    nc.sync.dma_start(out[lo:hi, cols].rearrange("(k p) m -> p k m", p=P), staged_all[:, lo // P:hi // P, :])
+                mine = staged[:, n * blocks:(n + 1) * blocks, :]
+                copy = nc.vector.tensor_copy if (c, n) == ON_VECTOR else nc.scalar.copy
+                copy(mine, bank[:])
+                nc.sync.dma_start(out[n * blocks * P:(n + 1) * blocks * P, cols].rearrange("(k p) m -> p k m", p=P), mine)
 
-        first_pass(0)
         scatter(LAST)
-        quantise_z0(slice(128, 384), "d3_0")
-        first_pass(1)
+        quantise_z0(chunks[1], "d3_0")
         tail_fetch(0)
         tail_tanh(0)
         tail_fetch(1)
         tail_tanh(1)
+        lead = CHUNKS[0]
+        codes = slot("z1_planes", [P, 2 * N + lead], U32)
+        w4_scales = slot("w4_scales", [P, 2 * N], U8)
+        w4q.append(quantise(w4_woven[0], codes[:, 0:N], w4_scales[:, 0:N]))
+        z0[0, lead] = quantise(z0_woven[0][:, 0:lead, :], codes[:, 2 * N:2 * N + lead], slot("z0_scales0", [P, lead], U8)[:])
+        w4q.append(quantise(w4_woven[1], codes[:, N:2 * N], w4_scales[:, N:2 * N]))
+        first_pass(0)
+        first_pass(1)
         tail_gain(0)
+        tail_gain(1)
         tail_fetch(2)
         tail_tanh(2)
         tail_close(0)
+        tail_close(1)
         tail_store(0)
-        tail_gain(1)
         tail_fetch(3)
         tail_tanh(3)
-        tail_close(1)
         tail_gain(2)
-        quantise_z0(slice(384, 512), "tz0")
-        quantise_z0(slice(512, 768), "tz1")
+        quantise_z0(slice(chunks[2].start, BANK), "tz0")
+        quantise_z0(slice(BANK, chunks[2].stop), "tz1")
         first_pass(2)
         tail_store(1)
         tail_close(2)
-        quantise_z0(slice(768, 1024), "tz2")
+        quantise_z0(chunks[3], "tz2")
         first_pass(3)
         tail_store(2)
         tail_gain(3)

from contextlib import ExitStack

import concourse.mybir as mybir
from concourse.masks import make_identity

K, T, S, T2, PR, H, N = 512, 4096, 1024, 2048, 1024, 1024, 512
FLOPS = 2 * (3 * K * H * S + H * N * PR)

F32 = mybir.dt.float32
BF16 = mybir.dt.bfloat16
I32 = mybir.dt.int32
U32 = mybir.dt.uint32
U16 = mybir.dt.uint16
U8 = mybir.dt.uint8
E4M3 = mybir.dt.float8_e4m3fn_x4
E2M1 = mybir.dt.float4_e2m1fn_x4
MULT = mybir.AluOpType.mult
ADD = mybir.AluOpType.add
ACT = mybir.ActivationFunctionType

P = 128
PACK = 4
QUADRANT = 32
SCALE_ROWS = K // 32
GROUP = 16
BANK = 512
LAST = H // P - 1
HEAD = 2 * P
TABLE_FIRST = T // 4
W2_ROWS = 4
TURN_BANKS = (6, 7)
PRIOR_BUFFERS = 5
EARLY_FETCH = HEAD
CHUNKS = (128, 256, 384, 256)
BANKS = ((0, 1), (2, 3), (4, 5, 6, 7), (0, 1))
ON_VECTOR = (3, 1)
SCALAR_GAINS = (0, 1)
D1, D2, D3 = 0, 1, 2
D1_TAGS = {2: "d1_0", 3: "d1_0", 4: "d1_1", 5: "d1_1", 6: "woven3b", 7: "raw3a"}
D2_TAGS = {2: "d2_0", 3: "d2_1", 4: "raw3c", 5: "d2_1", 6: "raw3c", 7: "d2_0"}
D3_TAGS = {2: "d3_2", 3: "d3_2", 4: "d3_0", 5: "d3_2", 6: "d3_0", 7: "d3_1"}


def tile_list_semijoin_cache_kernel(tc, tab_words, tab_scales, offs, offs2, offs3, w1_words, w1_scales,
                                                 w2_words, w2_scales, w3, wgs, prior, gain, w4, out):
    nc = tc.nc
    with ExitStack() as ctx:
        keep = ctx.enter_context(tc.tile_pool(name="keep", bufs=1))
        psum = ctx.enter_context(tc.psum_pool(name="psum", bufs=1))

        def slot(tag, shape, dtype):
            return keep.tile(shape, dtype, name=tag, tag=tag, align_bytes=64)

        def bank_tile(n, shape):
            return psum.tile(shape, F32, name="bank%d" % n, tag="bank%d" % n)

        def half_cols(half):
            return slice(half * BANK, (half + 1) * BANK)

        def entries(offsets, cols):
            return offsets[:, cols.start // GROUP:cols.stop // GROUP]

        def load(tag, shape, dtype, src):
            dst = slot(tag, shape, dtype)
            nc.sync.dma_start(dst[:], src)
            return dst

        def load_scales(queue, plane, rows, first):
            for r in range(PACK):
                queue.dma_start(plane[first + r:P:QUADRANT, :].bitcast(I32), rows[0, r:SCALE_ROWS:PACK, :].bitcast(I32))

        idx = keep.tile([P, S // GROUP], U16, name="idx")
        idx2 = keep.tile([P, S // GROUP], U16, name="idx2")
        idx3 = keep.tile([P, PR // GROUP], U16, name="idx3")
        table = slot("table", [P, T], I32)
        table_scales = slot("table_scales", [P, T], U8)
        w_scales = slot("w_scales", [P, 2, H], U8)
        nc.gpsimd.memset(w_scales[:, D2, :].bitcast(I32), 0)
        nc.gpsimd.memset(table_scales[:, 0:T // 2].bitcast(I32), 0)
        nc.vector.memset(table_scales[:, T // 2:T].bitcast(I32), 0)
        nc.vector.memset(w_scales[:, D1, :].bitcast(I32), 0)

        preload = keep.tile([P, 2], F32, name="preload")
        nc.vector.memset(preload[:, 0:1], 0.0)
        nc.scalar.activation(preload[:, 1:2], preload[:, 0:1], ACT.Tanh)

        w3_rows = w3.rearrange("(p j) c -> p j c", j=PACK)
        w1_i32 = w1_words[0].bitcast(I32)
        w2_i32 = w2_words[0].rearrange("p c i -> p (c i)").bitcast(I32)
        table_i32 = tab_words[0].rearrange("p t i -> p (t i)").bitcast(I32)

        nc.sync.dma_start(table[:, 0:TABLE_FIRST], table_i32[:, 0:TABLE_FIRST])
        nc.sync.dma_start(idx[:], offs)
        load_scales(nc.sync, table_scales[:], tab_scales, 0)
        w1a = load("w1a", [P, HEAD // 2], I32, w1_i32[:, 0:HEAD // 2])
        nc.sync.dma_start(table[:, TABLE_FIRST:T], table_i32[:, TABLE_FIRST:T])
        load_scales(nc.gpsimd, w_scales[:, D2, :], w2_scales, W2_ROWS)
        load_scales(nc.sync, w_scales[:, D1, :], w1_scales, 0)
        raw3a = load("raw3a", [P, PACK, HEAD], F32, w3_rows[:, :, 0:HEAD])
        wg = slot("wg", [P, S], F32)
        nc.sync.dma_start(wg[:, half_cols(0)], wgs[:, half_cols(0)])
        w2a = load("w2a", [P, HEAD], I32, w2_i32[:, 0:HEAD])
        nc.sync.dma_start(wg[:, half_cols(1)], wgs[:, half_cols(1)])
        nc.sync.dma_start(idx2[:], offs2)
        raw3b = load("raw3b", [P, PACK, HEAD], F32, w3_rows[:, :, HEAD:K])
        raw3c = load("raw3c", [P, PACK, K], F32, w3_rows[:, :, K:H])
        w1b = load("w1b", [P, HEAD // 2], I32, w1_i32[:, HEAD // 2:K // 2])
        w2b = load("w2b", [P, HEAD], I32, w2_i32[:, HEAD:K])
        nc.sync.dma_start(idx3[:], offs3)

        priors = {}

        def load_prior(i):
            rows = prior[i * P:(i + 1) * P, :] if i < PACK else prior[K:H, :].rearrange("(p t) m -> t p m", t=PACK)[i - PACK]
            priors[i] = load("prior%d" % (i % PRIOR_BUFFERS), [P, PR], F32, rows)

        w1c = load("w1c", [P, K // 2], I32, w1_i32[:, K // 2:K])
        w2c = load("w2c", [P, K], I32, w2_i32[:, K:H])
        wg_dealt = []

        def load_dealt_wgs(t):
            wg_dealt.append(slot("wg_dealt%d" % t, [P, S], F32))
            for a in (0, 2, 1, 3):
                nc.sync.dma_start(wg_dealt[t][QUADRANT * a:QUADRANT * (a + 1), :], wgs.rearrange("(c t) j -> t c j", t=PACK)[t])

        for t in range(PACK - 1):
            load_prior(t)
            load_dealt_wgs(t)
        gains = keep.tile([P, 2, PACK], F32, name="gains")
        nc.sync.dma_start(gains[:], gain.rearrange("(b p t) -> p b t", p=P, t=PACK))
        load_prior(PACK - 1)
        raw4 = [load(tag, [P, PACK, N], F32, w4[b * K:(b + 1) * K, :].rearrange("(p j) n -> p j n", j=PACK))
                for b, tag in enumerate(("raw4a", "z1_woven"))]
        load_dealt_wgs(PACK - 1)

        ident = keep.tile([P, P], F32, name="ident")
        make_identity(nc, ident[:])
        pages = [slot("page%d" % n, [P, T2], F32) for n in range(2)]
        nc.vector.memset(pages[0][:], 0.0)
        nc.gpsimd.memset(pages[1][:], 0.0)

        v_scales = slot("v_scales", [P, S], U8)
        nc.vector.tensor_copy(v_scales[:], table_scales[:].indirect(idx[:]))
        v_words = []
        for half in range(2):
            v_words.append(slot("v_words%d" % half, [P, BANK], U32))
            nc.vector.tensor_copy(v_words[half][:], table[:].bitcast(U32).indirect(entries(idx, half_cols(half))))
        scales_dealt = {}
        for which, tag in ((D2, "w2_scales_dealt"), (D1, "w1_scales_dealt")):
            scales_dealt[which] = slot(tag, [P, PACK, P], U8)
            nc.gpsimd.tensor_copy(scales_dealt[which][:], w_scales[:, which, K:H].rearrange("k (p t) -> k t p", t=PACK))

        def weave(woven, raw):
            nc.scalar.copy(woven.rearrange("p (c i) t -> p c t i", i=4), raw.rearrange("p t (c i) -> p c t i", i=4))
            return woven

        def quantise(woven, codes, scales):
            nc.vector.quantize_mx(out=codes.bitcast(E4M3), scales=scales, in_=woven.rearrange("p c t -> p (c t)"))
            return codes, scales

        w3q = {}

        def quantise_w3(woven, first, count, tag):
            codes = slot(tag, [P, count * P], U32)
            scales = slot("w3_scales%d" % first, [P, count * P], U8)
            quantise(woven, codes[:], scales[:])
            for k in range(count):
                w3q[first + k] = codes[:, k * P:(k + 1) * P], scales[:, k * P:(k + 1) * P]

        dealt = {}

        def stationary(i, which):
            if which == D3:
                codes, scales = w3q[i]
                return codes.bitcast(E4M3), scales
            if i >= PACK:
                t = i - PACK
                if which == D1:
                    return dealt[D1][:, t, :].bitcast(E2M1), scales_dealt[D1][:, t, :]
                return dealt[D2][:, t, :].bitcast(E4M3), scales_dealt[D2][W2_ROWS:P, t, :]
            cols = slice(i * P, (i + 1) * P)
            if which == D1:
                return (w1a, w1b)[i // 2][:, i % 2 * P // 2:(i % 2 + 1) * P // 2].bitcast(E2M1), w_scales[:, D1, cols]
            return (w2a, w2b)[i // 2][:, i % 2 * P:(i % 2 + 1) * P].bitcast(E4M3), w_scales[W2_ROWS:P, D2, cols]

        def signature(i, which, half, n):
            lhs, lhs_scale = stationary(i, which)
            bank = bank_tile(n, [P, BANK])
            nc.tensor.matmul_mx(out=bank[:], lhsT=lhs, lhsT_scale=lhs_scale, rhs=v_words[half][:].bitcast(E4M3),
                                rhs_scale=v_scales[:, half_cols(half)], start=True, stop=True)
            return bank

        def copy_half(i, which, half, dst, n):
            nc.scalar.copy(dst, signature(i, which, half, n)[:])
            return dst

        def copy_out(i, which, dst, first):
            for half in range(2):
                copy_half(i, which, half, dst[:, half_cols(half)], first + half)
            return dst[:]

        joint = {}

        def scatter(i, cols=slice(0, S)):
            page = pages[i % 2][:].indirect(entries(idx2, cols))
            if i == LAST:
                nc.vector.tensor_tensor(page, joint[i][:, cols], wg_dealt[i - PACK][:, cols], MULT)
            else:
                nc.vector.tensor_copy(page, joint[i][:, cols])

        first, second = half_cols(0), half_cols(1)
        joint[0] = slot("h0", [P, S], F32)
        joint[1] = slot("h1", [P, S], F32)
        woven3a = weave(slot("woven3a", [P, HEAD, PACK], BF16)[:], raw3a[:])
        behind_weave = slot("raw3a", [P, 2, BANK], F32)
        ones = [behind_weave[:, D1, :], behind_weave[:, D2, :], slot("d3_1", [P, BANK], F32)]
        h0 = joint[0][:, first]
        nc.vector.tensor_tensor(h0, signature(0, D1, 0, 0)[:], wg[:, first], MULT)
        copy_half(1, D1, 0, ones[D1][:, first], 3)
        quantise_w3(woven3a, 0, 2, "w3_codes0")
        nc.vector.tensor_tensor(h0, signature(0, D2, 0, 1)[:], h0, MULT)
        copy_half(1, D2, 0, ones[D2][:, first], 4)
        nc.vector.tensor_tensor(h0, signature(0, D3, 0, 2)[:], h0, MULT)
        copy_half(1, D3, 0, ones[D3][:, first], 5)
        scatter(0, first)
        weighted = slot("weighted0", [P, BANK], F32)
        bank = signature(0, D1, 1, 6)
        for at in (0, HEAD):
            nc.vector.tensor_tensor(weighted[:, at:at + HEAD], bank[:, at:at + HEAD], wg[:, BANK + at:BANK + at + HEAD], MULT)
        u = slot("woven3a", [P, BANK], F32)
        v = slot("v_half", [P, BANK], F32)
        nc.gpsimd.tensor_tensor(u[:], ones[D1][:, first], wg[:, first], MULT)
        nc.gpsimd.tensor_tensor(v[:], ones[D2][:, first], ones[D3][:, first], MULT)
        nc.gpsimd.tensor_tensor(joint[1][:, first], u[:], v[:], MULT)
        woven3b = weave(slot("woven3b", [P, HEAD, PACK], BF16)[:], raw3b[:])
        zeros = {which: copy_half(0, which, 1, slot(tag, [P, BANK], F32)[:], n)
                 for which, tag, n in ((D3, "d3_0", 3), (D2, "d2_0", 5))}
        scatter(1, first)
        woven3c = slot("woven3c", [P, K, PACK], BF16)
        nc.scalar.copy(woven3c[:].rearrange("k (t p) j -> k p j t", t=PACK), raw3c[:].rearrange("k j (p t) -> k p j t", t=PACK))
        u = slot("woven3a", [P, BANK], F32)
        nc.gpsimd.tensor_tensor(u[:], zeros[D2], zeros[D3], MULT)
        behind_last_weave = slot("raw3c", [P, 2, S], F32)
        joint[0] = behind_last_weave[:, 0, :]
        nc.gpsimd.tensor_tensor(joint[0][:, second], u[:], weighted[:], MULT)
        twos = [copy_out(2, which, slot(tags[2], [P, S], F32), 2 * which) for which, tags in ((D1, D1_TAGS), (D2, D2_TAGS))]
        late_ones = [copy_half(1, which, 1, behind_last_weave[:, 1, half_cols(which)], 2 * which + 1) for which in (D1, D2)]
        quantise_w3(woven3c[:], PACK, PACK, "weighted0")
        quantise_w3(woven3b, 2, 2, "woven3a")
        scatter(0, second)
        weighted_one = slot("woven3c", [P, BANK], F32)
        nc.vector.tensor_tensor(weighted_one[:], signature(1, D3, 1, 7)[:], wg[:, second], MULT)
        behind_window = slot("woven3b", [P, BANK + S], F32)
        nc.gpsimd.tensor_tensor(behind_window[:, 0:BANK], late_ones[D1], late_ones[D2], MULT)
        nc.gpsimd.tensor_tensor(joint[1][:, second], behind_window[:, 0:BANK], weighted_one[:], MULT)

        def deal_words():
            dealt[D1] = slot("w1_dealt", [P, PACK, P], U16)
            dealt[D2] = slot("w2_dealt", [P, PACK, P], U32)
            nc.scalar.copy(dealt[D1][:].rearrange("k t p -> k p t"), w1c[:].bitcast(U16).rearrange("k (p t) -> k p t", t=PACK))
            nc.scalar.copy(dealt[D2][:].rearrange("k t p -> k p t"), w2c[:].bitcast(U32).rearrange("k (p t) -> k p t", t=PACK))

        def join(i):
            d1, d2 = twos if i == 2 else [copy_out(i, which, slot(tags[i], [P, S], F32), 2 * which)
                                          for which, tags in ((D1, D1_TAGS), (D2, D2_TAGS))]
            d3 = slot(D3_TAGS[i], [P, S], F32)
            weight = wg if i < PACK else wg_dealt[i - PACK]
            done = 0
            if i == 2:
                for half in range(2):
                    copy_half(i, D3, half, d3[:, half_cols(half)], 2 * half + 1)
            elif i == 3:
                done = HEAD
                v = slot("woven3c", [P, BANK], F32)
                bank = signature(i, D3, 0, 4)
                nc.vector.tensor_tensor(v[:, 0:done], bank[:, 0:done], weight[:, 0:done], MULT)
                nc.scalar.copy(d3[:, done:BANK], bank[:, done:BANK])
                copy_half(i, D3, 1, d3[:, second], 5)
            else:
                copy_out(i, D3, d3, 4)
            u = behind_window[:, BANK:BANK + S] if i == 2 else slot("raw3a", [P, S], F32)[:] if i == PACK else d1
            h = slot("h%d" % (i % 3), [P, S], F32)
            joint[i] = h
            nc.gpsimd.tensor_tensor(u, d1, d2, MULT)
            if i == LAST:
                nc.gpsimd.tensor_tensor(h[:], u, d3[:], MULT)
                return
            if not done:
                v = h
            cut = P if i == 2 else BANK
            nc.gpsimd.tensor_tensor(v[:, done:cut], d3[:, done:cut], weight[:, done:cut], MULT)
            nc.gpsimd.tensor_tensor(h[:, cut:S], d3[:, cut:S], weight[:, cut:S], MULT)
            nc.gpsimd.tensor_tensor(h[:, 0:cut], u[:, 0:cut], v[:, 0:cut], MULT)
            nc.gpsimd.tensor_tensor(h[:, cut:S], u[:, cut:S], h[:, cut:S], MULT)

        squashed = slot("table", [P, PR // P, PACK, P], F32)
        turns = []

        def turn_bank(shape):
            turns.append(0)
            return bank_tile(TURN_BANKS[len(turns) % 2], shape)

        waiting = []

        def gather(i, cols, x):
            nc.vector.tensor_copy(x, pages[i % 2][:].indirect(entries(idx3, cols)))

        def fetch(i, cols, x):
            gather(i, cols, x)
            if i >= PACK:
                waiting.append((i, cols, x))
            else:
                squash_turned(i, cols, x, turn_bank([P, PACK, P]))

        def add_turned(bank, x, y):
            for n, src in enumerate((x, y)):
                for k in range(PACK):
                    nc.tensor.matmul(bank[:, k, :], src[:, k * P:(k + 1) * P], ident[:], is_transpose=True,
                                     start=n == 0 and k == 0, stop=n == 1 and k == PACK - 1)

        def squash_turned(i, cols, x, bank):
            add_turned(bank, x, priors[i][:, cols])
            nc.scalar.activation(squashed[:, cols.start // P:cols.stop // P, :, QUADRANT * i:QUADRANT * (i + 1)],
                                 bank[:].rearrange("m k (p t) -> m k t p", t=PACK), ACT.Tanh)

        def squash_dealt_turned(i, cols, x):
            bank = turn_bank([P, PACK, P])
            add_turned(bank, x, priors[i][:, cols])
            bent = slot("bent", [P, PACK, P], F32)
            nc.scalar.activation(bent[:], bank[:], ACT.Tanh)
            for n in range(2):
                bank = bank_tile(n, [P, 2, P])
                for k in range(2):
                    nc.tensor.transpose(bank[:, k, :], bent[:, 2 * n + k, :], ident[:])
                at = cols.start + n * HEAD
                nc.scalar.activation(z1_planes[:, i - PACK, at:at + HEAD], bank[:].rearrange("p k m -> p (k m)"), ACT.Copy,
                                     scale=gains[:, 1, i - PACK:i - PACK + 1])

        def weave_z0(half):
            planes = slot("planes%d" % half, [P, PACK, BANK], BF16)
            for t in range(PACK):
                bank = turn_bank([P, BANK])
                for k in range(PACK):
                    nc.tensor.transpose(bank[:, k * P:(k + 1) * P], squashed[:, PACK * half + k, t, :], ident[:])
                nc.scalar.activation(planes[:, t, :], bank[:], ACT.Copy, scale=gains[:, 0, t:t + 1])
            return weave(slot("z0_woven%d" % half, [P, BANK, PACK], BF16)[:], planes[:])

        join(2)
        deal_words()
        fetched = [slot("table_scales", [P, PR], F32)]
        gather(0, slice(0, PR), fetched[0][:])
        scatter(1, second)
        fetched.append(slot("d2_0", [P, PR], F32))
        join(3)
        gather(1, slice(0, PR), fetched[1][:])
        for i, x in enumerate(fetched):
            for half in range(2):
                squash_turned(i, half_cols(half), x[:, half_cols(half)], bank_tile(4 * i + half, [P, PACK, P]))
        z0_woven = []
        z1_planes = slot("z1_planes", [P, PACK - 1, PR], BF16)
        for i in range(2, LAST):
            scatter(i)
            ahead = EARLY_FETCH if i == LAST - 2 else BANK
            x = slot(D3_TAGS[i + 1], [P, BANK + ahead], F32) if i < LAST - 1 else None
            if i == 2:
                gather(i, first, x[:, 0:BANK])
                join(i + 2)
                squash_turned(i, first, x[:, 0:BANK], turn_bank([P, PACK, P]))
            elif i < LAST - 1:
                join(i + 2)
                if i + 2 == LAST:
                    squash_dealt_turned(*waiting.pop())
                fetch(i - 1, second, x[:, 0:BANK])
                if i == PACK:
                    z0_woven.append(weave_z0(1))
                fetch(i, slice(0, ahead), x[:, BANK:BANK + ahead])
                if i + 2 == LAST:
                    squash_dealt_turned(*waiting.pop(0))
            if i + 2 <= LAST:
                load_prior(i + 2)
            if i == PACK - 1:
                z0_woven.append(weave_z0(0))

        w4_woven = [weave(slot("v_words%d" % b, [P, N, PACK], BF16)[:], raw4[b][:]) for b in range(2)]
        z1_woven = slot("z1_woven", [P, PR, PACK], BF16)

        def bend(i, cols, y, bent):
            t = i - PACK
            nc.scalar.activation(bent, y, ACT.Tanh)
            nc.scalar.activation(z1_planes[:, t, cols], bent, ACT.Copy, scale=gains[:, 1, t:t + 1])
            if i == LAST - 1:
                nc.scalar.copy(z1_woven[:, cols, 0:PACK - 1].rearrange("p (c i) t -> p c t i", i=4),
                               z1_planes[:, :, cols].rearrange("p t (c i) -> p c t i", i=4))

        i, cols, x = waiting.pop()
        sums = slot("raw3a", [P, 3, BANK], F32)
        bent = slot("planes1", [P, 2, BANK], F32)
        nc.gpsimd.tensor_tensor(sums[:, 0, cols], x, priors[i][:, cols], ADD)
        bend(i, cols, sums[:, 0, cols], bent[:, 0, cols])
        x = slot("d3_0", [P, 2 * PR - EARLY_FETCH], F32)
        bent = slot("planes1", [P, 2, PR - EARLY_FETCH], F32)
        late = [(LAST - 2, slice(EARLY_FETCH, PR), x[:, PR:2 * PR - EARLY_FETCH])]
        late.extend((LAST - 1, half_cols(half), x[:, half_cols(half)]) for half in range(2))
        for i, cols, y in late:
            nc.vector.tensor_tensor(y, pages[i % 2][:].indirect(entries(idx3, cols)), priors[i][:, cols], ADD)
        for n, (i, cols, y) in enumerate(late):
            bend(i, cols, y, bent[:, n % 2, 0:cols.stop - cols.start])

        z0 = {}
        w4q = []

        def quantise_z0(cols, tag):
            mine = slice(cols.start % BANK, (cols.stop - 1) % BANK + 1)
            width = cols.stop - cols.start
            z0[cols.start, cols.stop] = quantise(z0_woven[cols.start // BANK][:, mine, :], slot(tag, [P, width], U32)[:],
                                                 slot("z0_scales%d" % cols.start, [P, width], U8)[:])

        chunks = [slice(sum(CHUNKS[:c]), sum(CHUNKS[:c + 1])) for c in range(len(CHUNKS))]

        def estimate_pass(b, banks, pieces):
            w_codes, w_scales4 = w4q[b]
            per_bank = N // P // len(banks)
            steps = [(part, n) for part in range(len(pieces)) for n in range(N // P)]
            if b == 1:
                steps = [(part, n) for n in range(N // P) for part in range(len(pieces))]
            for part, n in steps:
                at, z_codes, z_scales = pieces[part]
                cols = slice(n * P, (n + 1) * P)
                nc.tensor.matmul_mx(out=banks[n // per_bank][:, n % per_bank, at], lhsT=w_codes[:, cols].bitcast(E4M3),
                                    lhsT_scale=w_scales4[:, cols], rhs=z_codes.bitcast(E4M3), rhs_scale=z_scales,
                                    start=b == 0 and part == 0 and n % per_bank == 0,
                                    stop=b == 1 and part == len(pieces) - 1 and n % per_bank == per_bank - 1)

        opened = {}

        def first_pass(c):
            cols = chunks[c]
            opened[c] = [bank_tile(n, [P, N // P // len(BANKS[c]), CHUNKS[c]]) for n in BANKS[c]]
            pieces = []
            for (start, stop), (z_codes, z_scales) in z0.items():
                if cols.start <= start and stop <= cols.stop:
                    pieces.append((slice(start - cols.start, stop - cols.start), z_codes, z_scales))
            estimate_pass(0, opened[c], pieces)

        res = slot("table", [P, N // P * PR], F32)
        squash = {}
        probed = {}
        x_tail = slot("planes1", [P, 2, max(CHUNKS)], F32)

        def tail_fetch(c):
            cols = chunks[c]
            x = x_tail[:, c % 2, 0:CHUNKS[c]]
            nc.vector.tensor_tensor(x, pages[LAST % 2][:].indirect(entries(idx3, cols)), priors[LAST][:, cols], ADD)
            probed[c] = x

        def tail_tanh(c):
            squash[c] = slot("tz%d" % c, [P, CHUNKS[c]], F32)
            nc.scalar.activation(squash[c][:], probed[c], ACT.Tanh)

        def tail_gain(c):
            if c in SCALAR_GAINS:
                nc.scalar.activation(z1_woven[:, chunks[c], PACK - 1], squash[c][:], ACT.Copy, scale=gains[:, 1, PACK - 1:PACK])
            else:
                nc.vector.tensor_scalar(z1_woven[:, chunks[c], PACK - 1], squash[c][:], gains[:, 1, PACK - 1:PACK], None, MULT)

        def tail_close(c):
            cols = chunks[c]
            z_codes, z_scales = quantise(z1_woven[:, cols, :], slot("z1_codes%d" % c, [P, CHUNKS[c]], U32)[:],
                                         slot("z1_scales%d" % c, [P, CHUNKS[c]], U8)[:])
            cuts = [slice(0, HEAD), slice(HEAD, CHUNKS[c])] if CHUNKS[c] > HEAD else [slice(0, CHUNKS[c])]
            estimate_pass(1, opened[c], [(at, z_codes[:, at], z_scales[:, at]) for at in cuts])

        def tail_store(c):
            cols = chunks[c]
            staged = res[:, N // P * cols.start:N // P * cols.stop].rearrange("p (k m) -> p k m", m=CHUNKS[c])
            blocks = N // P // len(opened[c])
            for n, bank in enumerate(opened[c]):
                mine = staged[:, n * blocks:(n + 1) * blocks, :]
                copy = nc.vector.tensor_copy if (c, n) == ON_VECTOR else nc.scalar.copy
                copy(mine, bank[:])
                nc.sync.dma_start(out[n * blocks * P:(n + 1) * blocks * P, cols].rearrange("(k p) m -> p k m", p=P), mine)

        scatter(LAST)
        quantise_z0(chunks[1], "d3_0")
        tail_fetch(0)
        tail_tanh(0)
        tail_fetch(1)
        tail_tanh(1)
        lead = CHUNKS[0]
        codes = slot("z1_planes", [P, 2 * N + lead], U32)
        w4_scales = slot("w4_scales", [P, 2 * N], U8)
        w4q.append(quantise(w4_woven[0], codes[:, 0:N], w4_scales[:, 0:N]))
        z0[0, lead] = quantise(z0_woven[0][:, 0:lead, :], codes[:, 2 * N:2 * N + lead], slot("z0_scales0", [P, lead], U8)[:])
        w4q.append(quantise(w4_woven[1], codes[:, N:2 * N], w4_scales[:, N:2 * N]))
        first_pass(0)
        first_pass(1)
        tail_gain(0)
        tail_gain(1)
        tail_fetch(2)
        tail_tanh(2)
        tail_close(0)
        tail_close(1)
        tail_store(0)
        tail_fetch(3)
        tail_tanh(3)
        tail_gain(2)
        quantise_z0(slice(chunks[2].start, BANK), "tz0")
        quantise_z0(slice(BANK, chunks[2].stop), "tz1")
        first_pass(2)
        tail_store(1)
        tail_close(2)
        quantise_z0(chunks[3], "tz2")
        first_pass(3)
        tail_store(2)
        tail_gain(3)
        tail_close(3)
        tail_store(3)
